import numpy as np
import ml_dtypes


def mxq(x, axis, fmt="e4m3"):
    dtype, down = {"e4m3": (ml_dtypes.float8_e4m3fn, 7), "e5m2": (ml_dtypes.float8_e5m2, 14)}[fmt]
    v = np.moveaxis(np.asarray(x, np.float32).astype(ml_dtypes.bfloat16).astype(np.float64), axis, -1)
    blocks = v.reshape(v.shape[:-1] + (-1, 32))
    amax = np.abs(blocks).max(-1, keepdims=True)
    byte = np.maximum(np.where(amax > 0, np.frexp(amax)[1] - 1 + 127, 0) - down, 1)
    scale = np.exp2(byte - 127.0)
    codes = (blocks / scale).astype(np.float32).astype(dtype).astype(np.float64)
    return np.moveaxis((codes * scale).reshape(v.shape), -1, axis)


WIDE = False


def mx_kscale(k):
    if not WIDE:
        return np.ones(k)
    levels = np.array([10, -10, 5, -5, 0])
    if k % 512:
        return np.exp2(np.random.permutation(np.resize(levels, k // 32))).repeat(32)
    a = np.empty((k // 512, 16))
    for p in range(k // 512):
        a[p, :8] = np.random.permutation(np.resize(levels, 8))
        for g in range(8):
            far = levels[np.abs(levels - a[p, g]) >= 10]
            a[p, g + 8] = far[np.random.randint(len(far))]
    return np.exp2(a.ravel()).repeat(32)


def f64(x):
    return np.asarray(x).astype(np.float64)


def striped(idx):
    return np.tile(idx.reshape(-1, 16).T, (8, 1)).astype(np.uint16)


def unstriped(offs):
    return offs[:16].T.reshape(-1).astype(np.int64)


E2M1 = np.array([0.0, 0.5, 1.0, 1.5, 2.0, 3.0, 4.0, 6.0, -0.0, -0.5, -1.0, -1.5, -2.0, -3.0, -4.0, -6.0])


def pack_weight(w, fmt):
    k, n = w.shape
    w = f64(np.asarray(w, np.float32).astype(ml_dtypes.bfloat16)).reshape(k // 32, 32, n)
    amax = np.abs(w).max(1)
    if fmt == "e4m3":
        byte = np.frexp(amax)[1] - 1 + 127 - 7
    else:
        mant, ex = np.frexp(amax / 6.0)
        byte = np.where(mant > 0.5, ex, ex - 1) + 127
    byte = np.clip(np.where(amax > 0, byte, 1), 1, 254)
    scaled = (w * np.exp2(127.0 - byte)[:, None, :]).reshape(k, n).astype(np.float32)
    by_word = np.ascontiguousarray(scaled.reshape(k // 512, 128, 4, n).transpose(0, 1, 3, 2))
    if fmt == "e4m3":
        words = by_word.astype(ml_dtypes.float8_e4m3fn).view(np.uint8)
    else:
        c = by_word.astype(ml_dtypes.float4_e2m1fn).view(np.uint8) & 0xF
        words = (c[..., 0::2] | (c[..., 1::2] << 4)).reshape(k // 512, 128, 2 * n)
    return np.ascontiguousarray(words), np.ascontiguousarray(byte.astype(np.uint8).reshape(k // 512, 16, n))


def unpack_weight(words, scales, fmt):
    g, _, n = scales.shape
    words = np.ascontiguousarray(words).reshape(g, 128, n, -1)
    if fmt == "e4m3":
        vals = words.view(ml_dtypes.float8_e4m3fn).astype(np.float64)
    else:
        nib = np.empty((g, 128, n, 4), np.uint8)
        nib[..., 0::2] = words & 0xF
        nib[..., 1::2] = words >> 4
        vals = E2M1[nib]
    vals = vals * np.repeat(np.exp2(scales.astype(np.float64) - 127.0), 8, axis=1)[..., None]
    return vals.transpose(0, 1, 3, 2).reshape(g * 512, n)


def relu2(v):
    return np.maximum(v, 0.0) ** 2


K, T, E, C, N = 2048, 2048, 16, 256, 128


def by_expert(wq, xq):
    return np.concatenate([wq[e].T @ xq[:, e * C:(e + 1) * C] for e in range(E)], axis=1)


def setup_inputs():
    n = np.random.standard_normal
    s = mx_kscale(K)[:, None]
    first = np.random.permutation(np.repeat(np.arange(E), T // E))
    second = (first + 1 + np.random.permutation(np.repeat(np.arange(E - 1), -(-T // (E - 1)))[:T])) % E
    while np.bincount(second, minlength=E).max() != T // E:
        load = np.bincount(second, minlength=E); hi, lo = int(load.argmax()), int(load.argmin())
        t = np.flatnonzero((second == hi) & (first != lo))[0]; second[t] = lo
    slot_token = np.empty(E * C, np.int64); pos = np.empty((2, T), np.int64); fill = np.zeros(E, np.int64)
    place = np.stack([np.random.permutation(C) for _ in range(E)])
    for r, deal in enumerate((first, second)):
        for t in np.random.permutation(T):
            e = deal[t]; j = e * C + place[e, fill[e]]; fill[e] += 1; slot_token[j] = t; pos[r, t] = j
    g = np.random.uniform(0.2, 0.8, T)
    x = pack_weight(n((K, T)) * s, "e4m3")
    return {
        "x_words": x[0],
        "x_scales": x[1],
        "w": (n((E, K, N)) / np.sqrt(K) / s[None]).astype(np.float32),
        "b": (0.3 * n((N, E))).astype(np.float32),
        "gate": np.stack([np.tile(g, (N, 1)), np.tile(1.0 - g, (N, 1))]).astype(np.float32),
        "offs": striped(slot_token),
        "pos1": striped(pos[0]),
        "pos2": striped(pos[1]),
    }


def reference(x_words, x_scales, w, b, gate, offs, pos1, pos2):
    idx = unstriped(offs)
    xq = unpack_weight(x_words, x_scales, "e4m3")[:, idx]
    y = by_expert(mxq(f64(w), 1, "e4m3"), xq)
    y = relu2(y + np.repeat(f64(b), C, axis=1))
    return f64(gate[0]) * y[:, unstriped(pos1)] + f64(gate[1]) * y[:, unstriped(pos2)]

@@ -1,0 +1,193 @@
+from contextlib import ExitStack
+
+import concourse.mybir as mybir
+
+K, T, E, C, N = 2048, 2048, 16, 256, 128
+SLOTS = E * C
+P = 128
+PACK = 4
+PASSES = K // (P * PACK)
+FLOPS = 2 * K * SLOTS * N
+
+F32 = mybir.dt.float32
+BF16 = mybir.dt.bfloat16
+I32 = mybir.dt.int32
+U32 = mybir.dt.uint32
+U16 = mybir.dt.uint16
+U8 = mybir.dt.uint8
+FP8X4 = mybir.dt.float8_e4m3fn_x4
+ACT = mybir.ActivationFunctionType
+ALU = mybir.AluOpType
+
+WIDE = [(0, 1536), (1536, 3072), (3072, 4096)]
+GROUPS = [(0, 4), (4, 8), (8, 12), (12, 14), (14, 15), (15, 16)]
+CHUNKS = [(0, 512), (512, 1024), (1024, 1536), (1536, 1792), (1792, 2048)]
+RUN = 4
+
+
+def tile_moe_pkd_lin_relu2_kernel(
+    tc, x_words, x_scales, w, b, gate, offs, pos1, pos2, out
+):
+    nc = tc.nc
+    with ExitStack() as ctx:
+        keep = ctx.enter_context(tc.tile_pool(name="keep", bufs=1))
+        wide = ctx.enter_context(tc.tile_pool(name="wide", bufs=5))
+        half = ctx.enter_context(tc.tile_pool(name="half", bufs=6))
+        small = ctx.enter_context(tc.tile_pool(name="small", bufs=3))
+        psum = ctx.enter_context(tc.psum_pool(name="psum", bufs=8))
+
+        slot_list = keep.tile([P, SLOTS // 16], U16, name="slot_list")
+        first_list = keep.tile([P, T // 16], U16, name="first_list")
+        second_list = keep.tile([P, T // 16], U16, name="second_list")
+        token_scales = keep.tile([P, T], U8, name="token_scales", align_bytes=64)
+        slot_scales = keep.tile([P, SLOTS], U8, name="slot_scales", align_bytes=64)
+        token_words = [keep.tile([P, T], I32, name="token_words%d" % a, align_bytes=64) for a in range(PASSES)]
+        slot_words = [keep.tile([P, SLOTS], U32, name="slot_words%d" % a, align_bytes=64) for a in range(PASSES)]
+        w_codes = [keep.tile([P, PASSES * N], U32, name="w_codes%d" % e, align_bytes=64) for e in range(E)]
+        w_scales = [keep.tile([P, PASSES * N], U8, name="w_scales%d" % e, align_bytes=64) for e in range(E)]
+        bias = keep.tile([P, E], F32, name="bias")
+        y = keep.tile([P, SLOTS], F32, name="y")
+
+        rounded = {}
+        sums = {}
+
+        def load_words(a):
+            nc.sync.dma_start(out=token_words[a][:], in_=x_words[a].rearrange("p t r -> p (t r)").bitcast(I32))
+
+        def load_and_round(e):
+            raw = wide.tile([P, PASSES, PACK * N], F32, name="raw", tag="wide")
+            nc.sync.dma_start(out=raw[:], in_=w[e].rearrange("(a p j) n -> p a (j n)", a=PASSES, j=PACK))
+            rounded[e] = half.tile([P, PASSES * N * PACK], BF16, name="rounded", align_bytes=64)
+            nc.scalar.copy(
+                out=rounded[e][:].rearrange("p (a c i j) -> p a c j i", a=PASSES, i=RUN, j=PACK),
+                in_=raw[:].rearrange("p a (j c i) -> p a c j i", j=PACK, i=RUN),
+            )
+
+        def quantise(e):
+            nc.vector.quantize_mx(out=w_codes[e][:].bitcast(FP8X4), scales=w_scales[e][:], in_=rounded[e][:])
+
+        def gather_scales(lo, hi):
+            nc.vector.tensor_copy(
+                out=slot_scales[:, lo:hi], in_=token_scales[:].indirect(slot_list[:, lo // 16 : hi // 16])
+            )
+
+        def gather_words(a, lo, hi):
+            nc.vector.tensor_copy(
+                out=slot_words[a][:, lo:hi],
+                in_=token_words[a][:].bitcast(U32).indirect(slot_list[:, lo // 16 : hi // 16]),
+            )
+
+        def multiply(e):
+            sums[e] = psum.tile([P, C], F32, name="sums")
+            for a in range(PASSES):
+                nc.tensor.matmul_mx(
+                    out=sums[e][:],
+                    lhsT=w_codes[e][:, a * N : (a + 1) * N].bitcast(FP8X4),
+                    lhsT_scale=w_scales[e][:, a * N : (a + 1) * N],
+                    rhs=slot_words[a][:, e * C : (e + 1) * C].bitcast(FP8X4),
+                    rhs_scale=slot_scales[4 * a : P, e * C : (e + 1) * C],
+                    start=(a == 0),
+                    stop=(a == PASSES - 1),
+                )
+
+        def activate(e):
+            positive = small.tile([P, C], F32, name="positive")
+            nc.scalar.activation(out=positive[:], in_=sums[e][:], func=ACT.Relu, bias=bias[:, e : e + 1])
+            nc.scalar.activation(out=y[:, e * C : (e + 1) * C], in_=positive[:], func=ACT.Square)
+
+        def group(g):
+            lo, hi = GROUPS[g]
+            for a in (2, 3):
+                gather_words(a, lo * C, hi * C)
+            for e in range(lo, hi):
+                multiply(e)
+
+        def finish(g):
+            for e in range(GROUPS[g][0], GROUPS[g][1]):
+                activate(e)
+
+        nc.sync.dma_start(slot_list[:], offs)
+        nc.vector.memset(token_scales[:].bitcast(I32), 0)
+        for q in range(4):
+            nc.sync.dma_start(
+                out=token_scales[32 * q : 32 * q + 16, :].bitcast(I32),
+                in_=x_scales[:, 4 * q : 4 * q + 4, :].bitcast(I32),
+            )
+        load_and_round(0)
+        load_and_round(1)
+        load_words(0)
+        for lo, hi in WIDE:
+            gather_scales(lo, hi)
+        quantise(0)
+        quantise(1)
+        for e in (2, 3, 4):
+            load_and_round(e)
+        load_words(1)
+        for lo, hi in WIDE:
+            gather_words(0, lo, hi)
+        for e in (2, 3, 4):
+            quantise(e)
+        for e in (5, 6, 7):
+            load_and_round(e)
+        load_words(2)
+        load_and_round(8)
+        load_words(3)
+        nc.sync.dma_start(out=bias[:], in_=b)
+        nc.sync.dma_start(first_list[:], pos1)
+        nc.sync.dma_start(second_list[:], pos2)
+        for lo, hi in WIDE:
+            gather_words(1, lo, hi)
+        quantise(5)
+        quantise(6)
+        load_and_round(9)
+        load_and_round(10)
+        group(0)
+        for e in (7, 8, 9):
+            quantise(e)
+        load_and_round(11)
+        load_and_round(12)
+        load_and_round(13)
+        finish(0)
+        group(1)
+        for e in (10, 11):
+            quantise(e)
+        load_and_round(14)
+        load_and_round(15)
+        finish(1)
+        group(2)
+        quantise(12)
+        quantise(13)
+        finish(2)
+        group(3)
+        quantise(14)
+        quantise(15)
+        finish(3)
+        group(4)
+        group(5)
+        finish(4)
+        finish(5)
+
+        gates = []
+        for r in range(2):
+            gate_r = wide.tile([P, T], F32, name="gate_r", tag="wide")
+            nc.sync.dma_start(out=gate_r[:], in_=gate[r])
+            gates.append(gate_r)
+        first = wide.tile([P, T], F32, name="first", tag="wide")
+        second = wide.tile([P, T], F32, name="second", tag="wide")
+        total = wide.tile([P, T], F32, name="total", tag="wide")
+
+        def fetch(dst, lst, r, lo, hi):
+            nc.vector.tensor_tensor(
+                out=dst[:, lo:hi], in0=y[:].indirect(lst[:, lo // 16 : hi // 16]), in1=gates[r][:, lo:hi], op=ALU.mult
+            )
+
+        def combine(lo, hi):
+            nc.vector.tensor_tensor(out=total[:, lo:hi], in0=first[:, lo:hi], in1=second[:, lo:hi], op=ALU.add)
+            nc.sync.dma_start(out=out[:, lo:hi], in_=total[:, lo:hi])
+
+        for i, (lo, hi) in enumerate(CHUNKS):
+            fetch(first, first_list, 0, lo, hi)
+            if i > 0:
+                combine(*CHUNKS[i - 1])
+            fetch(second, second_list, 1, lo, hi)
+        combine(*CHUNKS[-1])

@@ -20,8 +20,9 @@ ACT = mybir.ActivationFunctionType
 ALU = mybir.AluOpType
 
 WIDE = [(0, 1536), (1536, 3072), (3072, 4096)]
-GROUPS = [(0, 4), (4, 8), (8, 12), (12, 14), (14, 15), (15, 16)]
-CHUNKS = [(0, 512), (512, 1024), (1024, 1536), (1536, 1792), (1792, 2048)]
+PAIRS = E // 2
+PAIR = 2 * C
+CHUNKS = [(0, 1024), (1024, 1664), (1664, 1920), (1920, 2048)]
 RUN = 4
 
 
@@ -31,9 +32,9 @@ def tile_moe_pkd_lin_relu2_kernel(
     nc = tc.nc
     with ExitStack() as ctx:
         keep = ctx.enter_context(tc.tile_pool(name="keep", bufs=1))
-        wide = ctx.enter_context(tc.tile_pool(name="wide", bufs=5))
-        half = ctx.enter_context(tc.tile_pool(name="half", bufs=6))
-        small = ctx.enter_context(tc.tile_pool(name="small", bufs=3))
+        wide = ctx.enter_context(tc.tile_pool(name="wide", bufs=1))
+        half = ctx.enter_context(tc.tile_pool(name="half", bufs=5))
+        small = ctx.enter_context(tc.tile_pool(name="small", bufs=4))
         psum = ctx.enter_context(tc.psum_pool(name="psum", bufs=8))
 
         slot_list = keep.tile([P, SLOTS // 16], U16, name="slot_list")
@@ -42,28 +43,37 @@ def tile_moe_pkd_lin_relu2_kernel(
         token_scales = keep.tile([P, T], U8, name="token_scales", align_bytes=64)
         slot_scales = keep.tile([P, SLOTS], U8, name="slot_scales", align_bytes=64)
         token_words = [keep.tile([P, T], I32, name="token_words%d" % a, align_bytes=64) for a in range(PASSES)]
-        slot_words = [keep.tile([P, SLOTS], U32, name="slot_words%d" % a, align_bytes=64) for a in range(PASSES)]
-        w_codes = [keep.tile([P, PASSES * N], U32, name="w_codes%d" % e, align_bytes=64) for e in range(E)]
-        w_scales = [keep.tile([P, PASSES * N], U8, name="w_scales%d" % e, align_bytes=64) for e in range(E)]
         bias = keep.tile([P, E], F32, name="bias")
         y = keep.tile([P, SLOTS], F32, name="y")
 
+        raw = {}
         rounded = {}
+        w_codes = {}
+        w_scales = {}
+        slot_words = {}
         sums = {}
+
+        def wide_tile(place, dtype, name):
+            return wide.tile([P, T], dtype, name=name, tag="wide%d" % place, align_bytes=64)
 
         def load_words(a):
             nc.sync.dma_start(out=token_words[a][:], in_=x_words[a].rearrange("p t r -> p (t r)").bitcast(I32))
 
-        def load_and_round(e):
-            raw = wide.tile([P, PASSES, PACK * N], F32, name="raw", tag="wide")
-            nc.sync.dma_start(out=raw[:], in_=w[e].rearrange("(a p j) n -> p a (j n)", a=PASSES, j=PACK))
+        def load_weights(e):
+            raw[e] = wide_tile(e, F32, "raw%d" % e)
+            nc.sync.dma_start(
+                out=raw[e][:].rearrange("p (a m) -> p a m", a=PASSES),
+                in_=w[e].rearrange("(a p j) n -> p a (j n)", a=PASSES, j=PACK),
+            )
+
+        def round_and_quantise(e):
             rounded[e] = half.tile([P, PASSES * N * PACK], BF16, name="rounded", align_bytes=64)
             nc.scalar.copy(
                 out=rounded[e][:].rearrange("p (a c i j) -> p a c j i", a=PASSES, i=RUN, j=PACK),
-                in_=raw[:].rearrange("p a (j c i) -> p a c j i", j=PACK, i=RUN),
+                in_=raw[e][:].rearrange("p (a j c i) -> p a c j i", a=PASSES, j=PACK, i=RUN),
             )
-
-        def quantise(e):
+            w_codes[e] = small.tile([P, PASSES * N], U32, name="w_codes", align_bytes=64)
+            w_scales[e] = small.tile([P, PASSES * N], U8, name="w_scales", align_bytes=64)
             nc.vector.quantize_mx(out=w_codes[e][:].bitcast(FP8X4), scales=w_scales[e][:], in_=rounded[e][:])
 
         def gather_scales(lo, hi):
@@ -71,110 +81,79 @@ def tile_moe_pkd_lin_relu2_kernel(
                 out=slot_scales[:, lo:hi], in_=token_scales[:].indirect(slot_list[:, lo // 16 : hi // 16])
             )
 
-        def gather_words(a, lo, hi):
-            nc.vector.tensor_copy(
-                out=slot_words[a][:, lo:hi],
-                in_=token_words[a][:].bitcast(U32).indirect(slot_list[:, lo // 16 : hi // 16]),
-            )
+        def gather_words(m, place):
+            slot_words[m] = wide_tile(place, U32, "slot_words%d" % m)
+            for a in range(PASSES):
+                nc.vector.tensor_copy(
+                    out=slot_words[m][:, a * PAIR : (a + 1) * PAIR],
+                    in_=token_words[a][:].bitcast(U32).indirect(slot_list[:, m * PAIR // 16 : (m + 1) * PAIR // 16]),
+                )
 
         def multiply(e):
             sums[e] = psum.tile([P, C], F32, name="sums")
             for a in range(PASSES):
+                first_word = a * PAIR + (e % 2) * C
                 nc.tensor.matmul_mx(
                     out=sums[e][:],
                     lhsT=w_codes[e][:, a * N : (a + 1) * N].bitcast(FP8X4),
                     lhsT_scale=w_scales[e][:, a * N : (a + 1) * N],
-                    rhs=slot_words[a][:, e * C : (e + 1) * C].bitcast(FP8X4),
+                    rhs=slot_words[e // 2][:, first_word : first_word + C].bitcast(FP8X4),
                     rhs_scale=slot_scales[4 * a : P, e * C : (e + 1) * C],
                     start=(a == 0),
                     stop=(a == PASSES - 1),
                 )
 
-        def activate(e):
-            positive = small.tile([P, C], F32, name="positive")
-            nc.scalar.activation(out=positive[:], in_=sums[e][:], func=ACT.Relu, bias=bias[:, e : e + 1])
-            nc.scalar.activation(out=y[:, e * C : (e + 1) * C], in_=positive[:], func=ACT.Square)
-
-        def group(g):
-            lo, hi = GROUPS[g]
-            for a in (2, 3):
-                gather_words(a, lo * C, hi * C)
-            for e in range(lo, hi):
-                multiply(e)
-
-        def finish(g):
-            for e in range(GROUPS[g][0], GROUPS[g][1]):
-                activate(e)
+        def activate(e, scratch):
+            positive = scratch[:, (e % 4) * C : (e % 4 + 1) * C]
+            nc.scalar.activation(out=positive, in_=sums[e][:], func=ACT.Relu, bias=bias[:, e : e + 1])
+            nc.scalar.activation(out=y[:, e * C : (e + 1) * C], in_=positive, func=ACT.Square)
 
         nc.sync.dma_start(slot_list[:], offs)
+        nc.sync.dma_start(first_list[:], pos1)
         nc.vector.memset(token_scales[:].bitcast(I32), 0)
         for q in range(4):
             nc.sync.dma_start(
                 out=token_scales[32 * q : 32 * q + 16, :].bitcast(I32),
                 in_=x_scales[:, 4 * q : 4 * q + 4, :].bitcast(I32),
             )
-        load_and_round(0)
-        load_and_round(1)
         load_words(0)
+        load_weights(0)
+        for a in range(1, PASSES):
+            load_words(a)
+        load_weights(1)
+        nc.sync.dma_start(out=bias[:], in_=b)
+        for e in range(2, E):
+            load_weights(e)
+        nc.sync.dma_start(second_list[:], pos2)
+
         for lo, hi in WIDE:
             gather_scales(lo, hi)
-        quantise(0)
-        quantise(1)
-        for e in (2, 3, 4):
-            load_and_round(e)
-        load_words(1)
-        for lo, hi in WIDE:
-            gather_words(0, lo, hi)
-        for e in (2, 3, 4):
-            quantise(e)
-        for e in (5, 6, 7):
-            load_and_round(e)
-        load_words(2)
-        load_and_round(8)
-        load_words(3)
-        nc.sync.dma_start(out=bias[:], in_=b)
-        nc.sync.dma_start(first_list[:], pos1)
-        nc.sync.dma_start(second_list[:], pos2)
-        for lo, hi in WIDE:
-            gather_words(1, lo, hi)
-        quantise(5)
-        quantise(6)
-        load_and_round(9)
-        load_and_round(10)
-        group(0)
-        for e in (7, 8, 9):
-            quantise(e)
-        load_and_round(11)
-        load_and_round(12)
-        load_and_round(13)
-        finish(0)
-        group(1)
-        for e in (10, 11):
-            quantise(e)
-        load_and_round(14)
-        load_and_round(15)
-        finish(1)
-        group(2)
-        quantise(12)
-        quantise(13)
-        finish(2)
-        group(3)
-        quantise(14)
-        quantise(15)
-        finish(3)
-        group(4)
-        group(5)
-        finish(4)
-        finish(5)
+        gather_words(0, E)
+        for e in range(E):
+            round_and_quantise(e)
+            multiply(e)
+            if e % 2 == 1 and e >= 3:
+                activate(e - 3, raw[e])
+                activate(e - 2, raw[e])
+            if e == 0:
+                gather_words(1, 0)
+            if e % 2 == 1 and (e + 3) // 2 < PAIRS:
+                gather_words((e + 3) // 2, e)
+        activate(E - 2, raw[E - 1])
+        last = raw[E - 2][:, 0:C]
+        nc.vector.tensor_scalar(
+            out=last, in0=sums[E - 1][:], scalar1=bias[:, E - 1 : E], scalar2=0.0, op0=ALU.add, op1=ALU.max
+        )
+        nc.vector.tensor_tensor(out=y[:, (E - 1) * C : E * C], in0=last, in1=last, op=ALU.mult)
 
         gates = []
         for r in range(2):
-            gate_r = wide.tile([P, T], F32, name="gate_r", tag="wide")
+            gate_r = wide_tile(2 + 2 * r, F32, "gate%d" % r)
             nc.sync.dma_start(out=gate_r[:], in_=gate[r])
             gates.append(gate_r)
-        first = wide.tile([P, T], F32, name="first", tag="wide")
-        second = wide.tile([P, T], F32, name="second", tag="wide")
-        total = wide.tile([P, T], F32, name="total", tag="wide")
+        first = wide_tile(6, F32, "first")
+        second = wide_tile(8, F32, "second")
+        total = wide_tile(10, F32, "total")
 
         def fetch(dst, lst, r, lo, hi):
             nc.vector.tensor_tensor(

@@ -1,6 +1,7 @@
 from contextlib import ExitStack
 
 import concourse.mybir as mybir
+from concourse.masks import make_identity
 
 K, T, E, C, N = 2048, 2048, 16, 256, 128
 SLOTS = E * C
@@ -21,8 +22,20 @@ ALU = mybir.AluOpType
 
 WIDE = [(0, 1536), (1536, 3072), (3072, 4096)]
 PAIRS = E // 2
-PAIR = 2 * C
-CHUNKS = [(0, 1024), (1024, 1664), (1664, 1920), (1920, 2048)]
+W = PASSES * N
+PIECES = [
+    ((0, 4), (0, 1), 16),
+    ((0, 4), (2, 3), 0),
+    ((4, 8), (0, 1), 2),
+    ((4, 8), (2, 3), 4),
+    ((8, 12), (0, 1), 6),
+    ((8, 12), (2, 3), 8),
+    ((12, 14), (0, 1, 2, 3), 10),
+    ((14, 16), (0, 1), 12),
+    ((14, 16), (2,), 14),
+]
+TURNED = [(0, 512), (512, 1024), (1024, 1280)]
+ADDED = [(1280, 1664), (1664, 1920), (1920, 2048)]
 RUN = 4
 
 
@@ -33,8 +46,8 @@ def tile_moe_pkd_lin_relu2_kernel(
     with ExitStack() as ctx:
         keep = ctx.enter_context(tc.tile_pool(name="keep", bufs=1))
         wide = ctx.enter_context(tc.tile_pool(name="wide", bufs=1))
-        half = ctx.enter_context(tc.tile_pool(name="half", bufs=5))
-        small = ctx.enter_context(tc.tile_pool(name="small", bufs=4))
+        half = ctx.enter_context(tc.tile_pool(name="half", bufs=3))
+        small = ctx.enter_context(tc.tile_pool(name="small", bufs=2))
         psum = ctx.enter_context(tc.psum_pool(name="psum", bufs=8))
 
         slot_list = keep.tile([P, SLOTS // 16], U16, name="slot_list")
@@ -45,6 +58,8 @@ def tile_moe_pkd_lin_relu2_kernel(
         token_words = [keep.tile([P, T], I32, name="token_words%d" % a, align_bytes=64) for a in range(PASSES)]
         bias = keep.tile([P, E], F32, name="bias")
         y = keep.tile([P, SLOTS], F32, name="y")
+        identity = keep.tile([P, P], F32, name="identity")
+        make_identity(nc, identity[:])
 
         raw = {}
         rounded = {}
@@ -66,47 +81,70 @@ def tile_moe_pkd_lin_relu2_kernel(
                 in_=w[e].rearrange("(a p j) n -> p a (j n)", a=PASSES, j=PACK),
             )
 
-        def round_and_quantise(e):
-            rounded[e] = half.tile([P, PASSES * N * PACK], BF16, name="rounded", align_bytes=64)
+        def round_weights(e):
+            if e % 2 == 0:
+                rounded[e // 2] = half.tile([P, 2 * W * PACK], BF16, name="rounded", align_bytes=64)
+            own = rounded[e // 2][:, (e % 2) * W * PACK : (e % 2 + 1) * W * PACK]
             nc.scalar.copy(
-                out=rounded[e][:].rearrange("p (a c i j) -> p a c j i", a=PASSES, i=RUN, j=PACK),
+                out=own.rearrange("p (a c i j) -> p a c j i", a=PASSES, i=RUN, j=PACK),
                 in_=raw[e][:].rearrange("p (a j c i) -> p a c j i", a=PASSES, j=PACK, i=RUN),
             )
-            w_codes[e] = small.tile([P, PASSES * N], U32, name="w_codes", align_bytes=64)
-            w_scales[e] = small.tile([P, PASSES * N], U8, name="w_scales", align_bytes=64)
-            nc.vector.quantize_mx(out=w_codes[e][:].bitcast(FP8X4), scales=w_scales[e][:], in_=rounded[e][:])
+
+        def quantise(lo, hi):
+            m = lo // 2
+            if lo % 2 == 0:
+                w_codes[m] = small.tile([P, 2 * W], U32, name="w_codes", align_bytes=64)
+                w_scales[m] = small.tile([P, 2 * W], U8, name="w_scales", align_bytes=64)
+            c0, c1 = (lo - 2 * m) * W, (hi - 2 * m) * W
+            nc.vector.quantize_mx(
+                out=w_codes[m][:, c0:c1].bitcast(FP8X4),
+                scales=w_scales[m][:, c0:c1],
+                in_=rounded[m][:, c0 * PACK : c1 * PACK],
+            )
 
         def gather_scales(lo, hi):
             nc.vector.tensor_copy(
                 out=slot_scales[:, lo:hi], in_=token_scales[:].indirect(slot_list[:, lo // 16 : hi // 16])
             )
 
-        def gather_words(m, place):
-            slot_words[m] = wide_tile(place, U32, "slot_words%d" % m)
-            for a in range(PASSES):
-                nc.vector.tensor_copy(
-                    out=slot_words[m][:, a * PAIR : (a + 1) * PAIR],
-                    in_=token_words[a][:].bitcast(U32).indirect(slot_list[:, m * PAIR // 16 : (m + 1) * PAIR // 16]),
-                )
+        def gather_pass(dst, a, lo, hi):
+            nc.vector.tensor_copy(
+                out=dst, in_=token_words[a][:].bitcast(U32).indirect(slot_list[:, lo * C // 16 : hi * C // 16])
+            )
+            for e in range(lo, hi):
+                slot_words[e, a] = dst[:, (e - lo) * C : (e - lo + 1) * C]
 
-        def multiply(e):
-            sums[e] = psum.tile([P, C], F32, name="sums")
-            for a in range(PASSES):
-                first_word = a * PAIR + (e % 2) * C
+        def gather_piece(piece):
+            (lo, hi), passes, place = piece
+            words = wide_tile(place, U32, "slot_words%d" % place)
+            width = (hi - lo) * C
+            for i, a in enumerate(passes):
+                gather_pass(words[:, i * width : (i + 1) * width], a, lo, hi)
+
+        def multiply(e, passes):
+            for a in passes:
+                if a == 0:
+                    sums[e] = psum.tile([P, C], F32, name="sums", tag="bank")
+                first_word = (e % 2) * W + a * N
                 nc.tensor.matmul_mx(
                     out=sums[e][:],
-                    lhsT=w_codes[e][:, a * N : (a + 1) * N].bitcast(FP8X4),
-                    lhsT_scale=w_scales[e][:, a * N : (a + 1) * N],
-                    rhs=slot_words[e // 2][:, first_word : first_word + C].bitcast(FP8X4),
+                    lhsT=w_codes[e // 2][:, first_word : first_word + N].bitcast(FP8X4),
+                    lhsT_scale=w_scales[e // 2][:, first_word : first_word + N],
+                    rhs=slot_words[e, a].bitcast(FP8X4),
                     rhs_scale=slot_scales[4 * a : P, e * C : (e + 1) * C],
                     start=(a == 0),
                     stop=(a == PASSES - 1),
                 )
 
-        def activate(e, scratch):
-            positive = scratch[:, (e % 4) * C : (e % 4 + 1) * C]
-            nc.scalar.activation(out=positive, in_=sums[e][:], func=ACT.Relu, bias=bias[:, e : e + 1])
-            nc.scalar.activation(out=y[:, e * C : (e + 1) * C], in_=positive, func=ACT.Square)
+        def activate(lo, hi, scratch):
+            for e in range(lo, hi):
+                nc.scalar.activation(
+                    out=scratch[:, (e - lo) * C : (e - lo + 1) * C],
+                    in_=sums[e][:],
+                    func=ACT.Relu,
+                    bias=bias[:, e : e + 1],
+                )
+            nc.scalar.activation(out=y[:, lo * C : hi * C], in_=scratch[:, 0 : (hi - lo) * C], func=ACT.Square)
 
         nc.sync.dma_start(slot_list[:], offs)
         nc.sync.dma_start(first_list[:], pos1)
@@ -128,19 +166,34 @@ def tile_moe_pkd_lin_relu2_kernel(
 
         for lo, hi in WIDE:
             gather_scales(lo, hi)
-        gather_words(0, E)
-        for e in range(E):
-            round_and_quantise(e)
-            multiply(e)
-            if e % 2 == 1 and e >= 3:
-                activate(e - 3, raw[e])
-                activate(e - 2, raw[e])
-            if e == 0:
-                gather_words(1, 0)
-            if e % 2 == 1 and (e + 3) // 2 < PAIRS:
-                gather_words((e + 3) // 2, e)
-        activate(E - 2, raw[E - 1])
-        last = raw[E - 2][:, 0:C]
+        gather_piece(PIECES[0])
+        every = range(PASSES)
+        for m in range(PAIRS - 1):
+            round_weights(2 * m)
+            gather_piece(PIECES[m + 1])
+            round_weights(2 * m + 1)
+            quantise(2 * m, 2 * m + 2)
+            multiply(2 * m, every)
+            multiply(2 * m + 1, every)
+            if 0 < m < PAIRS - 3:
+                activate(2 * m - 2, 2 * m, raw[2 * m + 1][:, 0 : 2 * C])
+            if m == PAIRS - 2:
+                activate(E - 8, E - 6, raw[E - 3][:, 0 : 2 * C])
+        round_weights(E - 2)
+        gather_piece(PIECES[PAIRS])
+        quantise(E - 2, E - 1)
+        multiply(E - 2, range(PASSES - 1))
+        round_weights(E - 1)
+        activate(E - 6, E - 4, raw[E - 3][:, 2 * C : 4 * C])
+        activate(E - 4, E - 2, raw[E - 3][:, 4 * C : 6 * C])
+        quantise(E - 1, E)
+        multiply(E - 1, range(PASSES - 1))
+        words = wide_tile(E - 1, U32, "last_words")
+        for e in (E - 2, E - 1):
+            gather_pass(words[:, (e % 2) * C : (e % 2 + 1) * C], PASSES - 1, e, e + 1)
+            multiply(e, [PASSES - 1])
+        activate(E - 2, E - 1, raw[E - 5][:, 0:C])
+        last = raw[E - 5][:, C : 2 * C]
         nc.vector.tensor_scalar(
             out=last, in0=sums[E - 1][:], scalar1=bias[:, E - 1 : E], scalar2=0.0, op0=ALU.add, op1=ALU.max
         )
@@ -148,12 +201,12 @@ def tile_moe_pkd_lin_relu2_kernel(
 
         gates = []
         for r in range(2):
-            gate_r = wide_tile(2 + 2 * r, F32, "gate%d" % r)
+            gate_r = wide_tile(1 + 2 * r, F32, "gate%d" % r)
             nc.sync.dma_start(out=gate_r[:], in_=gate[r])
             gates.append(gate_r)
-        first = wide_tile(6, F32, "first")
-        second = wide_tile(8, F32, "second")
-        total = wide_tile(10, F32, "total")
+        first = wide_tile(5, F32, "first")
+        second = wide_tile(7, F32, "second")
+        total = wide_tile(9, F32, "total")
 
         def fetch(dst, lst, r, lo, hi):
             nc.vector.tensor_tensor(
@@ -164,9 +217,34 @@ def tile_moe_pkd_lin_relu2_kernel(
             nc.vector.tensor_tensor(out=total[:, lo:hi], in0=first[:, lo:hi], in1=second[:, lo:hi], op=ALU.add)
             nc.sync.dma_start(out=out[:, lo:hi], in_=total[:, lo:hi])
 
-        for i, (lo, hi) in enumerate(CHUNKS):
+        def combine_turned(lo, hi):
+            width = hi - lo
+            summed = psum.tile([P, width], F32, name="summed", tag="bank")
+            for c in range(0, width, P):
+                for r, term in enumerate((first, second)):
+                    nc.tensor.matmul(
+                        summed[:, c : c + P],
+                        term[:, lo + c : lo + c + P],
+                        identity[:],
+                        start=(r == 0),
+                        stop=(r == 1),
+                        is_transpose=True,
+                    )
+            nc.scalar.copy(out=turned[:, lo:hi], in_=summed[:])
+            back = psum.tile([P, width], F32, name="back", tag="bank")
+            for c in range(0, width, P):
+                nc.tensor.transpose(back[:, c : c + P], turned[:, lo + c : lo + c + P], identity[:])
+            nc.scalar.copy(out=total[:, lo:hi], in_=back[:])
+            nc.scalar.dma_start(out=out[:, lo:hi], in_=total[:, lo:hi])
+
+        turned = wide_tile(E - 3, F32, "turned")
+        for lo, hi in TURNED:
+            fetch(first, first_list, 0, lo, hi)
+            fetch(second, second_list, 1, lo, hi)
+            combine_turned(lo, hi)
+        for i, (lo, hi) in enumerate(ADDED):
             fetch(first, first_list, 0, lo, hi)
             if i > 0:
-                combine(*CHUNKS[i - 1])
+                combine(*ADDED[i - 1])
             fetch(second, second_list, 1, lo, hi)
-        combine(*CHUNKS[-1])
+        combine(*ADDED[-1])

@@ -32,7 +32,7 @@ PIECES = [
     ((8, 12), (2, 3), 8),
     ((12, 14), (0, 1, 2, 3), 10),
     ((14, 16), (0, 1), 12),
-    ((14, 16), (2,), 14),
+    ((14, 16), (2, 3), 13),
 ]
 TURNED = [(0, 512), (512, 1024), (1024, 1280)]
 ADDED = [(1280, 1664), (1664, 1920), (1920, 2048)]
@@ -61,6 +61,7 @@ def tile_moe_pkd_lin_relu2_kernel(
         identity = keep.tile([P, P], F32, name="identity")
         make_identity(nc, identity[:])
 
+        raw_end = keep.tile([P, W], F32, name="raw_end")
         raw = {}
         rounded = {}
         w_codes = {}
@@ -74,11 +75,33 @@ def tile_moe_pkd_lin_relu2_kernel(
         def load_words(a):
             nc.sync.dma_start(out=token_words[a][:], in_=x_words[a].rearrange("p t r -> p (t r)").bitcast(I32))
 
+        def load_passes(dst, e, a0, a1):
+            nc.sync.dma_start(
+                out=dst[:, 0 : (a1 - a0) * W].rearrange("p (a m) -> p a m", m=W),
+                in_=w[e].rearrange("(a p j) n -> p a (j n)", a=PASSES, j=PACK)[:, a0:a1, :],
+            )
+
         def load_weights(e):
             raw[e] = wide_tile(e, F32, "raw%d" % e)
-            nc.sync.dma_start(
-                out=raw[e][:].rearrange("p (a m) -> p a m", a=PASSES),
-                in_=w[e].rearrange("(a p j) n -> p a (j n)", a=PASSES, j=PACK),
+            if e < E - 1:
+                load_passes(raw[e], e, 0, PASSES)
+            else:
+                load_passes(raw[e], e, 0, PASSES - 1)
+                load_passes(raw_end, e, PASSES - 1, PASSES)
+
+        def round_passes(src, e, a0, a1):
+            own = rounded[e // 2][:, ((e % 2) * PASSES + a0) * W : ((e % 2) * PASSES + a1) * W]
+            nc.scalar.copy(
+                out=own.rearrange("p (a c i j) -> p a c j i", a=a1 - a0, i=RUN, j=PACK),
+                in_=src[:, 0 : (a1 - a0) * W].rearrange("p (a j c i) -> p a c j i", a=a1 - a0, j=PACK, i=RUN),
+            )
+
+        def quantise_passes(e, a0, a1):
+            c0, c1 = (e % 2) * W + a0 * N, (e % 2) * W + a1 * N
+            nc.vector.quantize_mx(
+                out=w_codes[e // 2][:, c0:c1].bitcast(FP8X4),
+                scales=w_scales[e // 2][:, c0:c1],
+                in_=rounded[e // 2][:, c0 * PACK : c1 * PACK],
             )
 
         def round_weights(e):
@@ -179,20 +202,20 @@ def tile_moe_pkd_lin_relu2_kernel(
                 activate(2 * m - 2, 2 * m, raw[2 * m + 1][:, 0 : 2 * C])
             if m == PAIRS - 2:
                 activate(E - 8, E - 6, raw[E - 3][:, 0 : 2 * C])
-        round_weights(E - 2)
         gather_piece(PIECES[PAIRS])
+        round_weights(E - 2)
         quantise(E - 2, E - 1)
-        multiply(E - 2, range(PASSES - 1))
-        round_weights(E - 1)
-        activate(E - 6, E - 4, raw[E - 3][:, 2 * C : 4 * C])
-        activate(E - 4, E - 2, raw[E - 3][:, 4 * C : 6 * C])
-        quantise(E - 1, E)
+        multiply(E - 2, every)
+        activate(E - 6, E - 4, raw[E - 2][:, 0 : 2 * C])
+        round_passes(raw[E - 1], E - 1, 0, PASSES - 1)
+        quantise_passes(E - 1, 0, 2)
+        quantise_passes(E - 1, 2, 3)
         multiply(E - 1, range(PASSES - 1))
-        words = wide_tile(E - 1, U32, "last_words")
-        for e in (E - 2, E - 1):
-            gather_pass(words[:, (e % 2) * C : (e % 2 + 1) * C], PASSES - 1, e, e + 1)
-            multiply(e, [PASSES - 1])
-        activate(E - 2, E - 1, raw[E - 5][:, 0:C])
+        activate(E - 4, E - 2, raw[E - 1][:, 0 : 2 * C])
+        round_passes(raw_end, E - 1, PASSES - 1, PASSES)
+        quantise_passes(E - 1, PASSES - 1, PASSES)
+        multiply(E - 1, [PASSES - 1])
+        activate(E - 2, E - 1, raw_end[:, 0:C])
         last = raw[E - 5][:, C : 2 * C]
         nc.vector.tensor_scalar(
             out=last, in0=sums[E - 1][:], scalar1=bias[:, E - 1 : E], scalar2=0.0, op0=ALU.add, op1=ALU.max

@@ -37,6 +37,7 @@ PIECES = [
 TURNED = [(0, 512), (512, 1024), (1024, 1280)]
 ADDED = [(1280, 1664), (1664, 1920), (1920, 2048)]
 RUN = 4
+LAG = 2
 
 
 def tile_moe_pkd_lin_relu2_kernel(
@@ -59,6 +60,7 @@ def tile_moe_pkd_lin_relu2_kernel(
         bias = keep.tile([P, E], F32, name="bias")
         y = keep.tile([P, SLOTS], F32, name="y")
         identity = keep.tile([P, P], F32, name="identity")
+        nc.gpsimd.memset(token_scales[:].bitcast(I32), 0)
         make_identity(nc, identity[:])
 
         raw_end = keep.tile([P, W], F32, name="raw_end")
@@ -171,7 +173,6 @@ def tile_moe_pkd_lin_relu2_kernel(
 
         nc.sync.dma_start(slot_list[:], offs)
         nc.sync.dma_start(first_list[:], pos1)
-        nc.vector.memset(token_scales[:].bitcast(I32), 0)
         for q in range(4):
             nc.sync.dma_start(
                 out=token_scales[32 * q : 32 * q + 16, :].bitcast(I32),
@@ -198,10 +199,8 @@ def tile_moe_pkd_lin_relu2_kernel(
             quantise(2 * m, 2 * m + 2)
             multiply(2 * m, every)
             multiply(2 * m + 1, every)
-            if 0 < m < PAIRS - 3:
-                activate(2 * m - 2, 2 * m, raw[2 * m + 1][:, 0 : 2 * C])
-            if m == PAIRS - 2:
-                activate(E - 8, E - 6, raw[E - 3][:, 0 : 2 * C])
+            if m >= LAG:
+                activate(2 * (m - LAG), 2 * (m - LAG + 1), raw[2 * m + 1][:, 0 : 2 * C])
         gather_piece(PIECES[PAIRS])
         round_weights(E - 2)
         quantise(E - 2, E - 1)
@@ -211,10 +210,10 @@ def tile_moe_pkd_lin_relu2_kernel(
         quantise_passes(E - 1, 0, 2)
         quantise_passes(E - 1, 2, 3)
         multiply(E - 1, range(PASSES - 1))
-        activate(E - 4, E - 2, raw[E - 1][:, 0 : 2 * C])
         round_passes(raw_end, E - 1, PASSES - 1, PASSES)
         quantise_passes(E - 1, PASSES - 1, PASSES)
         multiply(E - 1, [PASSES - 1])
+        activate(E - 4, E - 2, raw_end[:, 0 : 2 * C])
         activate(E - 2, E - 1, raw_end[:, 0:C])
         last = raw[E - 5][:, C : 2 * C]
         nc.vector.tensor_scalar(

@@ -32,12 +32,14 @@ PIECES = [
     ((8, 12), (2, 3), 8),
     ((12, 14), (0, 1, 2, 3), 10),
     ((14, 16), (0, 1), 12),
-    ((14, 16), (2, 3), 13),
+    ((14, 15), (2, 3), 13),
+    ((15, 16), (2, 3), 14),
 ]
-TURNED = [(0, 512), (512, 1024), (1024, 1280)]
-ADDED = [(1280, 1664), (1664, 1920), (1920, 2048)]
+TURNED = [(lo, lo + 256) for lo in range(0, 1536, 256)]
+ADDED = [(1536, 1792), (1792, 1920), (1920, 2048)]
 RUN = 4
 LAG = 2
+ON_GPSIMD = (1, 3, 5, 7, 9, 11)
 
 
 def tile_moe_pkd_lin_relu2_kernel(
@@ -47,9 +49,9 @@ def tile_moe_pkd_lin_relu2_kernel(
     with ExitStack() as ctx:
         keep = ctx.enter_context(tc.tile_pool(name="keep", bufs=1))
         wide = ctx.enter_context(tc.tile_pool(name="wide", bufs=1))
-        half = ctx.enter_context(tc.tile_pool(name="half", bufs=3))
+        half = ctx.enter_context(tc.tile_pool(name="half", bufs=1))
         small = ctx.enter_context(tc.tile_pool(name="small", bufs=2))
-        psum = ctx.enter_context(tc.psum_pool(name="psum", bufs=8))
+        psum = ctx.enter_context(tc.psum_pool(name="psum", bufs=1))
 
         slot_list = keep.tile([P, SLOTS // 16], U16, name="slot_list")
         first_list = keep.tile([P, T // 16], U16, name="first_list")
@@ -74,6 +76,10 @@ def tile_moe_pkd_lin_relu2_kernel(
         def wide_tile(place, dtype, name):
             return wide.tile([P, T], dtype, name=name, tag="wide%d" % place, align_bytes=64)
 
+        def rounded_tile(e):
+            place = (e // 2) % 3 if e <= 2 * len(ON_GPSIMD) else e - E + 6
+            return half.tile([P, W * PACK], BF16, name="rounded%d" % e, tag="rounded%d" % place, align_bytes=64)
+
         def load_words(a):
             nc.sync.dma_start(out=token_words[a][:], in_=x_words[a].rearrange("p t r -> p (t r)").bitcast(I32))
 
@@ -92,7 +98,7 @@ def tile_moe_pkd_lin_relu2_kernel(
                 load_passes(raw_end, e, PASSES - 1, PASSES)
 
         def round_passes(src, e, a0, a1):
-            own = rounded[e // 2][:, ((e % 2) * PASSES + a0) * W : ((e % 2) * PASSES + a1) * W]
+            own = rounded[e][:, a0 * W : a1 * W]
             nc.scalar.copy(
                 out=own.rearrange("p (a c i j) -> p a c j i", a=a1 - a0, i=RUN, j=PACK),
                 in_=src[:, 0 : (a1 - a0) * W].rearrange("p (a j c i) -> p a c j i", a=a1 - a0, j=PACK, i=RUN),
@@ -103,13 +109,23 @@ def tile_moe_pkd_lin_relu2_kernel(
             nc.vector.quantize_mx(
                 out=w_codes[e // 2][:, c0:c1].bitcast(FP8X4),
                 scales=w_scales[e // 2][:, c0:c1],
-                in_=rounded[e // 2][:, c0 * PACK : c1 * PACK],
+                in_=rounded[e][:, a0 * W : a1 * W],
             )
 
         def round_weights(e):
-            if e % 2 == 0:
-                rounded[e // 2] = half.tile([P, 2 * W * PACK], BF16, name="rounded", align_bytes=64)
-            own = rounded[e // 2][:, (e % 2) * W * PACK : (e % 2 + 1) * W * PACK]
+            if e in ON_GPSIMD:
+                rounded[e] = rounded_tile(e)
+                nc.gpsimd.tensor_scalar(
+                    out=rounded[e][:].rearrange("p (a c j) -> p a c j", a=PASSES, j=PACK),
+                    in0=raw[e][:].rearrange("p (a j c) -> p a c j", a=PASSES, j=PACK),
+                    scalar1=1.0,
+                    scalar2=0.0,
+                    op0=ALU.mult,
+                    op1=ALU.add,
+                )
+                return
+            rounded[e] = rounded_tile(e)
+            own = rounded[e][:]
             nc.scalar.copy(
                 out=own.rearrange("p (a c i j) -> p a c j i", a=PASSES, i=RUN, j=PACK),
                 in_=raw[e][:].rearrange("p (a j c i) -> p a c j i", a=PASSES, j=PACK, i=RUN),
@@ -120,12 +136,8 @@ def tile_moe_pkd_lin_relu2_kernel(
             if lo % 2 == 0:
                 w_codes[m] = small.tile([P, 2 * W], U32, name="w_codes", align_bytes=64)
                 w_scales[m] = small.tile([P, 2 * W], U8, name="w_scales", align_bytes=64)
-            c0, c1 = (lo - 2 * m) * W, (hi - 2 * m) * W
-            nc.vector.quantize_mx(
-                out=w_codes[m][:, c0:c1].bitcast(FP8X4),
-                scales=w_scales[m][:, c0:c1],
-                in_=rounded[m][:, c0 * PACK : c1 * PACK],
-            )
+            for e in range(lo, hi):
+                quantise_passes(e, 0, PASSES)
 
         def gather_scales(lo, hi):
             nc.vector.tensor_copy(
@@ -149,7 +161,7 @@ def tile_moe_pkd_lin_relu2_kernel(
         def multiply(e, passes):
             for a in passes:
                 if a == 0:
-                    sums[e] = psum.tile([P, C], F32, name="sums", tag="bank")
+                    sums[e] = psum.tile([P, C], F32, name="sums", tag="bank%d" % (e % 8))
                 first_word = (e % 2) * W + a * N
                 nc.tensor.matmul_mx(
                     out=sums[e][:],
@@ -194,27 +206,30 @@ def tile_moe_pkd_lin_relu2_kernel(
         every = range(PASSES)
         for m in range(PAIRS - 1):
             round_weights(2 * m)
-            gather_piece(PIECES[m + 1])
-            round_weights(2 * m + 1)
-            quantise(2 * m, 2 * m + 2)
-            multiply(2 * m, every)
-            multiply(2 * m + 1, every)
             if m >= LAG:
-                activate(2 * (m - LAG), 2 * (m - LAG + 1), raw[2 * m + 1][:, 0 : 2 * C])
+                activate(2 * (m - LAG), 2 * (m - LAG + 1), raw[2 * m][:, 0 : 2 * C])
+            quantise(2 * m, 2 * m + 1)
+            gather_piece(PIECES[m + 1])
+            multiply(2 * m, every)
+            round_weights(2 * m + 1)
+            quantise(2 * m + 1, 2 * m + 2)
+            multiply(2 * m + 1, every)
         gather_piece(PIECES[PAIRS])
         round_weights(E - 2)
         quantise(E - 2, E - 1)
         multiply(E - 2, every)
-        activate(E - 6, E - 4, raw[E - 2][:, 0 : 2 * C])
+        gather_piece(PIECES[PAIRS + 1])
+        rounded[E - 1] = rounded_tile(E - 1)
         round_passes(raw[E - 1], E - 1, 0, PASSES - 1)
+        round_passes(raw_end, E - 1, PASSES - 1, PASSES)
         quantise_passes(E - 1, 0, 2)
         quantise_passes(E - 1, 2, 3)
         multiply(E - 1, range(PASSES - 1))
-        round_passes(raw_end, E - 1, PASSES - 1, PASSES)
         quantise_passes(E - 1, PASSES - 1, PASSES)
         multiply(E - 1, [PASSES - 1])
-        activate(E - 4, E - 2, raw_end[:, 0 : 2 * C])
-        activate(E - 2, E - 1, raw_end[:, 0:C])
+        activate(E - 6, E - 4, raw_end[:, 0 : 2 * C])
+        activate(E - 4, E - 2, raw[E - 1][:, 0 : 2 * C])
+        activate(E - 2, E - 1, raw[E - 1][:, 2 * C : 3 * C])
         last = raw[E - 5][:, C : 2 * C]
         nc.vector.tensor_scalar(
             out=last, in0=sums[E - 1][:], scalar1=bias[:, E - 1 : E], scalar2=0.0, op0=ALU.add, op1=ALU.max
@@ -239,9 +254,9 @@ def tile_moe_pkd_lin_relu2_kernel(
             nc.vector.tensor_tensor(out=total[:, lo:hi], in0=first[:, lo:hi], in1=second[:, lo:hi], op=ALU.add)
             nc.sync.dma_start(out=out[:, lo:hi], in_=total[:, lo:hi])
 
-        def combine_turned(lo, hi):
+        def sum_turned(i, lo, hi):
             width = hi - lo
-            summed = psum.tile([P, width], F32, name="summed", tag="bank")
+            summed = psum.tile([P, width], F32, name="summed", tag="bank%d" % (i % 2))
             for c in range(0, width, P):
                 for r, term in enumerate((first, second)):
                     nc.tensor.matmul(
@@ -253,17 +268,23 @@ def tile_moe_pkd_lin_relu2_kernel(
                         is_transpose=True,
                     )
             nc.scalar.copy(out=turned[:, lo:hi], in_=summed[:])
-            back = psum.tile([P, width], F32, name="back", tag="bank")
+
+        def turn_back(i, lo, hi):
+            width = hi - lo
+            back = psum.tile([P, width], F32, name="back", tag="bank%d" % (2 + i % 2))
             for c in range(0, width, P):
                 nc.tensor.transpose(back[:, c : c + P], turned[:, lo + c : lo + c + P], identity[:])
             nc.scalar.copy(out=total[:, lo:hi], in_=back[:])
             nc.scalar.dma_start(out=out[:, lo:hi], in_=total[:, lo:hi])
 
         turned = wide_tile(E - 3, F32, "turned")
-        for lo, hi in TURNED:
+        for i, (lo, hi) in enumerate(TURNED):
             fetch(first, first_list, 0, lo, hi)
             fetch(second, second_list, 1, lo, hi)
-            combine_turned(lo, hi)
+            sum_turned(i, lo, hi)
+            if i > 0:
+                turn_back(i - 1, *TURNED[i - 1])
+        turn_back(len(TURNED) - 1, *TURNED[-1])
         for i, (lo, hi) in enumerate(ADDED):
             fetch(first, first_list, 0, lo, hi)
             if i > 0:

@@ -31,12 +31,11 @@ PIECES = [
     ((8, 12), (0, 1), 6),
     ((8, 12), (2, 3), 8),
     ((12, 14), (0, 1, 2, 3), 10),
-    ((14, 16), (0, 1), 12),
-    ((14, 15), (2, 3), 13),
-    ((15, 16), (2, 3), 14),
+    ((14, 15), (0, 1, 2, 3), 12),
+    ((15, 16), (0, 1), 13),
 ]
-TURNED = [(lo, lo + 256) for lo in range(0, 1536, 256)]
-ADDED = [(1536, 1792), (1792, 1920), (1920, 2048)]
+TURNED = [(0, 128)] + [(lo, lo + 256) for lo in range(128, 1408, 256)]
+ADDED = [(1408, 1664), (1664, 1920), (1920, 2048)]
 RUN = 4
 LAG = 2
 ON_GPSIMD = (1, 3, 5, 7, 9, 11)
@@ -97,19 +96,18 @@ def tile_moe_pkd_lin_relu2_kernel(
                 load_passes(raw[e], e, 0, PASSES - 1)
                 load_passes(raw_end, e, PASSES - 1, PASSES)
 
-        def round_passes(src, e, a0, a1):
-            own = rounded[e][:, a0 * W : a1 * W]
+        def round_passes(own, src, count):
             nc.scalar.copy(
-                out=own.rearrange("p (a c i j) -> p a c j i", a=a1 - a0, i=RUN, j=PACK),
-                in_=src[:, 0 : (a1 - a0) * W].rearrange("p (a j c i) -> p a c j i", a=a1 - a0, j=PACK, i=RUN),
+                out=own.rearrange("p (a c i j) -> p a c j i", a=count, i=RUN, j=PACK),
+                in_=src.rearrange("p (a j c i) -> p a c j i", a=count, j=PACK, i=RUN),
             )
 
-        def quantise_passes(e, a0, a1):
+        def quantise_passes(e, a0, a1, src):
             c0, c1 = (e % 2) * W + a0 * N, (e % 2) * W + a1 * N
             nc.vector.quantize_mx(
                 out=w_codes[e // 2][:, c0:c1].bitcast(FP8X4),
                 scales=w_scales[e // 2][:, c0:c1],
-                in_=rounded[e][:, a0 * W : a1 * W],
+                in_=src,
             )
 
         def round_weights(e):
@@ -137,7 +135,7 @@ def tile_moe_pkd_lin_relu2_kernel(
                 w_codes[m] = small.tile([P, 2 * W], U32, name="w_codes", align_bytes=64)
                 w_scales[m] = small.tile([P, 2 * W], U8, name="w_scales", align_bytes=64)
             for e in range(lo, hi):
-                quantise_passes(e, 0, PASSES)
+                quantise_passes(e, 0, PASSES, rounded[e][:])
 
         def gather_scales(lo, hi):
             nc.vector.tensor_copy(
@@ -218,23 +216,29 @@ def tile_moe_pkd_lin_relu2_kernel(
         round_weights(E - 2)
         quantise(E - 2, E - 1)
         multiply(E - 2, every)
-        gather_piece(PIECES[PAIRS + 1])
-        rounded[E - 1] = rounded_tile(E - 1)
-        round_passes(raw[E - 1], E - 1, 0, PASSES - 1)
-        round_passes(raw_end, E - 1, PASSES - 1, PASSES)
-        quantise_passes(E - 1, 0, 2)
-        quantise_passes(E - 1, 2, 3)
-        multiply(E - 1, range(PASSES - 1))
-        quantise_passes(E - 1, PASSES - 1, PASSES)
-        multiply(E - 1, [PASSES - 1])
+        front = keep.tile([P, 2 * W], BF16, name="front", tag="front", align_bytes=64)
+        rear = keep.tile([P, 2 * W], BF16, name="rear", align_bytes=64)
+        round_passes(front[:], raw[E - 1][:, 0 : 2 * W], 2)
+        round_passes(rear[:, 0:W], raw[E - 1][:, 2 * W : 3 * W], 1)
+        round_passes(rear[:, W : 2 * W], raw_end[:], 1)
+        quantise_passes(E - 1, 0, 2, front[:])
+        quantise_passes(E - 1, 2, 3, rear[:, 0:W])
+        last_words = keep.tile([P, 2 * C], U32, name="last_words", tag="front", align_bytes=64)
+        for a in (2, 3):
+            gather_pass(last_words[:, (a - 2) * C : (a - 1) * C], a, E - 1, E)
+        quantise_passes(E - 1, 3, 4, rear[:, W : 2 * W])
+        multiply(E - 1, every)
         activate(E - 6, E - 4, raw_end[:, 0 : 2 * C])
         activate(E - 4, E - 2, raw[E - 1][:, 0 : 2 * C])
         activate(E - 2, E - 1, raw[E - 1][:, 2 * C : 3 * C])
-        last = raw[E - 5][:, C : 2 * C]
-        nc.vector.tensor_scalar(
-            out=last, in0=sums[E - 1][:], scalar1=bias[:, E - 1 : E], scalar2=0.0, op0=ALU.add, op1=ALU.max
-        )
-        nc.vector.tensor_tensor(out=y[:, (E - 1) * C : E * C], in0=last, in1=last, op=ALU.mult)
+        last = raw[E - 5]
+        halves = [slice(h * N, (h + 1) * N) for h in range(2)]
+        for h in halves:
+            nc.vector.tensor_scalar(
+                out=last[:, h], in0=sums[E - 1][:, h], scalar1=bias[:, E - 1 : E], scalar2=0.0, op0=ALU.add, op1=ALU.max
+            )
+        for h in halves:
+            nc.vector.tensor_tensor(out=y[:, (E - 1) * C : E * C][:, h], in0=last[:, h], in1=last[:, h], op=ALU.mult)
 
         gates = []
         for r in range(2):
@@ -287,7 +291,7 @@ def tile_moe_pkd_lin_relu2_kernel(
         turn_back(len(TURNED) - 1, *TURNED[-1])
         for i, (lo, hi) in enumerate(ADDED):
             fetch(first, first_list, 0, lo, hi)
+            fetch(second, second_list, 1, lo, hi)
             if i > 0:
                 combine(*ADDED[i - 1])
-            fetch(second, second_list, 1, lo, hi)
         combine(*ADDED[-1])

@@ -23,21 +23,22 @@ ALU = mybir.AluOpType
 WIDE = [(0, 1536), (1536, 3072), (3072, 4096)]
 PAIRS = E // 2
 W = PASSES * N
+HEAD = 6
 PIECES = [
-    ((0, 4), (0, 1), 16),
-    ((0, 4), (2, 3), 0),
-    ((4, 8), (0, 1), 2),
-    ((4, 8), (2, 3), 4),
-    ((8, 12), (0, 1), 6),
-    ((8, 12), (2, 3), 8),
-    ((12, 14), (0, 1, 2, 3), 10),
-    ((14, 15), (0, 1, 2, 3), 12),
-    ((15, 16), (0, 1), 13),
+    ((0, 6), (2,), 0),
+    ((0, 6), (3,), 2),
+    ((6, 10), (0, 1), 4),
+    ((6, 10), (2, 3), 6),
+    ((10, 14), (0, 1), 8),
+    ((10, 14), (2, 3), 10),
+    ((14, 16), (0, 1), 12),
+    ((14, 15), (2, 3), 13),
 ]
-TURNED = [(0, 128)] + [(lo, lo + 256) for lo in range(128, 1408, 256)]
-ADDED = [(1408, 1664), (1664, 1920), (1920, 2048)]
+TURNED = [(0, 256), (256, 768), (768, 1280)]
+ADDED = [(1280, 1792), (1792, 1920), (1920, 2048)]
+BLOCK = 256
 RUN = 4
-LAG = 2
+BEHIND = {6: (0,), 8: (1, 2), 10: (3,)}
 ON_GPSIMD = (1, 3, 5, 7, 9, 11)
 
 
@@ -66,7 +67,6 @@ def tile_moe_pkd_lin_relu2_kernel(
 
         raw_end = keep.tile([P, W], F32, name="raw_end")
         raw = {}
-        rounded = {}
         w_codes = {}
         w_scales = {}
         slot_words = {}
@@ -75,9 +75,11 @@ def tile_moe_pkd_lin_relu2_kernel(
         def wide_tile(place, dtype, name):
             return wide.tile([P, T], dtype, name=name, tag="wide%d" % place, align_bytes=64)
 
-        def rounded_tile(e):
-            place = (e // 2) % 3 if e <= 2 * len(ON_GPSIMD) else e - E + 6
-            return half.tile([P, W * PACK], BF16, name="rounded%d" % e, tag="rounded%d" % place, align_bytes=64)
+        strip = half.tile([P, (PAIRS - 1) * W * PACK], BF16, name="strip", align_bytes=64)
+
+        def rounded(lo, hi):
+            room = lo // 2 if lo < E - 3 else lo - (E - 3)
+            return strip[:, room * W * PACK : (room + hi - lo) * W * PACK]
 
         def load_words(a):
             nc.sync.dma_start(out=token_words[a][:], in_=x_words[a].rearrange("p t r -> p (t r)").bitcast(I32))
@@ -89,10 +91,11 @@ def tile_moe_pkd_lin_relu2_kernel(
             )
 
         def load_weights(e):
-            raw[e] = wide_tile(e, F32, "raw%d" % e)
             if e < E - 1:
+                raw[e] = wide_tile(e, F32, "raw%d" % e)
                 load_passes(raw[e], e, 0, PASSES)
             else:
+                raw[e] = keep.tile([P, (PASSES - 1) * W], F32, name="raw_last")
                 load_passes(raw[e], e, 0, PASSES - 1)
                 load_passes(raw_end, e, PASSES - 1, PASSES)
 
@@ -102,40 +105,33 @@ def tile_moe_pkd_lin_relu2_kernel(
                 in_=src.rearrange("p (a j c i) -> p a c j i", a=count, j=PACK, i=RUN),
             )
 
-        def quantise_passes(e, a0, a1, src):
-            c0, c1 = (e % 2) * W + a0 * N, (e % 2) * W + a1 * N
-            nc.vector.quantize_mx(
-                out=w_codes[e // 2][:, c0:c1].bitcast(FP8X4),
-                scales=w_scales[e // 2][:, c0:c1],
-                in_=src,
-            )
+        def quantise_into(codes, scales, src):
+            nc.vector.quantize_mx(out=codes.bitcast(FP8X4), scales=scales, in_=src)
 
         def round_weights(e):
             if e in ON_GPSIMD:
-                rounded[e] = rounded_tile(e)
                 nc.gpsimd.tensor_scalar(
-                    out=rounded[e][:].rearrange("p (a c j) -> p a c j", a=PASSES, j=PACK),
+                    out=rounded(e, e + 1).rearrange("p (a c j) -> p a c j", a=PASSES, j=PACK),
                     in0=raw[e][:].rearrange("p (a j c) -> p a c j", a=PASSES, j=PACK),
                     scalar1=1.0,
                     scalar2=0.0,
                     op0=ALU.mult,
                     op1=ALU.add,
                 )
-                return
-            rounded[e] = rounded_tile(e)
-            own = rounded[e][:]
-            nc.scalar.copy(
-                out=own.rearrange("p (a c i j) -> p a c j i", a=PASSES, i=RUN, j=PACK),
-                in_=raw[e][:].rearrange("p (a j c i) -> p a c j i", a=PASSES, j=PACK, i=RUN),
-            )
+            else:
+                round_passes(rounded(e, e + 1), raw[e][:], PASSES)
 
         def quantise(lo, hi):
-            m = lo // 2
-            if lo % 2 == 0:
-                w_codes[m] = small.tile([P, 2 * W], U32, name="w_codes", align_bytes=64)
-                w_scales[m] = small.tile([P, 2 * W], U8, name="w_scales", align_bytes=64)
+            if lo == 0:
+                codes = keep.tile([P, W], U32, name="first_codes", tag="lone_codes", align_bytes=64)
+                scales = keep.tile([P, W], U8, name="first_scales", tag="lone_scales", align_bytes=64)
+            else:
+                codes = small.tile([P, 2 * W], U32, name="codes", align_bytes=64)
+                scales = small.tile([P, 2 * W], U8, name="scales", align_bytes=64)
             for e in range(lo, hi):
-                quantise_passes(e, 0, PASSES, rounded[e][:])
+                w_codes[e] = codes[:, (e - lo) * W : (e - lo + 1) * W]
+                w_scales[e] = scales[:, (e - lo) * W : (e - lo + 1) * W]
+            quantise_into(codes[:, 0 : (hi - lo) * W], scales[:, 0 : (hi - lo) * W], rounded(lo, hi))
 
         def gather_scales(lo, hi):
             nc.vector.tensor_copy(
@@ -160,11 +156,10 @@ def tile_moe_pkd_lin_relu2_kernel(
             for a in passes:
                 if a == 0:
                     sums[e] = psum.tile([P, C], F32, name="sums", tag="bank%d" % (e % 8))
-                first_word = (e % 2) * W + a * N
                 nc.tensor.matmul_mx(
                     out=sums[e][:],
-                    lhsT=w_codes[e // 2][:, first_word : first_word + N].bitcast(FP8X4),
-                    lhsT_scale=w_scales[e // 2][:, first_word : first_word + N],
+                    lhsT=w_codes[e][:, a * N : (a + 1) * N].bitcast(FP8X4),
+                    lhsT_scale=w_scales[e][:, a * N : (a + 1) * N],
                     rhs=slot_words[e, a].bitcast(FP8X4),
                     rhs_scale=slot_scales[4 * a : P, e * C : (e + 1) * C],
                     start=(a == 0),
@@ -190,43 +185,64 @@ def tile_moe_pkd_lin_relu2_kernel(
             )
         load_words(0)
         load_weights(0)
-        for a in range(1, PASSES):
-            load_words(a)
+        load_words(1)
+        load_words(2)
         load_weights(1)
+        load_weights(2)
+        load_words(3)
         nc.sync.dma_start(out=bias[:], in_=b)
-        for e in range(2, E):
+        for e in range(3, E):
             load_weights(e)
         nc.sync.dma_start(second_list[:], pos2)
 
         for lo, hi in WIDE:
             gather_scales(lo, hi)
-        gather_piece(PIECES[0])
+        for a in (0, 1):
+            head_words = keep.tile([P, HEAD * C], U32, name="head_words%d" % a, align_bytes=64)
+            gather_pass(head_words[:], a, 0, HEAD)
         every = range(PASSES)
-        for m in range(PAIRS - 1):
-            round_weights(2 * m)
-            if m >= LAG:
-                activate(2 * (m - LAG), 2 * (m - LAG + 1), raw[2 * m][:, 0 : 2 * C])
-            quantise(2 * m, 2 * m + 1)
-            gather_piece(PIECES[m + 1])
-            multiply(2 * m, every)
+        round_weights(0)
+        quantise(0, 1)
+        multiplied = []
+
+        def multiply_ready():
+            ready = [e for e in w_codes if e not in multiplied and (e, PASSES - 1) in slot_words]
+            for e in ready:
+                multiply(e, every)
+            multiplied.extend(ready)
+
+        for m in range(PAIRS - 2):
+            gather_piece(PIECES[m])
+            multiply_ready()
             round_weights(2 * m + 1)
-            quantise(2 * m + 1, 2 * m + 2)
-            multiply(2 * m + 1, every)
-        gather_piece(PIECES[PAIRS])
+            round_weights(2 * m + 2)
+            for i, pair in enumerate(BEHIND.get(2 * m + 2, ())):
+                activate(2 * pair, 2 * pair + 2, raw[2 * m + 2][:, 2 * i * C : 2 * (i + 1) * C])
+            quantise(2 * m + 1, 2 * m + 3)
+            multiply_ready()
+        gather_piece(PIECES[PAIRS - 2])
+        round_weights(E - 3)
+        activate(E - 8, E - 6, raw[E - 3][:, 0 : 2 * C])
+        quantise(E - 3, E - 2)
+        multiply(E - 3, every)
+        gather_piece(PIECES[PAIRS - 1])
         round_weights(E - 2)
         quantise(E - 2, E - 1)
         multiply(E - 2, every)
         front = keep.tile([P, 2 * W], BF16, name="front", tag="front", align_bytes=64)
-        rear = keep.tile([P, 2 * W], BF16, name="rear", align_bytes=64)
+        rear = rounded(E - 1, E)
         round_passes(front[:], raw[E - 1][:, 0 : 2 * W], 2)
         round_passes(rear[:, 0:W], raw[E - 1][:, 2 * W : 3 * W], 1)
         round_passes(rear[:, W : 2 * W], raw_end[:], 1)
-        quantise_passes(E - 1, 0, 2, front[:])
-        quantise_passes(E - 1, 2, 3, rear[:, 0:W])
+        last_codes = keep.tile([P, W], U32, name="last_codes", tag="lone_codes", align_bytes=64)
+        last_scales = keep.tile([P, W], U8, name="last_scales", tag="lone_scales", align_bytes=64)
+        w_codes[E - 1], w_scales[E - 1] = last_codes[:], last_scales[:]
+        quantise_into(last_codes[:, 0 : 2 * N], last_scales[:, 0 : 2 * N], front[:])
+        quantise_into(last_codes[:, 2 * N : 3 * N], last_scales[:, 2 * N : 3 * N], rear[:, 0:W])
         last_words = keep.tile([P, 2 * C], U32, name="last_words", tag="front", align_bytes=64)
         for a in (2, 3):
             gather_pass(last_words[:, (a - 2) * C : (a - 1) * C], a, E - 1, E)
-        quantise_passes(E - 1, 3, 4, rear[:, W : 2 * W])
+        quantise_into(last_codes[:, 3 * N : 4 * N], last_scales[:, 3 * N : 4 * N], rear[:, W : 2 * W])
         multiply(E - 1, every)
         activate(E - 6, E - 4, raw_end[:, 0 : 2 * C])
         activate(E - 4, E - 2, raw[E - 1][:, 0 : 2 * C])
@@ -282,13 +298,14 @@ def tile_moe_pkd_lin_relu2_kernel(
             nc.scalar.dma_start(out=out[:, lo:hi], in_=total[:, lo:hi])
 
         turned = wide_tile(E - 3, F32, "turned")
-        for i, (lo, hi) in enumerate(TURNED):
+        for lo, hi in TURNED:
             fetch(first, first_list, 0, lo, hi)
             fetch(second, second_list, 1, lo, hi)
-            sum_turned(i, lo, hi)
-            if i > 0:
-                turn_back(i - 1, *TURNED[i - 1])
-        turn_back(len(TURNED) - 1, *TURNED[-1])
+            for at in range(lo, hi, BLOCK):
+                sum_turned(at // BLOCK, at, at + BLOCK)
+                if at > 0:
+                    turn_back(at // BLOCK - 1, at - BLOCK, at)
+        turn_back(TURNED[-1][1] // BLOCK - 1, TURNED[-1][1] - BLOCK, TURNED[-1][1])
         for i, (lo, hi) in enumerate(ADDED):
             fetch(first, first_list, 0, lo, hi)
             fetch(second, second_list, 1, lo, hi)

@@ -25,17 +25,17 @@ PAIRS = E // 2
 W = PASSES * N
 HEAD = 6
 PIECES = [
-    ((0, 6), (2,), 0),
-    ((0, 6), (3,), 2),
-    ((6, 10), (0, 1), 4),
-    ((6, 10), (2, 3), 6),
-    ((10, 14), (0, 1), 8),
-    ((10, 14), (2, 3), 10),
-    ((14, 16), (0, 1), 12),
-    ((14, 15), (2, 3), 13),
+    (0, [(0, 6, 2)]),
+    (2, [(0, 6, 3)]),
+    (4, [(6, 10, 0), (6, 10, 1)]),
+    (6, [(6, 10, 2), (6, 10, 3)]),
+    (8, [(10, 14, 0), (10, 14, 1)]),
+    (10, [(10, 14, 2), (10, 14, 3)]),
+    (12, [(14, 16, 0), (14, 16, 1)]),
+    (13, [(14, 15, 2), (14, 15, 3)]),
 ]
-TURNED = [(0, 256), (256, 768), (768, 1280)]
-ADDED = [(1280, 1792), (1792, 1920), (1920, 2048)]
+TURNED = [(0, 256), (256, 768), (768, 1280), (1280, 1536)]
+ADDED = [(1536, 1792), (1792, 1920), (1920, 2048)]
 BLOCK = 256
 RUN = 4
 BEHIND = {6: (0,), 8: (1, 2), 10: (3,)}
@@ -146,15 +146,16 @@ def tile_moe_pkd_lin_relu2_kernel(
                 slot_words[e, a] = dst[:, (e - lo) * C : (e - lo + 1) * C]
 
         def gather_piece(piece):
-            (lo, hi), passes, place = piece
+            place, parts = piece
             words = wide_tile(place, U32, "slot_words%d" % place)
-            width = (hi - lo) * C
-            for i, a in enumerate(passes):
-                gather_pass(words[:, i * width : (i + 1) * width], a, lo, hi)
+            at = 0
+            for lo, hi, a in parts:
+                gather_pass(words[:, at : at + (hi - lo) * C], a, lo, hi)
+                at = at + (hi - lo) * C
 
         def multiply(e, passes):
             for a in passes:
-                if a == 0:
+                if a == passes[0]:
                     sums[e] = psum.tile([P, C], F32, name="sums", tag="bank%d" % (e % 8))
                 nc.tensor.matmul_mx(
                     out=sums[e][:],
@@ -162,8 +163,8 @@ def tile_moe_pkd_lin_relu2_kernel(
                     lhsT_scale=w_scales[e][:, a * N : (a + 1) * N],
                     rhs=slot_words[e, a].bitcast(FP8X4),
                     rhs_scale=slot_scales[4 * a : P, e * C : (e + 1) * C],
-                    start=(a == 0),
-                    stop=(a == PASSES - 1),
+                    start=(a == passes[0]),
+                    stop=(a == passes[-1]),
                 )
 
         def activate(lo, hi, scratch):
@@ -183,8 +184,8 @@ def tile_moe_pkd_lin_relu2_kernel(
                 out=token_scales[32 * q : 32 * q + 16, :].bitcast(I32),
                 in_=x_scales[:, 4 * q : 4 * q + 4, :].bitcast(I32),
             )
-        load_words(0)
         load_weights(0)
+        load_words(0)
         load_words(1)
         load_words(2)
         load_weights(1)
@@ -208,7 +209,7 @@ def tile_moe_pkd_lin_relu2_kernel(
         def multiply_ready():
             ready = [e for e in w_codes if e not in multiplied and (e, PASSES - 1) in slot_words]
             for e in ready:
-                multiply(e, every)
+                multiply(e, list(reversed(every)))
             multiplied.extend(ready)
 
         for m in range(PAIRS - 2):

@@ -29,17 +29,18 @@ PIECES = [
     (2, [(0, 6, 3)]),
     (4, [(6, 10, 0), (6, 10, 1)]),
     (6, [(6, 10, 2), (6, 10, 3)]),
-    (8, [(10, 14, 0), (10, 14, 1)]),
-    (10, [(10, 14, 2), (10, 14, 3)]),
-    (12, [(14, 16, 0), (14, 16, 1)]),
-    (13, [(14, 15, 2), (14, 15, 3)]),
+    (8, [(10, 13, 0), (10, 13, 1), (13, 15, 0)]),
+    (10, [(10, 13, 2), (10, 13, 3)]),
+    (12, [(13, 15, 1), (13, 15, 2), (13, 15, 3)]),
+    (13, [(15, 16, 0), (15, 16, 1)]),
 ]
-TURNED = [(0, 256), (256, 768), (768, 1280), (1280, 1536)]
-ADDED = [(1536, 1792), (1792, 1920), (1920, 2048)]
+TURNED = [(0, 128), (128, 384), (384, 896), (896, 1152), (1152, 1408)]
+ADDED = [(1408, 1664), (1664, 1920), (1920, 2048)]
+GATED = [(0, 384), (384, 896), (896, 1408), (1408, 2048)]
 BLOCK = 256
 RUN = 4
 BEHIND = {6: (0,), 8: (1, 2), 10: (3,)}
-ON_GPSIMD = (1, 3, 5, 7, 9, 11)
+ON_GPSIMD = (1, 3, 5, 7, 9, 11, 13)
 
 
 def tile_moe_pkd_lin_relu2_kernel(
@@ -71,6 +72,7 @@ def tile_moe_pkd_lin_relu2_kernel(
         w_scales = {}
         slot_words = {}
         sums = {}
+        held = {}
 
         def wide_tile(place, dtype, name):
             return wide.tile([P, T], dtype, name=name, tag="wide%d" % place, align_bytes=64)
@@ -78,7 +80,7 @@ def tile_moe_pkd_lin_relu2_kernel(
         strip = half.tile([P, (PAIRS - 1) * W * PACK], BF16, name="strip", align_bytes=64)
 
         def rounded(lo, hi):
-            room = lo // 2 if lo < E - 3 else lo - (E - 3)
+            room = lo // 2 if lo < E - 2 else lo - (E - 2)
             return strip[:, room * W * PACK : (room + hi - lo) * W * PACK]
 
         def load_words(a):
@@ -123,15 +125,17 @@ def tile_moe_pkd_lin_relu2_kernel(
 
         def quantise(lo, hi):
             if lo == 0:
-                codes = keep.tile([P, W], U32, name="first_codes", tag="lone_codes", align_bytes=64)
-                scales = keep.tile([P, W], U8, name="first_scales", tag="lone_scales", align_bytes=64)
-            else:
-                codes = small.tile([P, 2 * W], U32, name="codes", align_bytes=64)
-                scales = small.tile([P, 2 * W], U8, name="scales", align_bytes=64)
+                held["codes"] = keep.tile([P, W], U32, name="first_codes", tag="lone_codes", align_bytes=64)
+                held["scales"] = keep.tile([P, W], U8, name="first_scales", tag="lone_scales", align_bytes=64)
+            elif lo % 2 == 1:
+                held["codes"] = small.tile([P, 2 * W], U32, name="codes", align_bytes=64)
+                held["scales"] = small.tile([P, 2 * W], U8, name="scales", align_bytes=64)
+            at = W if lo > 0 and lo % 2 == 0 else 0
             for e in range(lo, hi):
-                w_codes[e] = codes[:, (e - lo) * W : (e - lo + 1) * W]
-                w_scales[e] = scales[:, (e - lo) * W : (e - lo + 1) * W]
-            quantise_into(codes[:, 0 : (hi - lo) * W], scales[:, 0 : (hi - lo) * W], rounded(lo, hi))
+                w_codes[e] = held["codes"][:, at + (e - lo) * W : at + (e - lo + 1) * W]
+                w_scales[e] = held["scales"][:, at + (e - lo) * W : at + (e - lo + 1) * W]
+            columns = slice(at, at + (hi - lo) * W)
+            quantise_into(held["codes"][:, columns], held["scales"][:, columns], rounded(lo, hi))
 
         def gather_scales(lo, hi):
             nc.vector.tensor_copy(
@@ -209,10 +213,10 @@ def tile_moe_pkd_lin_relu2_kernel(
         def multiply_ready():
             ready = [e for e in w_codes if e not in multiplied and (e, PASSES - 1) in slot_words]
             for e in ready:
-                multiply(e, list(reversed(every)))
+                multiply(e, every)
             multiplied.extend(ready)
 
-        for m in range(PAIRS - 2):
+        for m in range(PAIRS - 3):
             gather_piece(PIECES[m])
             multiply_ready()
             round_weights(2 * m + 1)
@@ -221,15 +225,18 @@ def tile_moe_pkd_lin_relu2_kernel(
                 activate(2 * pair, 2 * pair + 2, raw[2 * m + 2][:, 2 * i * C : 2 * (i + 1) * C])
             quantise(2 * m + 1, 2 * m + 3)
             multiply_ready()
-        gather_piece(PIECES[PAIRS - 2])
-        round_weights(E - 3)
-        activate(E - 8, E - 6, raw[E - 3][:, 0 : 2 * C])
-        quantise(E - 3, E - 2)
-        multiply(E - 3, every)
-        gather_piece(PIECES[PAIRS - 1])
-        round_weights(E - 2)
-        quantise(E - 2, E - 1)
-        multiply(E - 2, every)
+        for m in (PAIRS - 3, PAIRS - 2):
+            gather_piece(PIECES[m])
+            multiply_ready()
+            for e in (2 * m + 1, 2 * m + 2):
+                round_weights(e)
+                quantise(e, e + 1)
+                multiply_ready()
+                if e == E - 3:
+                    gather_piece(PIECES[PAIRS - 1])
+            if m == PAIRS - 3:
+                activate(E - 8, E - 6, raw[E - 5][:, 0 : 2 * C])
+                activate(E - 6, E - 4, raw[E - 5][:, 2 * C : 4 * C])
         front = keep.tile([P, 2 * W], BF16, name="front", tag="front", align_bytes=64)
         rear = rounded(E - 1, E)
         round_passes(front[:], raw[E - 1][:, 0 : 2 * W], 2)
@@ -245,10 +252,9 @@ def tile_moe_pkd_lin_relu2_kernel(
             gather_pass(last_words[:, (a - 2) * C : (a - 1) * C], a, E - 1, E)
         quantise_into(last_codes[:, 3 * N : 4 * N], last_scales[:, 3 * N : 4 * N], rear[:, W : 2 * W])
         multiply(E - 1, every)
-        activate(E - 6, E - 4, raw_end[:, 0 : 2 * C])
-        activate(E - 4, E - 2, raw[E - 1][:, 0 : 2 * C])
+        activate(E - 4, E - 2, raw_end[:, 0 : 2 * C])
         activate(E - 2, E - 1, raw[E - 1][:, 2 * C : 3 * C])
-        last = raw[E - 5]
+        last = raw[E - 5][:, 4 * C : 5 * C]
         halves = [slice(h * N, (h + 1) * N) for h in range(2)]
         for h in halves:
             nc.vector.tensor_scalar(
@@ -258,17 +264,19 @@ def tile_moe_pkd_lin_relu2_kernel(
             nc.vector.tensor_tensor(out=y[:, (E - 1) * C : E * C][:, h], in0=last[:, h], in1=last[:, h], op=ALU.mult)
 
         gates = []
-        for r in range(2):
-            gate_r = wide_tile(1 + 2 * r, F32, "gate%d" % r)
-            nc.sync.dma_start(out=gate_r[:], in_=gate[r])
-            gates.append(gate_r)
+        for place, (lo, hi) in enumerate(GATED):
+            both = wide_tile(place, F32, "gates%d" % place)[:, 0 : 2 * (hi - lo)].rearrange("p (r t) -> p r t", r=2)
+            nc.sync.dma_start(out=both, in_=gate[:, :, lo:hi].rearrange("r p t -> p r t"))
+            gates.append(both)
         first = wide_tile(5, F32, "first")
         second = wide_tile(7, F32, "second")
         total = wide_tile(9, F32, "total")
 
         def fetch(dst, lst, r, lo, hi):
+            i = max(j for j, (start, end) in enumerate(GATED) if start <= lo)
+            own = gates[i][:, r, lo - GATED[i][0] : hi - GATED[i][0]]
             nc.vector.tensor_tensor(
-                out=dst[:, lo:hi], in0=y[:].indirect(lst[:, lo // 16 : hi // 16]), in1=gates[r][:, lo:hi], op=ALU.mult
+                out=dst[:, lo:hi], in0=y[:].indirect(lst[:, lo // 16 : hi // 16]), in1=own, op=ALU.mult
             )
 
         def combine(lo, hi):
@@ -299,14 +307,16 @@ def tile_moe_pkd_lin_relu2_kernel(
             nc.scalar.dma_start(out=out[:, lo:hi], in_=total[:, lo:hi])
 
         turned = wide_tile(E - 3, F32, "turned")
+        blocks = []
         for lo, hi in TURNED:
             fetch(first, first_list, 0, lo, hi)
             fetch(second, second_list, 1, lo, hi)
             for at in range(lo, hi, BLOCK):
-                sum_turned(at // BLOCK, at, at + BLOCK)
-                if at > 0:
-                    turn_back(at // BLOCK - 1, at - BLOCK, at)
-        turn_back(TURNED[-1][1] // BLOCK - 1, TURNED[-1][1] - BLOCK, TURNED[-1][1])
+                blocks.append((at, min(at + BLOCK, hi)))
+                sum_turned(len(blocks) - 1, *blocks[-1])
+                if len(blocks) > 1:
+                    turn_back(len(blocks) - 2, *blocks[-2])
+        turn_back(len(blocks) - 1, *blocks[-1])
         for i, (lo, hi) in enumerate(ADDED):
             fetch(first, first_list, 0, lo, hi)
             fetch(second, second_list, 1, lo, hi)

@@ -32,11 +32,11 @@ PIECES = [
     (8, [(10, 13, 0), (10, 13, 1), (13, 15, 0)]),
     (10, [(10, 13, 2), (10, 13, 3)]),
     (12, [(13, 15, 1), (13, 15, 2), (13, 15, 3)]),
-    (13, [(15, 16, 0), (15, 16, 1)]),
+    (1, [(15, 16, 0), (15, 16, 1)]),
 ]
 TURNED = [(0, 128), (128, 384), (384, 896), (896, 1152), (1152, 1408)]
 ADDED = [(1408, 1664), (1664, 1920), (1920, 2048)]
-GATED = [(0, 384), (384, 896), (896, 1408), (1408, 2048)]
+LATE = {13: 1, 14: 3, 15: 5}
 BLOCK = 256
 RUN = 4
 BEHIND = {6: (0,), 8: (1, 2), 10: (3,)}
@@ -66,7 +66,7 @@ def tile_moe_pkd_lin_relu2_kernel(
         nc.gpsimd.memset(token_scales[:].bitcast(I32), 0)
         make_identity(nc, identity[:])
 
-        raw_end = keep.tile([P, W], F32, name="raw_end")
+        gates = [keep.tile([P, T], F32, name="gate%d" % r) for r in range(2)]
         raw = {}
         w_codes = {}
         w_scales = {}
@@ -93,13 +93,12 @@ def tile_moe_pkd_lin_relu2_kernel(
             )
 
         def load_weights(e):
+            raw[e] = wide_tile(LATE.get(e, e), F32, "raw%d" % e)
             if e < E - 1:
-                raw[e] = wide_tile(e, F32, "raw%d" % e)
                 load_passes(raw[e], e, 0, PASSES)
             else:
-                raw[e] = keep.tile([P, (PASSES - 1) * W], F32, name="raw_last")
                 load_passes(raw[e], e, 0, PASSES - 1)
-                load_passes(raw_end, e, PASSES - 1, PASSES)
+                load_passes(raw[e][:, (PASSES - 1) * W :], e, PASSES - 1, PASSES)
 
         def round_passes(own, src, count):
             nc.scalar.copy(
@@ -196,8 +195,10 @@ def tile_moe_pkd_lin_relu2_kernel(
         load_weights(2)
         load_words(3)
         nc.sync.dma_start(out=bias[:], in_=b)
-        for e in range(3, E):
+        for e in range(3, E - 3):
             load_weights(e)
+        for r in range(2):
+            nc.sync.dma_start(out=gates[r][:], in_=gate[r])
         nc.sync.dma_start(second_list[:], pos2)
 
         for lo, hi in WIDE:
@@ -221,6 +222,9 @@ def tile_moe_pkd_lin_relu2_kernel(
             multiply_ready()
             round_weights(2 * m + 1)
             round_weights(2 * m + 2)
+            for e in LATE:
+                if LATE[e] == 2 * m + 1:
+                    load_weights(e)
             for i, pair in enumerate(BEHIND.get(2 * m + 2, ())):
                 activate(2 * pair, 2 * pair + 2, raw[2 * m + 2][:, 2 * i * C : 2 * (i + 1) * C])
             quantise(2 * m + 1, 2 * m + 3)
@@ -241,7 +245,7 @@ def tile_moe_pkd_lin_relu2_kernel(
         rear = rounded(E - 1, E)
         round_passes(front[:], raw[E - 1][:, 0 : 2 * W], 2)
         round_passes(rear[:, 0:W], raw[E - 1][:, 2 * W : 3 * W], 1)
-        round_passes(rear[:, W : 2 * W], raw_end[:], 1)
+        round_passes(rear[:, W : 2 * W], raw[E - 1][:, 3 * W : 4 * W], 1)
         last_codes = keep.tile([P, W], U32, name="last_codes", tag="lone_codes", align_bytes=64)
         last_scales = keep.tile([P, W], U8, name="last_scales", tag="lone_scales", align_bytes=64)
         w_codes[E - 1], w_scales[E - 1] = last_codes[:], last_scales[:]
@@ -252,7 +256,7 @@ def tile_moe_pkd_lin_relu2_kernel(
             gather_pass(last_words[:, (a - 2) * C : (a - 1) * C], a, E - 1, E)
         quantise_into(last_codes[:, 3 * N : 4 * N], last_scales[:, 3 * N : 4 * N], rear[:, W : 2 * W])
         multiply(E - 1, every)
-        activate(E - 4, E - 2, raw_end[:, 0 : 2 * C])
+        activate(E - 4, E - 2, raw[E - 1][:, 3 * W : 4 * W])
         activate(E - 2, E - 1, raw[E - 1][:, 2 * C : 3 * C])
         last = raw[E - 5][:, 4 * C : 5 * C]
         halves = [slice(h * N, (h + 1) * N) for h in range(2)]
@@ -263,20 +267,13 @@ def tile_moe_pkd_lin_relu2_kernel(
         for h in halves:
             nc.vector.tensor_tensor(out=y[:, (E - 1) * C : E * C][:, h], in0=last[:, h], in1=last[:, h], op=ALU.mult)
 
-        gates = []
-        for place, (lo, hi) in enumerate(GATED):
-            both = wide_tile(place, F32, "gates%d" % place)[:, 0 : 2 * (hi - lo)].rearrange("p (r t) -> p r t", r=2)
-            nc.sync.dma_start(out=both, in_=gate[:, :, lo:hi].rearrange("r p t -> p r t"))
-            gates.append(both)
-        first = wide_tile(5, F32, "first")
+        first = wide_tile(0, F32, "first")
         second = wide_tile(7, F32, "second")
         total = wide_tile(9, F32, "total")
 
         def fetch(dst, lst, r, lo, hi):
-            i = max(j for j, (start, end) in enumerate(GATED) if start <= lo)
-            own = gates[i][:, r, lo - GATED[i][0] : hi - GATED[i][0]]
             nc.vector.tensor_tensor(
-                out=dst[:, lo:hi], in0=y[:].indirect(lst[:, lo // 16 : hi // 16]), in1=own, op=ALU.mult
+                out=dst[:, lo:hi], in0=y[:].indirect(lst[:, lo // 16 : hi // 16]), in1=gates[r][:, lo:hi], op=ALU.mult
             )
 
         def combine(lo, hi):
@@ -306,7 +303,7 @@ def tile_moe_pkd_lin_relu2_kernel(
             nc.scalar.copy(out=total[:, lo:hi], in_=back[:])
             nc.scalar.dma_start(out=out[:, lo:hi], in_=total[:, lo:hi])
 
-        turned = wide_tile(E - 3, F32, "turned")
+        turned = wide_tile(1, F32, "turned")
         blocks = []
         for lo, hi in TURNED:
             fetch(first, first_list, 0, lo, hi)

@@ -21,26 +21,17 @@ ACT = mybir.ActivationFunctionType
 ALU = mybir.AluOpType
 
 WIDE = [(0, 1536), (1536, 3072), (3072, 4096)]
-PAIRS = E // 2
 W = PASSES * N
-HEAD = 6
-PIECES = [
-    (0, [(0, 6, 2)]),
-    (2, [(0, 6, 3)]),
-    (4, [(6, 10, 0), (6, 10, 1)]),
-    (6, [(6, 10, 2), (6, 10, 3)]),
-    (8, [(10, 13, 0), (10, 13, 1), (13, 15, 0)]),
-    (10, [(10, 13, 2), (10, 13, 3)]),
-    (12, [(13, 15, 1), (13, 15, 2), (13, 15, 3)]),
-    (1, [(15, 16, 0), (15, 16, 1)]),
-]
+PLACE = T * 4
+PLACES = 12
+HEAD = 5
+GROUP = 3
+ROOMS = 8
 TURNED = [(0, 128), (128, 384), (384, 896), (896, 1152), (1152, 1408)]
 ADDED = [(1408, 1664), (1664, 1920), (1920, 2048)]
-LATE = {13: 1, 14: 3, 15: 5}
+GATED = [(0, 896), (896, 1408), (1408, 2048)]
 BLOCK = 256
 RUN = 4
-BEHIND = {6: (0,), 8: (1, 2), 10: (3,)}
-ON_GPSIMD = (1, 3, 5, 7, 9, 11, 13)
 
 
 def tile_moe_pkd_lin_relu2_kernel(
@@ -50,7 +41,6 @@ def tile_moe_pkd_lin_relu2_kernel(
     with ExitStack() as ctx:
         keep = ctx.enter_context(tc.tile_pool(name="keep", bufs=1))
         wide = ctx.enter_context(tc.tile_pool(name="wide", bufs=1))
-        half = ctx.enter_context(tc.tile_pool(name="half", bufs=1))
         small = ctx.enter_context(tc.tile_pool(name="small", bufs=2))
         psum = ctx.enter_context(tc.psum_pool(name="psum", bufs=1))
 
@@ -66,111 +56,101 @@ def tile_moe_pkd_lin_relu2_kernel(
         nc.gpsimd.memset(token_scales[:].bitcast(I32), 0)
         make_identity(nc, identity[:])
 
-        gates = [keep.tile([P, T], F32, name="gate%d" % r) for r in range(2)]
         raw = {}
         w_codes = {}
         w_scales = {}
         slot_words = {}
         sums = {}
-        held = {}
 
-        def wide_tile(place, dtype, name):
-            return wide.tile([P, T], dtype, name=name, tag="wide%d" % place, align_bytes=64)
+        def placed(name, columns, dtype, at):
+            return wide.tile([P, columns], dtype, name=name, offset=at, align_bytes=64)
 
-        strip = half.tile([P, (PAIRS - 1) * W * PACK], BF16, name="strip", align_bytes=64)
+        def place_of(e):
+            return PLACE * (e if e < PLACES else 2 * (e - PLACES) + 1)
 
-        def rounded(lo, hi):
-            room = lo // 2 if lo < E - 2 else lo - (E - 2)
-            return strip[:, room * W * PACK : (room + hi - lo) * W * PACK]
+        strip_at = 0
+        strip = placed("strip", ROOMS * W * PACK, BF16, strip_at)
+        places_at = ROOMS * W * PACK * 2
+
+        def rounded(e, count=1):
+            room = e // 2 if e < E - 1 else (E - 3) // 2 - 1
+            return strip[:, room * W * PACK : (room + count) * W * PACK]
 
         def load_words(a):
             nc.sync.dma_start(out=token_words[a][:], in_=x_words[a].rearrange("p t r -> p (t r)").bitcast(I32))
 
-        def load_passes(dst, e, a0, a1):
-            nc.sync.dma_start(
-                out=dst[:, 0 : (a1 - a0) * W].rearrange("p (a m) -> p a m", m=W),
-                in_=w[e].rearrange("(a p j) n -> p a (j n)", a=PASSES, j=PACK)[:, a0:a1, :],
-            )
-
         def load_weights(e):
-            raw[e] = wide_tile(LATE.get(e, e), F32, "raw%d" % e)
-            if e < E - 1:
-                load_passes(raw[e], e, 0, PASSES)
-            else:
-                load_passes(raw[e], e, 0, PASSES - 1)
-                load_passes(raw[e][:, (PASSES - 1) * W :], e, PASSES - 1, PASSES)
-
-        def round_passes(own, src, count):
-            nc.scalar.copy(
-                out=own.rearrange("p (a c i j) -> p a c j i", a=count, i=RUN, j=PACK),
-                in_=src.rearrange("p (a j c i) -> p a c j i", a=count, j=PACK, i=RUN),
+            raw[e] = placed("raw%d" % e, T, F32, places_at + place_of(e))
+            nc.sync.dma_start(
+                out=raw[e][:].rearrange("p (a m) -> p a m", m=W),
+                in_=w[e].rearrange("(a p j) n -> p a (j n)", a=PASSES, j=PACK),
             )
 
-        def quantise_into(codes, scales, src):
-            nc.vector.quantize_mx(out=codes.bitcast(FP8X4), scales=scales, in_=src)
+        def round_on_scalar(e):
+            nc.scalar.copy(
+                out=rounded(e).rearrange("p (a c i j) -> p a c j i", a=PASSES, i=RUN, j=PACK),
+                in_=raw[e][:].rearrange("p (a j c i) -> p a c j i", a=PASSES, j=PACK, i=RUN),
+            )
 
-        def round_weights(e):
-            if e in ON_GPSIMD:
-                nc.gpsimd.tensor_scalar(
-                    out=rounded(e, e + 1).rearrange("p (a c j) -> p a c j", a=PASSES, j=PACK),
-                    in0=raw[e][:].rearrange("p (a j c) -> p a c j", a=PASSES, j=PACK),
-                    scalar1=1.0,
-                    scalar2=0.0,
-                    op0=ALU.mult,
-                    op1=ALU.add,
-                )
+        def round_on_gpsimd(e):
+            nc.gpsimd.tensor_scalar(
+                out=rounded(e).rearrange("p (a c j) -> p a c j", a=PASSES, j=PACK),
+                in0=raw[e][:].rearrange("p (a j c) -> p a c j", a=PASSES, j=PACK),
+                scalar1=1.0,
+                scalar2=0.0,
+                op0=ALU.mult,
+                op1=ALU.add,
+            )
+
+        def quantise(*experts):
+            if len(experts) == 1:
+                codes = keep.tile([P, W], U32, name="lone_codes", align_bytes=64)
+                scales = keep.tile([P, W], U8, name="lone_scales", align_bytes=64)
             else:
-                round_passes(rounded(e, e + 1), raw[e][:], PASSES)
-
-        def quantise(lo, hi):
-            if lo == 0:
-                held["codes"] = keep.tile([P, W], U32, name="first_codes", tag="lone_codes", align_bytes=64)
-                held["scales"] = keep.tile([P, W], U8, name="first_scales", tag="lone_scales", align_bytes=64)
-            elif lo % 2 == 1:
-                held["codes"] = small.tile([P, 2 * W], U32, name="codes", align_bytes=64)
-                held["scales"] = small.tile([P, 2 * W], U8, name="scales", align_bytes=64)
-            at = W if lo > 0 and lo % 2 == 0 else 0
-            for e in range(lo, hi):
-                w_codes[e] = held["codes"][:, at + (e - lo) * W : at + (e - lo + 1) * W]
-                w_scales[e] = held["scales"][:, at + (e - lo) * W : at + (e - lo + 1) * W]
-            columns = slice(at, at + (hi - lo) * W)
-            quantise_into(held["codes"][:, columns], held["scales"][:, columns], rounded(lo, hi))
+                codes = small.tile([P, 2 * W], U32, name="codes", align_bytes=64)
+                scales = small.tile([P, 2 * W], U8, name="scales", align_bytes=64)
+            for i, e in enumerate(experts):
+                w_codes[e] = codes[:, i * W : (i + 1) * W]
+                w_scales[e] = scales[:, i * W : (i + 1) * W]
+            nc.vector.quantize_mx(
+                out=codes[:].bitcast(FP8X4), scales=scales[:], in_=rounded(experts[0], len(experts))
+            )
 
         def gather_scales(lo, hi):
             nc.vector.tensor_copy(
                 out=slot_scales[:, lo:hi], in_=token_scales[:].indirect(slot_list[:, lo // 16 : hi // 16])
             )
 
-        def gather_pass(dst, a, lo, hi):
-            nc.vector.tensor_copy(
-                out=dst, in_=token_words[a][:].bitcast(U32).indirect(slot_list[:, lo * C // 16 : hi * C // 16])
-            )
-            for e in range(lo, hi):
-                slot_words[e, a] = dst[:, (e - lo) * C : (e - lo + 1) * C]
-
-        def gather_piece(piece):
-            place, parts = piece
-            words = wide_tile(place, U32, "slot_words%d" % place)
-            at = 0
-            for lo, hi, a in parts:
-                gather_pass(words[:, at : at + (hi - lo) * C], a, lo, hi)
-                at = at + (hi - lo) * C
-
-        def multiply(e, passes):
-            for a in passes:
-                if a == passes[0]:
-                    sums[e] = psum.tile([P, C], F32, name="sums", tag="bank%d" % (e % 8))
-                nc.tensor.matmul_mx(
-                    out=sums[e][:],
-                    lhsT=w_codes[e][:, a * N : (a + 1) * N].bitcast(FP8X4),
-                    lhsT_scale=w_scales[e][:, a * N : (a + 1) * N],
-                    rhs=slot_words[e, a].bitcast(FP8X4),
-                    rhs_scale=slot_scales[4 * a : P, e * C : (e + 1) * C],
-                    start=(a == passes[0]),
-                    stop=(a == passes[-1]),
+        def gather_words(words, lo, hi, passes):
+            width = (hi - lo) * C
+            for i, a in enumerate(passes):
+                dst = words[:, i * width : (i + 1) * width]
+                nc.vector.tensor_copy(
+                    out=dst, in_=token_words[a][:].bitcast(U32).indirect(slot_list[:, lo * C // 16 : hi * C // 16])
                 )
+                for e in range(lo, hi):
+                    slot_words[e, a] = dst[:, (e - lo) * C : (e - lo + 1) * C]
 
-        def activate(lo, hi, scratch):
+        multiplied = []
+
+        def multiply_ready():
+            ready = [e for e in w_codes if e not in multiplied and (e, PASSES - 1) in slot_words]
+            for e in ready:
+                sums[e] = psum.tile([P, C], F32, name="sums", tag="bank%d" % (e % 8))
+                for a in range(PASSES):
+                    nc.tensor.matmul_mx(
+                        out=sums[e][:],
+                        lhsT=w_codes[e][:, a * N : (a + 1) * N].bitcast(FP8X4),
+                        lhsT_scale=w_scales[e][:, a * N : (a + 1) * N],
+                        rhs=slot_words[e, a].bitcast(FP8X4),
+                        rhs_scale=slot_scales[4 * a : P, e * C : (e + 1) * C],
+                        start=(a == 0),
+                        stop=(a == PASSES - 1),
+                    )
+            multiplied.extend(ready)
+
+        def activate(lo, hi, at):
+            scratch = placed("positive%d" % lo, (hi - lo) * C, F32, at)
             for e in range(lo, hi):
                 nc.scalar.activation(
                     out=scratch[:, (e - lo) * C : (e - lo + 1) * C],
@@ -178,7 +158,7 @@ def tile_moe_pkd_lin_relu2_kernel(
                     func=ACT.Relu,
                     bias=bias[:, e : e + 1],
                 )
-            nc.scalar.activation(out=y[:, lo * C : hi * C], in_=scratch[:, 0 : (hi - lo) * C], func=ACT.Square)
+            nc.scalar.activation(out=y[:, lo * C : hi * C], in_=scratch[:], func=ACT.Square)
 
         nc.sync.dma_start(slot_list[:], offs)
         nc.sync.dma_start(first_list[:], pos1)
@@ -188,92 +168,94 @@ def tile_moe_pkd_lin_relu2_kernel(
                 in_=x_scales[:, 4 * q : 4 * q + 4, :].bitcast(I32),
             )
         load_weights(0)
-        load_words(0)
-        load_words(1)
-        load_words(2)
+        for a in range(PASSES):
+            load_words(a)
         load_weights(1)
         load_weights(2)
-        load_words(3)
         nc.sync.dma_start(out=bias[:], in_=b)
-        for e in range(3, E - 3):
+        for e in range(3, PLACES):
             load_weights(e)
-        for r in range(2):
-            nc.sync.dma_start(out=gates[r][:], in_=gate[r])
         nc.sync.dma_start(second_list[:], pos2)
 
         for lo, hi in WIDE:
             gather_scales(lo, hi)
-        for a in (0, 1):
+        for a in range(PASSES):
             head_words = keep.tile([P, HEAD * C], U32, name="head_words%d" % a, align_bytes=64)
-            gather_pass(head_words[:], a, 0, HEAD)
-        every = range(PASSES)
-        round_weights(0)
-        quantise(0, 1)
-        multiplied = []
+            gather_words(head_words, 0, HEAD, [a])
+        round_on_scalar(0)
+        quantise(0)
+        multiply_ready()
 
-        def multiply_ready():
-            ready = [e for e in w_codes if e not in multiplied and (e, PASSES - 1) in slot_words]
-            for e in ready:
-                multiply(e, every)
-            multiplied.extend(ready)
-
-        for m in range(PAIRS - 3):
-            gather_piece(PIECES[m])
+        gates = []
+        quarter = PLACE // 4
+        for odd in range(1, E - 1, 2):
+            even = odd + 1
+            round_on_gpsimd(odd)
+            round_on_scalar(even)
+            if PLACES + odd // 2 < E:
+                load_weights(PLACES + odd // 2)
+            if odd == 11:
+                for i, (lo, hi) in enumerate(GATED):
+                    at = places_at + (9 * PLACE if i == 0 else 11 * PLACE + (lo - GATED[1][0]) * 8)
+                    both = placed("gates%d" % i, 2 * (hi - lo), F32, at)[:].rearrange("p (r t) -> p r t", r=2)
+                    nc.sync.dma_start(out=both, in_=gate[:, :, lo:hi].rearrange("r p t -> p r t"))
+                    gates.append(both)
+            at = places_at + place_of(even)
+            if 4 <= even <= 12:
+                activate(even - 4, even - 2, at + 3 * quarter)
+            if even < E - 2:
+                quantise(odd, even)
+            else:
+                quantise(even)
             multiply_ready()
-            round_weights(2 * m + 1)
-            round_weights(2 * m + 2)
-            for e in LATE:
-                if LATE[e] == 2 * m + 1:
-                    load_weights(e)
-            for i, pair in enumerate(BEHIND.get(2 * m + 2, ())):
-                activate(2 * pair, 2 * pair + 2, raw[2 * m + 2][:, 2 * i * C : 2 * (i + 1) * C])
-            quantise(2 * m + 1, 2 * m + 3)
+            run = odd // 2
+            if even < E - 2:
+                lo = HEAD + GROUP * (run // 2)
+                words = placed("words%d" % run, 2 * GROUP * C, U32, at)
+                gather_words(words, lo, lo + GROUP, [2 * (run % 2), 2 * (run % 2) + 1])
+            else:
+                gather_words(placed("words%d" % run, 2 * C, U32, at), even, even + 1, [0, 1])
             multiply_ready()
-        for m in (PAIRS - 3, PAIRS - 2):
-            gather_piece(PIECES[m])
-            multiply_ready()
-            for e in (2 * m + 1, 2 * m + 2):
-                round_weights(e)
-                quantise(e, e + 1)
-                multiply_ready()
-                if e == E - 3:
-                    gather_piece(PIECES[PAIRS - 1])
-            if m == PAIRS - 3:
-                activate(E - 8, E - 6, raw[E - 5][:, 0 : 2 * C])
-                activate(E - 6, E - 4, raw[E - 5][:, 2 * C : 4 * C])
-        front = keep.tile([P, 2 * W], BF16, name="front", tag="front", align_bytes=64)
-        rear = rounded(E - 1, E)
-        round_passes(front[:], raw[E - 1][:, 0 : 2 * W], 2)
-        round_passes(rear[:, 0:W], raw[E - 1][:, 2 * W : 3 * W], 1)
-        round_passes(rear[:, W : 2 * W], raw[E - 1][:, 3 * W : 4 * W], 1)
-        last_codes = keep.tile([P, W], U32, name="last_codes", tag="lone_codes", align_bytes=64)
-        last_scales = keep.tile([P, W], U8, name="last_scales", tag="lone_scales", align_bytes=64)
-        w_codes[E - 1], w_scales[E - 1] = last_codes[:], last_scales[:]
-        quantise_into(last_codes[:, 0 : 2 * N], last_scales[:, 0 : 2 * N], front[:])
-        quantise_into(last_codes[:, 2 * N : 3 * N], last_scales[:, 2 * N : 3 * N], rear[:, 0:W])
-        last_words = keep.tile([P, 2 * C], U32, name="last_words", tag="front", align_bytes=64)
-        for a in (2, 3):
-            gather_pass(last_words[:, (a - 2) * C : (a - 1) * C], a, E - 1, E)
-        quantise_into(last_codes[:, 3 * N : 4 * N], last_scales[:, 3 * N : 4 * N], rear[:, W : 2 * W])
-        multiply(E - 1, every)
-        activate(E - 4, E - 2, raw[E - 1][:, 3 * W : 4 * W])
-        activate(E - 2, E - 1, raw[E - 1][:, 2 * C : 3 * C])
-        last = raw[E - 5][:, 4 * C : 5 * C]
+        round_on_scalar(E - 1)
+        quantise(E - 1, E - 3)
+        multiply_ready()
+        at = places_at + place_of(E - 1)
+        gather_words(placed("words_rear", 2 * C, U32, at), E - 2, E - 1, [2, 3])
+        multiply_ready()
+        gather_words(placed("words_last", PASSES * C, U32, strip_at), E - 1, E, range(PASSES))
         halves = [slice(h * N, (h + 1) * N) for h in range(2)]
-        for h in halves:
+        ends = [psum.tile([P, N], F32, name="ends", tag="bank%d" % bank) for bank in (7, 0)]
+        for a in range(PASSES):
+            for h, columns in enumerate(halves):
+                nc.tensor.matmul_mx(
+                    out=ends[h][:],
+                    lhsT=w_codes[E - 1][:, a * N : (a + 1) * N].bitcast(FP8X4),
+                    lhsT_scale=w_scales[E - 1][:, a * N : (a + 1) * N],
+                    rhs=slot_words[E - 1, a][:, columns].bitcast(FP8X4),
+                    rhs_scale=slot_scales[4 * a : P, (E - 1) * C : E * C][:, columns],
+                    start=(a == 0),
+                    stop=(a == PASSES - 1),
+                )
+        activate(E - 6, E - 4, at + quarter)
+        activate(E - 4, E - 2, at + 2 * quarter)
+        activate(E - 2, E - 1, at + 3 * quarter)
+        last = keep.tile([P, C], F32, name="last")
+        for end, h in zip(ends, halves):
             nc.vector.tensor_scalar(
-                out=last[:, h], in0=sums[E - 1][:, h], scalar1=bias[:, E - 1 : E], scalar2=0.0, op0=ALU.add, op1=ALU.max
+                out=last[:, h], in0=end[:], scalar1=bias[:, E - 1 : E], scalar2=0.0, op0=ALU.add, op1=ALU.max
             )
         for h in halves:
             nc.vector.tensor_tensor(out=y[:, (E - 1) * C : E * C][:, h], in0=last[:, h], in1=last[:, h], op=ALU.mult)
 
-        first = wide_tile(0, F32, "first")
-        second = wide_tile(7, F32, "second")
-        total = wide_tile(9, F32, "total")
+        first = placed("first", T, F32, places_at)
+        second = placed("second", T, F32, places_at + 2 * PLACE)
+        total = placed("total", T, F32, places_at + 4 * PLACE)
 
         def fetch(dst, lst, r, lo, hi):
+            i = max(j for j, (start, end) in enumerate(GATED) if start <= lo)
+            own = gates[i][:, r, lo - GATED[i][0] : hi - GATED[i][0]]
             nc.vector.tensor_tensor(
-                out=dst[:, lo:hi], in0=y[:].indirect(lst[:, lo // 16 : hi // 16]), in1=gates[r][:, lo:hi], op=ALU.mult
+                out=dst[:, lo:hi], in0=y[:].indirect(lst[:, lo // 16 : hi // 16]), in1=own, op=ALU.mult
             )
 
         def combine(lo, hi):
@@ -303,7 +285,7 @@ def tile_moe_pkd_lin_relu2_kernel(
             nc.scalar.copy(out=total[:, lo:hi], in_=back[:])
             nc.scalar.dma_start(out=out[:, lo:hi], in_=total[:, lo:hi])
 
-        turned = wide_tile(1, F32, "turned")
+        turned = placed("turned", T, F32, places_at + 6 * PLACE)
         blocks = []
         for lo, hi in TURNED:
             fetch(first, first_list, 0, lo, hi)

@@ -53,7 +53,7 @@ def tile_moe_pkd_lin_relu2_kernel(
         bias = keep.tile([P, E], F32, name="bias")
         y = keep.tile([P, SLOTS], F32, name="y")
         identity = keep.tile([P, P], F32, name="identity")
-        nc.gpsimd.memset(token_scales[:].bitcast(I32), 0)
+        nc.gpsimd.memset(token_scales[64:P, :].bitcast(I32), 0)
         make_identity(nc, identity[:])
 
         raw = {}
@@ -137,15 +137,16 @@ def tile_moe_pkd_lin_relu2_kernel(
             ready = [e for e in w_codes if e not in multiplied and (e, PASSES - 1) in slot_words]
             for e in ready:
                 sums[e] = psum.tile([P, C], F32, name="sums", tag="bank%d" % (e % 8))
-                for a in range(PASSES):
+                order = range(PASSES - 1, -1, -1)
+                for a in order:
                     nc.tensor.matmul_mx(
                         out=sums[e][:],
                         lhsT=w_codes[e][:, a * N : (a + 1) * N].bitcast(FP8X4),
                         lhsT_scale=w_scales[e][:, a * N : (a + 1) * N],
                         rhs=slot_words[e, a].bitcast(FP8X4),
                         rhs_scale=slot_scales[4 * a : P, e * C : (e + 1) * C],
-                        start=(a == 0),
-                        stop=(a == PASSES - 1),
+                        start=(a == order[0]),
+                        stop=(a == order[-1]),
                     )
             multiplied.extend(ready)
 
@@ -160,13 +161,19 @@ def tile_moe_pkd_lin_relu2_kernel(
                 )
             nc.scalar.activation(out=y[:, lo * C : hi * C], in_=scratch[:], func=ACT.Square)
 
-        nc.sync.dma_start(slot_list[:], offs)
-        nc.sync.dma_start(first_list[:], pos1)
-        for q in range(4):
+        def load_scales(q):
             nc.sync.dma_start(
                 out=token_scales[32 * q : 32 * q + 16, :].bitcast(I32),
                 in_=x_scales[:, 4 * q : 4 * q + 4, :].bitcast(I32),
             )
+
+        load_scales(0)
+        load_scales(1)
+        nc.sync.dma_start(slot_list[:], offs)
+        for q in range(2):
+            nc.sync.dma_start(out=token_scales[32 * q + 16 : 32 * q + 32, :].bitcast(I32), in_=x_scales[q].bitcast(I32))
+        load_scales(2)
+        load_scales(3)
         load_weights(0)
         for a in range(PASSES):
             load_words(a)
@@ -175,6 +182,7 @@ def tile_moe_pkd_lin_relu2_kernel(
         nc.sync.dma_start(out=bias[:], in_=b)
         for e in range(3, PLACES):
             load_weights(e)
+        nc.sync.dma_start(first_list[:], pos1)
         nc.sync.dma_start(second_list[:], pos2)
 
         for lo, hi in WIDE:
@@ -240,12 +248,15 @@ def tile_moe_pkd_lin_relu2_kernel(
         activate(E - 4, E - 2, at + 2 * quarter)
         activate(E - 2, E - 1, at + 3 * quarter)
         last = keep.tile([P, C], F32, name="last")
-        for end, h in zip(ends, halves):
-            nc.vector.tensor_scalar(
-                out=last[:, h], in0=end[:], scalar1=bias[:, E - 1 : E], scalar2=0.0, op0=ALU.add, op1=ALU.max
-            )
-        for h in halves:
-            nc.vector.tensor_tensor(out=y[:, (E - 1) * C : E * C][:, h], in0=last[:, h], in1=last[:, h], op=ALU.mult)
+        y_last = y[:, (E - 1) * C : E * C]
+        nc.scalar.activation(out=last[:, halves[0]], in_=ends[0][:], func=ACT.Relu, bias=bias[:, E - 1 : E])
+        nc.scalar.activation(out=y_last[:, halves[0]], in_=last[:, halves[0]], func=ACT.Square)
+        nc.vector.tensor_scalar(
+            out=last[:, halves[1]], in0=ends[1][:], scalar1=bias[:, E - 1 : E], scalar2=0.0, op0=ALU.add, op1=ALU.max
+        )
+        nc.vector.tensor_tensor(
+            out=y_last[:, halves[1]], in0=last[:, halves[1]], in1=last[:, halves[1]], op=ALU.mult
+        )
 
         first = placed("first", T, F32, places_at)
         second = placed("second", T, F32, places_at + 2 * PLACE)

@@ -25,12 +25,14 @@ W = PASSES * N
 PLACE = T * 4
 PLACES = 12
 HEAD = 5
+SIX = 6
 GROUP = 3
+BEHIND = {4: (0, 2), 6: (2, 4), 8: (4, 5), 12: (5, 7)}
 ROOMS = 8
-TURNED = [(0, 128), (128, 384), (384, 896), (896, 1152), (1152, 1408)]
-ADDED = [(1408, 1664), (1664, 1920), (1920, 2048)]
-GATED = [(0, 896), (896, 1408), (1408, 2048)]
-BLOCK = 256
+TURNED = [(0, 512), (512, 896), (896, 1280), (1280, 1536)]
+ADDED = [(1536, 1920), (1920, 2048)]
+GATED = [(0, 896), (896, 1536), (1536, 2048)]
+BLOCK = 512
 RUN = 4
 
 
@@ -41,7 +43,7 @@ def tile_moe_pkd_lin_relu2_kernel(
     with ExitStack() as ctx:
         keep = ctx.enter_context(tc.tile_pool(name="keep", bufs=1))
         wide = ctx.enter_context(tc.tile_pool(name="wide", bufs=1))
-        small = ctx.enter_context(tc.tile_pool(name="small", bufs=2))
+        small = ctx.enter_context(tc.tile_pool(name="small", bufs=3))
         psum = ctx.enter_context(tc.psum_pool(name="psum", bufs=1))
 
         slot_list = keep.tile([P, SLOTS // 16], U16, name="slot_list")
@@ -137,7 +139,7 @@ def tile_moe_pkd_lin_relu2_kernel(
             ready = [e for e in w_codes if e not in multiplied and (e, PASSES - 1) in slot_words]
             for e in ready:
                 sums[e] = psum.tile([P, C], F32, name="sums", tag="bank%d" % (e % 8))
-                order = range(PASSES - 1, -1, -1)
+                order = range(PASSES - 1, -1, -1) if e < E - 2 else range(PASSES)
                 for a in order:
                     nc.tensor.matmul_mx(
                         out=sums[e][:],
@@ -209,28 +211,31 @@ def tile_moe_pkd_lin_relu2_kernel(
                     nc.sync.dma_start(out=both, in_=gate[:, :, lo:hi].rearrange("r p t -> p r t"))
                     gates.append(both)
             at = places_at + place_of(even)
-            if 4 <= even <= 12:
-                activate(even - 4, even - 2, at + 3 * quarter)
+            if even in BEHIND:
+                activate(*BEHIND[even], at + 3 * quarter)
             if even < E - 2:
                 quantise(odd, even)
             else:
                 quantise(even)
             multiply_ready()
             run = odd // 2
-            if even < E - 2:
-                lo = HEAD + GROUP * (run // 2)
+            if run < PASSES:
+                gather_words(placed("words%d" % run, SIX * C, U32, at), HEAD, HEAD + SIX, [run])
+            elif even < E - 2:
                 words = placed("words%d" % run, 2 * GROUP * C, U32, at)
-                gather_words(words, lo, lo + GROUP, [2 * (run % 2), 2 * (run % 2) + 1])
+                gather_words(words, HEAD + SIX, E - 2, [2 * (run % 2), 2 * (run % 2) + 1])
             else:
-                gather_words(placed("words%d" % run, 2 * C, U32, at), even, even + 1, [0, 1])
+                gather_words(placed("words%d" % run, 2 * C, U32, at), E - 2, E, [0])
             multiply_ready()
         round_on_scalar(E - 1)
         quantise(E - 1, E - 3)
         multiply_ready()
         at = places_at + place_of(E - 1)
-        gather_words(placed("words_rear", 2 * C, U32, at), E - 2, E - 1, [2, 3])
+        gather_words(placed("words_pair", 2 * C, U32, at), E - 2, E, [1])
+        gather_words(placed("words_rear", 2 * C, U32, strip_at), E - 2, E - 1, [2, 3])
         multiply_ready()
-        gather_words(placed("words_last", PASSES * C, U32, strip_at), E - 1, E, range(PASSES))
+        gather_words(placed("words_last", 2 * C, U32, strip_at + quarter), E - 1, E, [2, 3])
+        activate(7, 9, at + quarter)
         halves = [slice(h * N, (h + 1) * N) for h in range(2)]
         ends = [psum.tile([P, N], F32, name="ends", tag="bank%d" % bank) for bank in (7, 0)]
         for a in range(PASSES):
@@ -244,18 +249,20 @@ def tile_moe_pkd_lin_relu2_kernel(
                     start=(a == 0),
                     stop=(a == PASSES - 1),
                 )
-        activate(E - 6, E - 4, at + quarter)
-        activate(E - 4, E - 2, at + 2 * quarter)
-        activate(E - 2, E - 1, at + 3 * quarter)
-        last = keep.tile([P, C], F32, name="last")
+        activate(9, 11, at + 2 * quarter)
+        activate(11, 13, at + 3 * quarter)
+        activate(13, 14, at + quarter)
+        activate(14, 15, at + quarter)
+        front = placed("front", N, F32, at + quarter)
+        rear = keep.tile([P, N], F32, name="rear")
         y_last = y[:, (E - 1) * C : E * C]
-        nc.scalar.activation(out=last[:, halves[0]], in_=ends[0][:], func=ACT.Relu, bias=bias[:, E - 1 : E])
-        nc.scalar.activation(out=y_last[:, halves[0]], in_=last[:, halves[0]], func=ACT.Square)
+        nc.scalar.activation(out=front[:], in_=ends[0][:], func=ACT.Relu, bias=bias[:, E - 1 : E])
+        nc.scalar.activation(out=y_last[:, halves[0]], in_=front[:], func=ACT.Square)
         nc.vector.tensor_scalar(
-            out=last[:, halves[1]], in0=ends[1][:], scalar1=bias[:, E - 1 : E], scalar2=0.0, op0=ALU.add, op1=ALU.max
+            out=rear[:], in0=ends[1][:], scalar1=bias[:, E - 1 : E], scalar2=0.0, op0=ALU.add, op1=ALU.max
         )
         nc.vector.tensor_tensor(
-            out=y_last[:, halves[1]], in0=last[:, halves[1]], in1=last[:, halves[1]], op=ALU.mult
+            out=y_last[:, halves[1]], in0=rear[:], in1=rear[:], op=ALU.mult
         )
 
         first = placed("first", T, F32, places_at)
@@ -307,9 +314,11 @@ def tile_moe_pkd_lin_relu2_kernel(
                 if len(blocks) > 1:
                     turn_back(len(blocks) - 2, *blocks[-2])
         turn_back(len(blocks) - 1, *blocks[-1])
-        for i, (lo, hi) in enumerate(ADDED):
-            fetch(first, first_list, 0, lo, hi)
-            fetch(second, second_list, 1, lo, hi)
-            if i > 0:
-                combine(*ADDED[i - 1])
-        combine(*ADDED[-1])
+        (lo, mid), (mid, hi) = ADDED
+        fetch(first, first_list, 0, lo, mid)
+        fetch(second, second_list, 1, lo, mid)
+        fetch(first, first_list, 0, mid, hi)
+        combine(lo, mid - P)
+        fetch(second, second_list, 1, mid, hi)
+        combine(mid - P, mid)
+        combine(mid, hi)

@@ -20,20 +20,29 @@ FP8X4 = mybir.dt.float8_e4m3fn_x4
 ACT = mybir.ActivationFunctionType
 ALU = mybir.AluOpType
 
-WIDE = [(0, 1536), (1536, 3072), (3072, 4096)]
-W = PASSES * N
-PLACE = T * 4
+STRIPE = 16
+QUADRANT = 32
+LIVE = PASSES * 4
+BANKS = 8
+WORDS = PASSES * N
+VALUES = WORDS * PACK
+
+ROOMS = E // 2
 PLACES = 12
-HEAD = 5
-SIX = 6
-GROUP = 3
+PLACES_AT = ROOMS * VALUES * 2
+PLACE = VALUES * 4
+QUARTER = PLACE // 4
+
+SCALE_GATHERS = [(0, 1536), (1536, 3072), (3072, 4096)]
+FIRST_GROUP = (0, 5)
+SECOND_GROUP = (5, 11)
+THIRD_GROUP = (11, 14)
 BEHIND = {4: (0, 2), 6: (2, 4), 8: (4, 5), 12: (5, 7)}
-ROOMS = 8
-TURNED = [(0, 512), (512, 896), (896, 1280), (1280, 1536)]
-ADDED = [(1536, 1920), (1920, 2048)]
-GATED = [(0, 896), (896, 1536), (1536, 2048)]
-BLOCK = 512
-RUN = 4
+TURNED = [(0, 128), (128, 384), (384, 640), (640, 896), (896, 1152), (1152, 1408)]
+ADDED = [(1408, 1664), (1664, 1920), (1920, 2048)]
+GATED = [(0, 896), (896, 1408), (1408, 2048)]
+GATE_PLACES = (9, 11)
+LINE = 4
 
 
 def tile_moe_pkd_lin_relu2_kernel(
@@ -42,20 +51,20 @@ def tile_moe_pkd_lin_relu2_kernel(
     nc = tc.nc
     with ExitStack() as ctx:
         keep = ctx.enter_context(tc.tile_pool(name="keep", bufs=1))
-        wide = ctx.enter_context(tc.tile_pool(name="wide", bufs=1))
-        small = ctx.enter_context(tc.tile_pool(name="small", bufs=3))
+        reused = ctx.enter_context(tc.tile_pool(name="reused", bufs=1))
+        pairs = ctx.enter_context(tc.tile_pool(name="pairs", bufs=3))
         psum = ctx.enter_context(tc.psum_pool(name="psum", bufs=1))
 
-        slot_list = keep.tile([P, SLOTS // 16], U16, name="slot_list")
-        first_list = keep.tile([P, T // 16], U16, name="first_list")
-        second_list = keep.tile([P, T // 16], U16, name="second_list")
+        slot_list = keep.tile([P, SLOTS // STRIPE], U16, name="slot_list")
+        first_list = keep.tile([P, T // STRIPE], U16, name="first_list")
+        second_list = keep.tile([P, T // STRIPE], U16, name="second_list")
         token_scales = keep.tile([P, T], U8, name="token_scales", align_bytes=64)
         slot_scales = keep.tile([P, SLOTS], U8, name="slot_scales", align_bytes=64)
         token_words = [keep.tile([P, T], I32, name="token_words%d" % a, align_bytes=64) for a in range(PASSES)]
         bias = keep.tile([P, E], F32, name="bias")
         y = keep.tile([P, SLOTS], F32, name="y")
         identity = keep.tile([P, P], F32, name="identity")
-        nc.gpsimd.memset(token_scales[64:P, :].bitcast(I32), 0)
+        nc.gpsimd.memset(token_scales[2 * QUADRANT : P, :].bitcast(I32), 0)
         make_identity(nc, identity[:])
 
         raw = {}
@@ -64,40 +73,44 @@ def tile_moe_pkd_lin_relu2_kernel(
         slot_words = {}
         sums = {}
 
-        def placed(name, columns, dtype, at):
-            return wide.tile([P, columns], dtype, name=name, offset=at, align_bytes=64)
+        def placed(name, columns, dtype, byte):
+            return reused.tile([P, columns], dtype, name=name, offset=byte, align_bytes=64)
 
         def place_of(e):
-            return PLACE * (e if e < PLACES else 2 * (e - PLACES) + 1)
+            return PLACES_AT + PLACE * (e if e < PLACES else 2 * (e - PLACES) + 1)
 
-        strip_at = 0
-        strip = placed("strip", ROOMS * W * PACK, BF16, strip_at)
-        places_at = ROOMS * W * PACK * 2
+        rooms = placed("rooms", ROOMS * VALUES, BF16, 0)
 
         def rounded(e, count=1):
             room = e // 2 if e < E - 1 else (E - 3) // 2 - 1
-            return strip[:, room * W * PACK : (room + count) * W * PACK]
+            return rooms[:, room * VALUES : (room + count) * VALUES]
+
+        def load_scales(q):
+            nc.sync.dma_start(
+                out=token_scales[QUADRANT * q : QUADRANT * q + LIVE, :].bitcast(I32),
+                in_=x_scales[:, 4 * q : 4 * q + 4, :].bitcast(I32),
+            )
 
         def load_words(a):
             nc.sync.dma_start(out=token_words[a][:], in_=x_words[a].rearrange("p t r -> p (t r)").bitcast(I32))
 
         def load_weights(e):
-            raw[e] = placed("raw%d" % e, T, F32, places_at + place_of(e))
+            raw[e] = placed("raw%d" % e, VALUES, F32, place_of(e))
             nc.sync.dma_start(
-                out=raw[e][:].rearrange("p (a m) -> p a m", m=W),
+                out=raw[e][:].rearrange("p (a m) -> p a m", a=PASSES),
                 in_=w[e].rearrange("(a p j) n -> p a (j n)", a=PASSES, j=PACK),
             )
 
         def round_on_scalar(e):
             nc.scalar.copy(
-                out=rounded(e).rearrange("p (a c i j) -> p a c j i", a=PASSES, i=RUN, j=PACK),
-                in_=raw[e][:].rearrange("p (a j c i) -> p a c j i", a=PASSES, j=PACK, i=RUN),
+                out=rounded(e).rearrange("p (a c i j) -> p a c j i", a=PASSES, i=LINE, j=PACK),
+                in_=raw[e][:].rearrange("p (a j c i) -> p a c j i", a=PASSES, j=PACK, i=LINE),
             )
 
         def round_on_gpsimd(e):
             nc.gpsimd.tensor_scalar(
-                out=rounded(e).rearrange("p (a c j) -> p a c j", a=PASSES, j=PACK),
-                in0=raw[e][:].rearrange("p (a j c) -> p a c j", a=PASSES, j=PACK),
+                out=rounded(e).rearrange("p (a n j) -> p a n j", a=PASSES, j=PACK),
+                in0=raw[e][:].rearrange("p (a j n) -> p a n j", a=PASSES, j=PACK),
                 scalar1=1.0,
                 scalar2=0.0,
                 op0=ALU.mult,
@@ -106,74 +119,72 @@ def tile_moe_pkd_lin_relu2_kernel(
 
         def quantise(*experts):
             if len(experts) == 1:
-                codes = keep.tile([P, W], U32, name="lone_codes", align_bytes=64)
-                scales = keep.tile([P, W], U8, name="lone_scales", align_bytes=64)
+                codes = keep.tile([P, WORDS], U32, name="lone_codes", align_bytes=64)
+                scales = keep.tile([P, WORDS], U8, name="lone_scales", align_bytes=64)
             else:
-                codes = small.tile([P, 2 * W], U32, name="codes", align_bytes=64)
-                scales = small.tile([P, 2 * W], U8, name="scales", align_bytes=64)
+                codes = pairs.tile([P, 2 * WORDS], U32, name="codes", align_bytes=64)
+                scales = pairs.tile([P, 2 * WORDS], U8, name="scales", align_bytes=64)
             for i, e in enumerate(experts):
-                w_codes[e] = codes[:, i * W : (i + 1) * W]
-                w_scales[e] = scales[:, i * W : (i + 1) * W]
+                w_codes[e] = codes[:, i * WORDS : (i + 1) * WORDS]
+                w_scales[e] = scales[:, i * WORDS : (i + 1) * WORDS]
             nc.vector.quantize_mx(
                 out=codes[:].bitcast(FP8X4), scales=scales[:], in_=rounded(experts[0], len(experts))
             )
 
-        def gather_scales(lo, hi):
-            nc.vector.tensor_copy(
-                out=slot_scales[:, lo:hi], in_=token_scales[:].indirect(slot_list[:, lo // 16 : hi // 16])
-            )
-
-        def gather_words(words, lo, hi, passes):
+        def gather_words(words, group, passes):
+            lo, hi = group
             width = (hi - lo) * C
+            offsets = slot_list[:, lo * C // STRIPE : hi * C // STRIPE]
             for i, a in enumerate(passes):
                 dst = words[:, i * width : (i + 1) * width]
-                nc.vector.tensor_copy(
-                    out=dst, in_=token_words[a][:].bitcast(U32).indirect(slot_list[:, lo * C // 16 : hi * C // 16])
-                )
+                nc.vector.tensor_copy(out=dst, in_=token_words[a][:].bitcast(U32).indirect(offsets))
                 for e in range(lo, hi):
                     slot_words[e, a] = dst[:, (e - lo) * C : (e - lo + 1) * C]
 
-        multiplied = []
+        def multiply_pass(dst, e, a, columns, start, stop):
+            nc.tensor.matmul_mx(
+                out=dst,
+                lhsT=w_codes[e][:, a * N : (a + 1) * N].bitcast(FP8X4),
+                lhsT_scale=w_scales[e][:, a * N : (a + 1) * N],
+                rhs=slot_words[e, a][:, columns].bitcast(FP8X4),
+                rhs_scale=slot_scales[4 * a : P, e * C : (e + 1) * C][:, columns],
+                start=start,
+                stop=stop,
+            )
 
         def multiply_ready():
-            ready = [e for e in w_codes if e not in multiplied and (e, PASSES - 1) in slot_words]
+            ready = [e for e in w_codes if e not in sums and (e, PASSES - 1) in slot_words]
             for e in ready:
-                sums[e] = psum.tile([P, C], F32, name="sums", tag="bank%d" % (e % 8))
+                sums[e] = psum.tile([P, C], F32, name="sums", tag="bank%d" % (e % BANKS))
                 order = range(PASSES - 1, -1, -1) if e < E - 2 else range(PASSES)
                 for a in order:
-                    nc.tensor.matmul_mx(
-                        out=sums[e][:],
-                        lhsT=w_codes[e][:, a * N : (a + 1) * N].bitcast(FP8X4),
-                        lhsT_scale=w_scales[e][:, a * N : (a + 1) * N],
-                        rhs=slot_words[e, a].bitcast(FP8X4),
-                        rhs_scale=slot_scales[4 * a : P, e * C : (e + 1) * C],
-                        start=(a == order[0]),
-                        stop=(a == order[-1]),
-                    )
-            multiplied.extend(ready)
+                    multiply_pass(sums[e][:], e, a, slice(0, C), a == order[0], a == order[-1])
 
-        def activate(lo, hi, at):
-            scratch = placed("positive%d" % lo, (hi - lo) * C, F32, at)
+        def activate(lo, hi, byte):
+            positive = placed("positive%d" % lo, (hi - lo) * C, F32, byte)
             for e in range(lo, hi):
                 nc.scalar.activation(
-                    out=scratch[:, (e - lo) * C : (e - lo + 1) * C],
+                    out=positive[:, (e - lo) * C : (e - lo + 1) * C],
                     in_=sums[e][:],
                     func=ACT.Relu,
                     bias=bias[:, e : e + 1],
                 )
-            nc.scalar.activation(out=y[:, lo * C : hi * C], in_=scratch[:], func=ACT.Square)
+            nc.scalar.activation(out=y[:, lo * C : hi * C], in_=positive[:], func=ACT.Square)
 
-        def load_scales(q):
-            nc.sync.dma_start(
-                out=token_scales[32 * q : 32 * q + 16, :].bitcast(I32),
-                in_=x_scales[:, 4 * q : 4 * q + 4, :].bitcast(I32),
-            )
+        def load_gates():
+            starts = [place_of(GATE_PLACES[0]), place_of(GATE_PLACES[1])]
+            starts.append(starts[1] + 2 * (GATED[1][1] - GATED[1][0]) * 4)
+            for byte, (lo, hi) in zip(starts, GATED):
+                both = placed("gates%d" % lo, 2 * (hi - lo), F32, byte)[:].rearrange("p (r t) -> p r t", r=2)
+                nc.sync.dma_start(out=both, in_=gate[:, :, lo:hi].rearrange("r p t -> p r t"))
+                gates.append(both)
 
         load_scales(0)
         load_scales(1)
         nc.sync.dma_start(slot_list[:], offs)
         for q in range(2):
-            nc.sync.dma_start(out=token_scales[32 * q + 16 : 32 * q + 32, :].bitcast(I32), in_=x_scales[q].bitcast(I32))
+            unused = token_scales[QUADRANT * q + LIVE : QUADRANT * (q + 1), :]
+            nc.sync.dma_start(out=unused.bitcast(I32), in_=x_scales[q].bitcast(I32))
         load_scales(2)
         load_scales(3)
         load_weights(0)
@@ -187,103 +198,93 @@ def tile_moe_pkd_lin_relu2_kernel(
         nc.sync.dma_start(first_list[:], pos1)
         nc.sync.dma_start(second_list[:], pos2)
 
-        for lo, hi in WIDE:
-            gather_scales(lo, hi)
+        for lo, hi in SCALE_GATHERS:
+            nc.vector.tensor_copy(
+                out=slot_scales[:, lo:hi], in_=token_scales[:].indirect(slot_list[:, lo // STRIPE : hi // STRIPE])
+            )
         for a in range(PASSES):
-            head_words = keep.tile([P, HEAD * C], U32, name="head_words%d" % a, align_bytes=64)
-            gather_words(head_words, 0, HEAD, [a])
+            first_words = keep.tile([P, FIRST_GROUP[1] * C], U32, name="first_words%d" % a, align_bytes=64)
+            gather_words(first_words, FIRST_GROUP, [a])
         round_on_scalar(0)
         quantise(0)
         multiply_ready()
 
         gates = []
-        quarter = PLACE // 4
-        for odd in range(1, E - 1, 2):
+        last_pair = (E - 2, E)
+        for run, odd in enumerate(range(1, E - 1, 2)):
             even = odd + 1
             round_on_gpsimd(odd)
             round_on_scalar(even)
-            if PLACES + odd // 2 < E:
-                load_weights(PLACES + odd // 2)
-            if odd == 11:
-                for i, (lo, hi) in enumerate(GATED):
-                    at = places_at + (9 * PLACE if i == 0 else 11 * PLACE + (lo - GATED[1][0]) * 8)
-                    both = placed("gates%d" % i, 2 * (hi - lo), F32, at)[:].rearrange("p (r t) -> p r t", r=2)
-                    nc.sync.dma_start(out=both, in_=gate[:, :, lo:hi].rearrange("r p t -> p r t"))
-                    gates.append(both)
-            at = places_at + place_of(even)
+            if PLACES + run < E:
+                load_weights(PLACES + run)
+            if odd == GATE_PLACES[1]:
+                load_gates()
             if even in BEHIND:
-                activate(*BEHIND[even], at + 3 * quarter)
+                activate(*BEHIND[even], place_of(even) + 3 * QUARTER)
             if even < E - 2:
                 quantise(odd, even)
             else:
                 quantise(even)
             multiply_ready()
-            run = odd // 2
             if run < PASSES:
-                gather_words(placed("words%d" % run, SIX * C, U32, at), HEAD, HEAD + SIX, [run])
+                group, passes = SECOND_GROUP, [run]
             elif even < E - 2:
-                words = placed("words%d" % run, 2 * GROUP * C, U32, at)
-                gather_words(words, HEAD + SIX, E - 2, [2 * (run % 2), 2 * (run % 2) + 1])
+                group, passes = THIRD_GROUP, [2 * (run - PASSES), 2 * (run - PASSES) + 1]
             else:
-                gather_words(placed("words%d" % run, 2 * C, U32, at), E - 2, E, [0])
+                group, passes = last_pair, [0]
+            words = placed("words%d" % run, len(passes) * (group[1] - group[0]) * C, U32, place_of(even))
+            gather_words(words, group, passes)
             multiply_ready()
+
         round_on_scalar(E - 1)
         quantise(E - 1, E - 3)
         multiply_ready()
-        at = places_at + place_of(E - 1)
-        gather_words(placed("words_pair", 2 * C, U32, at), E - 2, E, [1])
-        gather_words(placed("words_rear", 2 * C, U32, strip_at), E - 2, E - 1, [2, 3])
+        last_place = place_of(E - 1)
+        gather_words(placed("words_pair", 2 * C, U32, last_place), last_pair, [1])
+        gather_words(placed("words_rear", 2 * C, U32, 0), (E - 2, E - 1), [2, 3])
         multiply_ready()
-        gather_words(placed("words_last", 2 * C, U32, strip_at + quarter), E - 1, E, [2, 3])
-        activate(7, 9, at + quarter)
-        halves = [slice(h * N, (h + 1) * N) for h in range(2)]
-        ends = [psum.tile([P, N], F32, name="ends", tag="bank%d" % bank) for bank in (7, 0)]
+        gather_words(placed("words_last", 2 * C, U32, QUARTER), (E - 1, E), [2, 3])
+
+        activate(7, 9, last_place + QUARTER)
+        halves = [slice(0, C // 2), slice(C // 2, C)]
+        half_sums = [psum.tile([P, C // 2], F32, name="half_sums", tag="bank%d" % (e % BANKS)) for e in (7, 8)]
         for a in range(PASSES):
-            for h, columns in enumerate(halves):
-                nc.tensor.matmul_mx(
-                    out=ends[h][:],
-                    lhsT=w_codes[E - 1][:, a * N : (a + 1) * N].bitcast(FP8X4),
-                    lhsT_scale=w_scales[E - 1][:, a * N : (a + 1) * N],
-                    rhs=slot_words[E - 1, a][:, columns].bitcast(FP8X4),
-                    rhs_scale=slot_scales[4 * a : P, (E - 1) * C : E * C][:, columns],
-                    start=(a == 0),
-                    stop=(a == PASSES - 1),
-                )
-        activate(9, 11, at + 2 * quarter)
-        activate(11, 13, at + 3 * quarter)
-        activate(13, 14, at + quarter)
-        activate(14, 15, at + quarter)
-        front = placed("front", N, F32, at + quarter)
-        rear = keep.tile([P, N], F32, name="rear")
+            for half_sum, columns in zip(half_sums, halves):
+                multiply_pass(half_sum[:], E - 1, a, columns, a == 0, a == PASSES - 1)
+        activate(9, 11, last_place + 2 * QUARTER)
+        activate(11, 13, last_place + 3 * QUARTER)
+        activate(13, 14, last_place + QUARTER)
+        activate(14, 15, last_place + QUARTER)
+        front = placed("front", C // 2, F32, last_place + QUARTER)
+        rear = keep.tile([P, C // 2], F32, name="rear")
         y_last = y[:, (E - 1) * C : E * C]
-        nc.scalar.activation(out=front[:], in_=ends[0][:], func=ACT.Relu, bias=bias[:, E - 1 : E])
+        last_bias = bias[:, E - 1 : E]
+        nc.scalar.activation(out=front[:], in_=half_sums[0][:], func=ACT.Relu, bias=last_bias)
         nc.scalar.activation(out=y_last[:, halves[0]], in_=front[:], func=ACT.Square)
         nc.vector.tensor_scalar(
-            out=rear[:], in0=ends[1][:], scalar1=bias[:, E - 1 : E], scalar2=0.0, op0=ALU.add, op1=ALU.max
+            out=rear[:], in0=half_sums[1][:], scalar1=last_bias, scalar2=0.0, op0=ALU.add, op1=ALU.max
         )
-        nc.vector.tensor_tensor(
-            out=y_last[:, halves[1]], in0=rear[:], in1=rear[:], op=ALU.mult
-        )
+        nc.vector.tensor_tensor(out=y_last[:, halves[1]], in0=rear[:], in1=rear[:], op=ALU.mult)
 
-        first = placed("first", T, F32, places_at)
-        second = placed("second", T, F32, places_at + 2 * PLACE)
-        total = placed("total", T, F32, places_at + 4 * PLACE)
+        first = placed("first", T, F32, place_of(0))
+        second = placed("second", T, F32, place_of(2))
+        total = placed("total", T, F32, place_of(4))
+        turned = placed("turned", T, F32, place_of(6))
 
-        def fetch(dst, lst, r, lo, hi):
+        def fetch(lo, hi):
             i = max(j for j, (start, end) in enumerate(GATED) if start <= lo)
-            own = gates[i][:, r, lo - GATED[i][0] : hi - GATED[i][0]]
-            nc.vector.tensor_tensor(
-                out=dst[:, lo:hi], in0=y[:].indirect(lst[:, lo // 16 : hi // 16]), in1=own, op=ALU.mult
-            )
+            for r, (dst, positions) in enumerate(((first, first_list), (second, second_list))):
+                nc.vector.tensor_tensor(
+                    out=dst[:, lo:hi],
+                    in0=y[:].indirect(positions[:, lo // STRIPE : hi // STRIPE]),
+                    in1=gates[i][:, r, lo - GATED[i][0] : hi - GATED[i][0]],
+                    op=ALU.mult,
+                )
 
-        def combine(lo, hi):
-            nc.vector.tensor_tensor(out=total[:, lo:hi], in0=first[:, lo:hi], in1=second[:, lo:hi], op=ALU.add)
-            nc.sync.dma_start(out=out[:, lo:hi], in_=total[:, lo:hi])
-
-        def sum_turned(i, lo, hi):
-            width = hi - lo
-            summed = psum.tile([P, width], F32, name="summed", tag="bank%d" % (i % 2))
-            for c in range(0, width, P):
+        def sum_turned(i):
+            lo, hi = TURNED[i]
+            summed = psum.tile([P, hi - lo], F32, name="summed", tag="bank%d" % (i % 2))
+            for c in range(0, hi - lo, P):
                 for r, term in enumerate((first, second)):
                     nc.tensor.matmul(
                         summed[:, c : c + P],
@@ -295,30 +296,26 @@ def tile_moe_pkd_lin_relu2_kernel(
                     )
             nc.scalar.copy(out=turned[:, lo:hi], in_=summed[:])
 
-        def turn_back(i, lo, hi):
-            width = hi - lo
-            back = psum.tile([P, width], F32, name="back", tag="bank%d" % (2 + i % 2))
-            for c in range(0, width, P):
+        def turn_back(i):
+            lo, hi = TURNED[i]
+            back = psum.tile([P, hi - lo], F32, name="back", tag="bank%d" % (2 + i % 2))
+            for c in range(0, hi - lo, P):
                 nc.tensor.transpose(back[:, c : c + P], turned[:, lo + c : lo + c + P], identity[:])
             nc.scalar.copy(out=total[:, lo:hi], in_=back[:])
             nc.scalar.dma_start(out=out[:, lo:hi], in_=total[:, lo:hi])
 
-        turned = placed("turned", T, F32, places_at + 6 * PLACE)
-        blocks = []
-        for lo, hi in TURNED:
-            fetch(first, first_list, 0, lo, hi)
-            fetch(second, second_list, 1, lo, hi)
-            for at in range(lo, hi, BLOCK):
-                blocks.append((at, min(at + BLOCK, hi)))
-                sum_turned(len(blocks) - 1, *blocks[-1])
-                if len(blocks) > 1:
-                    turn_back(len(blocks) - 2, *blocks[-2])
-        turn_back(len(blocks) - 1, *blocks[-1])
-        (lo, mid), (mid, hi) = ADDED
-        fetch(first, first_list, 0, lo, mid)
-        fetch(second, second_list, 1, lo, mid)
-        fetch(first, first_list, 0, mid, hi)
-        combine(lo, mid - P)
-        fetch(second, second_list, 1, mid, hi)
-        combine(mid - P, mid)
-        combine(mid, hi)
+        def add(lo, hi):
+            nc.vector.tensor_tensor(out=total[:, lo:hi], in0=first[:, lo:hi], in1=second[:, lo:hi], op=ALU.add)
+            nc.sync.dma_start(out=out[:, lo:hi], in_=total[:, lo:hi])
+
+        for i, (lo, hi) in enumerate(TURNED):
+            fetch(lo, hi)
+            sum_turned(i)
+            if i > 0:
+                turn_back(i - 1)
+        turn_back(len(TURNED) - 1)
+        for i, (lo, hi) in enumerate(ADDED):
+            fetch(lo, hi)
+            if i > 0:
+                add(*ADDED[i - 1])
+        add(*ADDED[-1])

@@ -26,23 +26,24 @@ LIVE = PASSES * 4
 BANKS = 8
 WORDS = PASSES * N
 VALUES = WORDS * PACK
+LINE = 4
 
+ROOM = VALUES * 2
 ROOMS = E // 2
-PLACES = 12
-PLACES_AT = ROOMS * VALUES * 2
 PLACE = VALUES * 4
+PLACES = 12
+PLACES_AT = ROOMS * ROOM
 QUARTER = PLACE // 4
 
-SCALE_GATHERS = [(0, 1536), (1536, 3072), (3072, 4096)]
-FIRST_GROUP = (0, 5)
-SECOND_GROUP = (5, 11)
-THIRD_GROUP = (11, 14)
+RUN = 1536
+HEAD = 5
+BY_PASS = (5, 11)
+BY_TWO_PASSES = (11, 14)
 BEHIND = {4: (0, 2), 6: (2, 4), 8: (4, 5), 12: (5, 7)}
-TURNED = [(0, 128), (128, 384), (384, 640), (640, 896), (896, 1152), (1152, 1408)]
-ADDED = [(1408, 1664), (1664, 1920), (1920, 2048)]
-GATED = [(0, 896), (896, 1408), (1408, 2048)]
-GATE_PLACES = (9, 11)
-LINE = 4
+
+SHARED = [(0, 128), (128, 384), (384, 640), (640, 896), (896, 1152), (1152, 1408), (1408, 1664), (1664, 1792)]
+OWN = (1792, 2048)
+GATED = [(0, 896), (896, 1792), (1792, 2048)]
 
 
 def tile_moe_pkd_lin_relu2_kernel(
@@ -64,7 +65,12 @@ def tile_moe_pkd_lin_relu2_kernel(
         bias = keep.tile([P, E], F32, name="bias")
         y = keep.tile([P, SLOTS], F32, name="y")
         identity = keep.tile([P, P], F32, name="identity")
+        gate_rows = keep.tile([P, P], F32, name="gate_rows")
+        gate_columns = keep.tile([P, T // P], F32, name="gate_columns")
+        first_gates = [keep.tile([P, hi - lo], F32, name="first_gate%d" % lo) for lo, hi in GATED]
+        own_gate = keep.tile([P, OWN[1] - OWN[0]], F32, name="own_gate")
         nc.gpsimd.memset(token_scales[2 * QUADRANT : P, :].bitcast(I32), 0)
+        nc.gpsimd.memset(gate_rows[:], 0.0)
         make_identity(nc, identity[:])
 
         raw = {}
@@ -79,6 +85,12 @@ def tile_moe_pkd_lin_relu2_kernel(
         def place_of(e):
             return PLACES_AT + PLACE * (e if e < PLACES else 2 * (e - PLACES) + 1)
 
+        def bank(name, columns, i):
+            return psum.tile([P, columns], F32, name=name, tag="bank%d" % i)
+
+        def entries(listed, lo, hi):
+            return listed[:, lo // STRIPE : hi // STRIPE]
+
         rooms = placed("rooms", ROOMS * VALUES, BF16, 0)
 
         def rounded(e, count=1):
@@ -90,9 +102,6 @@ def tile_moe_pkd_lin_relu2_kernel(
                 out=token_scales[QUADRANT * q : QUADRANT * q + LIVE, :].bitcast(I32),
                 in_=x_scales[:, 4 * q : 4 * q + 4, :].bitcast(I32),
             )
-
-        def load_words(a):
-            nc.sync.dma_start(out=token_words[a][:], in_=x_words[a].rearrange("p t r -> p (t r)").bitcast(I32))
 
         def load_weights(e):
             raw[e] = placed("raw%d" % e, VALUES, F32, place_of(e))
@@ -131,13 +140,13 @@ def tile_moe_pkd_lin_relu2_kernel(
                 out=codes[:].bitcast(FP8X4), scales=scales[:], in_=rounded(experts[0], len(experts))
             )
 
-        def gather_words(words, group, passes):
-            lo, hi = group
+        def gather_words(words, lo, hi, passes):
             width = (hi - lo) * C
-            offsets = slot_list[:, lo * C // STRIPE : hi * C // STRIPE]
             for i, a in enumerate(passes):
                 dst = words[:, i * width : (i + 1) * width]
-                nc.vector.tensor_copy(out=dst, in_=token_words[a][:].bitcast(U32).indirect(offsets))
+                nc.vector.tensor_copy(
+                    out=dst, in_=token_words[a][:].bitcast(U32).indirect(entries(slot_list, lo * C, hi * C))
+                )
                 for e in range(lo, hi):
                     slot_words[e, a] = dst[:, (e - lo) * C : (e - lo + 1) * C]
 
@@ -155,7 +164,7 @@ def tile_moe_pkd_lin_relu2_kernel(
         def multiply_ready():
             ready = [e for e in w_codes if e not in sums and (e, PASSES - 1) in slot_words]
             for e in ready:
-                sums[e] = psum.tile([P, C], F32, name="sums", tag="bank%d" % (e % BANKS))
+                sums[e] = bank("sums", C, e % BANKS)
                 order = range(PASSES - 1, -1, -1) if e < E - 2 else range(PASSES)
                 for a in order:
                     multiply_pass(sums[e][:], e, a, slice(0, C), a == order[0], a == order[-1])
@@ -171,14 +180,6 @@ def tile_moe_pkd_lin_relu2_kernel(
                 )
             nc.scalar.activation(out=y[:, lo * C : hi * C], in_=positive[:], func=ACT.Square)
 
-        def load_gates():
-            starts = [place_of(GATE_PLACES[0]), place_of(GATE_PLACES[1])]
-            starts.append(starts[1] + 2 * (GATED[1][1] - GATED[1][0]) * 4)
-            for byte, (lo, hi) in zip(starts, GATED):
-                both = placed("gates%d" % lo, 2 * (hi - lo), F32, byte)[:].rearrange("p (r t) -> p r t", r=2)
-                nc.sync.dma_start(out=both, in_=gate[:, :, lo:hi].rearrange("r p t -> p r t"))
-                gates.append(both)
-
         load_scales(0)
         load_scales(1)
         nc.sync.dma_start(slot_list[:], offs)
@@ -189,36 +190,42 @@ def tile_moe_pkd_lin_relu2_kernel(
         load_scales(3)
         load_weights(0)
         for a in range(PASSES):
-            load_words(a)
+            nc.sync.dma_start(out=token_words[a][:], in_=x_words[a].rearrange("p t r -> p (t r)").bitcast(I32))
         load_weights(1)
         load_weights(2)
         nc.sync.dma_start(out=bias[:], in_=b)
+        nc.sync.dma_start(out=gate_rows[0 : T // P, :], in_=gate[1, 0].rearrange("(c t) -> c t", t=P))
         for e in range(3, PLACES):
             load_weights(e)
         nc.sync.dma_start(first_list[:], pos1)
         nc.sync.dma_start(second_list[:], pos2)
 
-        for lo, hi in SCALE_GATHERS:
+        turned_gate = bank("turned_gate", P, BANKS - 1)
+        nc.tensor.transpose(turned_gate[:], gate_rows[:], identity[:])
+        nc.scalar.copy(out=gate_columns[:], in_=turned_gate[:, 0 : T // P])
+
+        for lo in range(0, SLOTS, RUN):
+            hi = min(lo + RUN, SLOTS)
             nc.vector.tensor_copy(
-                out=slot_scales[:, lo:hi], in_=token_scales[:].indirect(slot_list[:, lo // STRIPE : hi // STRIPE])
+                out=slot_scales[:, lo:hi], in_=token_scales[:].indirect(entries(slot_list, lo, hi))
             )
         for a in range(PASSES):
-            first_words = keep.tile([P, FIRST_GROUP[1] * C], U32, name="first_words%d" % a, align_bytes=64)
-            gather_words(first_words, FIRST_GROUP, [a])
+            head_words = keep.tile([P, HEAD * C], U32, name="head_words%d" % a, align_bytes=64)
+            gather_words(head_words, 0, HEAD, [a])
         round_on_scalar(0)
         quantise(0)
         multiply_ready()
 
-        gates = []
-        last_pair = (E - 2, E)
         for run, odd in enumerate(range(1, E - 1, 2)):
             even = odd + 1
             round_on_gpsimd(odd)
             round_on_scalar(even)
             if PLACES + run < E:
                 load_weights(PLACES + run)
-            if odd == GATE_PLACES[1]:
-                load_gates()
+            if PLACES + run == E - 1:
+                nc.sync.dma_start(out=own_gate[:], in_=gate[1, :, OWN[0] : OWN[1]])
+                for i in (2, 0, 1):
+                    nc.sync.dma_start(out=first_gates[i][:], in_=gate[0, :, GATED[i][0] : GATED[i][1]])
             if even in BEHIND:
                 activate(*BEHIND[even], place_of(even) + 3 * QUARTER)
             if even < E - 2:
@@ -227,27 +234,27 @@ def tile_moe_pkd_lin_relu2_kernel(
                 quantise(even)
             multiply_ready()
             if run < PASSES:
-                group, passes = SECOND_GROUP, [run]
+                group, passes = BY_PASS, [run]
             elif even < E - 2:
-                group, passes = THIRD_GROUP, [2 * (run - PASSES), 2 * (run - PASSES) + 1]
+                group, passes = BY_TWO_PASSES, [2 * (run - PASSES), 2 * (run - PASSES) + 1]
             else:
-                group, passes = last_pair, [0]
+                group, passes = (E - 2, E), [0]
             words = placed("words%d" % run, len(passes) * (group[1] - group[0]) * C, U32, place_of(even))
-            gather_words(words, group, passes)
+            gather_words(words, *group, passes)
             multiply_ready()
 
         round_on_scalar(E - 1)
         quantise(E - 1, E - 3)
         multiply_ready()
         last_place = place_of(E - 1)
-        gather_words(placed("words_pair", 2 * C, U32, last_place), last_pair, [1])
-        gather_words(placed("words_rear", 2 * C, U32, 0), (E - 2, E - 1), [2, 3])
+        gather_words(placed("words_pair", 2 * C, U32, last_place), E - 2, E, [1])
+        gather_words(placed("words_rear", 2 * C, U32, 0), E - 2, E - 1, [2, 3])
         multiply_ready()
-        gather_words(placed("words_last", 2 * C, U32, QUARTER), (E - 1, E), [2, 3])
+        gather_words(placed("words_last", 2 * C, U32, QUARTER), E - 1, E, [2, 3])
 
         activate(7, 9, last_place + QUARTER)
         halves = [slice(0, C // 2), slice(C // 2, C)]
-        half_sums = [psum.tile([P, C // 2], F32, name="half_sums", tag="bank%d" % (e % BANKS)) for e in (7, 8)]
+        half_sums = [bank("half_sums", C // 2, e % BANKS) for e in (7, 8)]
         for a in range(PASSES):
             for half_sum, columns in zip(half_sums, halves):
                 multiply_pass(half_sum[:], E - 1, a, columns, a == 0, a == PASSES - 1)
@@ -266,56 +273,66 @@ def tile_moe_pkd_lin_relu2_kernel(
         )
         nc.vector.tensor_tensor(out=y_last[:, halves[1]], in0=rear[:], in1=rear[:], op=ALU.mult)
 
-        first = placed("first", T, F32, place_of(0))
-        second = placed("second", T, F32, place_of(2))
+        slot = 4 * C
+        strip_at = place_of(0)
+        fetched_at = strip_at + 4 * slot
+        scaled_at = place_of(2)
         total = placed("total", T, F32, place_of(4))
-        turned = placed("turned", T, F32, place_of(6))
+        products = {}
+        forward = {}
+        backward = {}
 
-        def fetch(lo, hi):
+        def first_gate(lo, hi):
             i = max(j for j, (start, end) in enumerate(GATED) if start <= lo)
-            for r, (dst, positions) in enumerate(((first, first_list), (second, second_list))):
-                nc.vector.tensor_tensor(
-                    out=dst[:, lo:hi],
-                    in0=y[:].indirect(positions[:, lo // STRIPE : hi // STRIPE]),
-                    in1=gates[i][:, r, lo - GATED[i][0] : hi - GATED[i][0]],
-                    op=ALU.mult,
+            return first_gates[i][:, lo - GATED[i][0] : hi - GATED[i][0]]
+
+        def gated(name, listed, lo, hi, byte, factor):
+            product = placed(name, hi - lo, F32, byte)
+            nc.vector.tensor_tensor(
+                out=product[:], in0=y[:].indirect(entries(listed, lo, hi)), in1=factor, op=ALU.mult
+            )
+            return product
+
+        def fetch(i):
+            lo, hi = SHARED[i]
+            byte = strip_at + slot * i if i < 2 else scaled_at + slot * (i - 2)
+            products[i] = gated("product%d" % i, first_list, lo, hi, byte, first_gate(lo, hi))
+            fetched = placed("fetched%d" % i, hi - lo, F32, fetched_at + slot * (i % 2))
+            nc.scalar.activation(out=fetched[:], in_=y[:].indirect(entries(second_list, lo, hi)), func=ACT.Copy)
+            forward[i] = bank("forward", hi - lo, i % 3)
+            for c in range(0, hi - lo, P):
+                nc.tensor.transpose(forward[i][:, c : c + P], fetched[:, c : c + P], identity[:])
+
+        def scale(i):
+            lo, hi = SHARED[i]
+            scaled = placed("scaled%d" % i, hi - lo, F32, scaled_at + slot * i)
+            for c in range(0, hi - lo, P):
+                block = (lo + c) // P
+                nc.scalar.activation(
+                    out=scaled[:, c : c + P],
+                    in_=forward[i][:, c : c + P],
+                    func=ACT.Copy,
+                    scale=gate_columns[:, block : block + 1],
                 )
-
-        def sum_turned(i):
-            lo, hi = TURNED[i]
-            summed = psum.tile([P, hi - lo], F32, name="summed", tag="bank%d" % (i % 2))
+            backward[i] = bank("backward", hi - lo, 3 + i % 5)
             for c in range(0, hi - lo, P):
-                for r, term in enumerate((first, second)):
-                    nc.tensor.matmul(
-                        summed[:, c : c + P],
-                        term[:, lo + c : lo + c + P],
-                        identity[:],
-                        start=(r == 0),
-                        stop=(r == 1),
-                        is_transpose=True,
-                    )
-            nc.scalar.copy(out=turned[:, lo:hi], in_=summed[:])
+                nc.tensor.transpose(backward[i][:, c : c + P], scaled[:, c : c + P], identity[:])
 
-        def turn_back(i):
-            lo, hi = TURNED[i]
-            back = psum.tile([P, hi - lo], F32, name="back", tag="bank%d" % (2 + i % 2))
-            for c in range(0, hi - lo, P):
-                nc.tensor.transpose(back[:, c : c + P], turned[:, lo + c : lo + c + P], identity[:])
-            nc.scalar.copy(out=total[:, lo:hi], in_=back[:])
-            nc.scalar.dma_start(out=out[:, lo:hi], in_=total[:, lo:hi])
-
-        def add(lo, hi):
-            nc.vector.tensor_tensor(out=total[:, lo:hi], in0=first[:, lo:hi], in1=second[:, lo:hi], op=ALU.add)
+        def add(lo, hi, one, other):
+            nc.vector.tensor_tensor(out=total[:, lo:hi], in0=one, in1=other, op=ALU.add)
             nc.sync.dma_start(out=out[:, lo:hi], in_=total[:, lo:hi])
 
-        for i, (lo, hi) in enumerate(TURNED):
-            fetch(lo, hi)
-            sum_turned(i)
-            if i > 0:
-                turn_back(i - 1)
-        turn_back(len(TURNED) - 1)
-        for i, (lo, hi) in enumerate(ADDED):
-            fetch(lo, hi)
-            if i > 0:
-                add(*ADDED[i - 1])
-        add(*ADDED[-1])
+        def add_shared(i):
+            add(*SHARED[i], backward[i][:], products[i][:])
+
+        own_first = gated("own_first", first_list, *OWN, strip_at + 2 * slot, first_gate(*OWN))
+        own_second = gated("own_second", second_list, *OWN, strip_at + 3 * slot, own_gate[:])
+        count = len(SHARED)
+        for i in range(count + 2):
+            if i >= 2:
+                scale(i - 2)
+                add_shared(i - 2)
+            if i == 1:
+                add(*OWN, own_first[:], own_second[:])
+            if i < count:
+                fetch(i)

@@ -43,6 +43,8 @@ BEHIND = {4: (0, 2), 6: (2, 4), 8: (4, 5), 12: (5, 7)}
 
 SHARED = [(0, 128), (128, 384), (384, 640), (640, 896), (896, 1152), (1152, 1408), (1408, 1664), (1664, 1792)]
 OWN = (1792, 2048)
+FETCHED = [(0, 2), (2, 4), (4, 6), (6, 8)]
+ADDED = [(0, 2), (2, 4), (4, 6), (6, 7), (7, 8)]
 GATED = [(0, 896), (896, 1792), (1792, 2048)]
 
 
@@ -250,10 +252,18 @@ def tile_moe_pkd_lin_relu2_kernel(
         gather_words(placed("words_pair", 2 * C, U32, last_place), E - 2, E, [1])
         gather_words(placed("words_rear", 2 * C, U32, 0), E - 2, E - 1, [2, 3])
         multiply_ready()
-        gather_words(placed("words_last", 2 * C, U32, QUARTER), E - 1, E, [2, 3])
+        words_last = placed("words_last", 2 * C, U32, QUARTER)
+        gather_words(words_last, E - 1, E, [2])
+        halves = [slice(0, C // 2), slice(C // 2, C)]
+        slot_words[E - 1, 3] = words_last[:, C : 2 * C]
+        for columns in halves:
+            lo = (E - 1) * C + columns.start
+            nc.vector.tensor_copy(
+                out=slot_words[E - 1, 3][:, columns],
+                in_=token_words[3][:].bitcast(U32).indirect(entries(slot_list, lo, lo + C // 2)),
+            )
 
         activate(7, 9, last_place + QUARTER)
-        halves = [slice(0, C // 2), slice(C // 2, C)]
         half_sums = [bank("half_sums", C // 2, e % BANKS) for e in (7, 8)]
         for a in range(PASSES):
             for half_sum, columns in zip(half_sums, halves):
@@ -277,8 +287,8 @@ def tile_moe_pkd_lin_relu2_kernel(
         strip_at = place_of(0)
         fetched_at = strip_at + 4 * slot
         scaled_at = place_of(2)
+        scaled_at2 = place_of(6)
         total = placed("total", T, F32, place_of(4))
-        products = {}
         forward = {}
         backward = {}
 
@@ -286,17 +296,16 @@ def tile_moe_pkd_lin_relu2_kernel(
             i = max(j for j, (start, end) in enumerate(GATED) if start <= lo)
             return first_gates[i][:, lo - GATED[i][0] : hi - GATED[i][0]]
 
-        def gated(name, listed, lo, hi, byte, factor):
-            product = placed(name, hi - lo, F32, byte)
+        def span(first, last):
+            return SHARED[first][0], SHARED[last - 1][1]
+
+        def gated(product, listed, lo, hi, factor):
             nc.vector.tensor_tensor(
-                out=product[:], in0=y[:].indirect(entries(listed, lo, hi)), in1=factor, op=ALU.mult
+                out=product, in0=y[:].indirect(entries(listed, lo, hi)), in1=factor, op=ALU.mult
             )
-            return product
 
         def fetch(i):
             lo, hi = SHARED[i]
-            byte = strip_at + slot * i if i < 2 else scaled_at + slot * (i - 2)
-            products[i] = gated("product%d" % i, first_list, lo, hi, byte, first_gate(lo, hi))
             fetched = placed("fetched%d" % i, hi - lo, F32, fetched_at + slot * (i % 2))
             nc.scalar.activation(out=fetched[:], in_=y[:].indirect(entries(second_list, lo, hi)), func=ACT.Copy)
             forward[i] = bank("forward", hi - lo, i % 3)
@@ -305,7 +314,9 @@ def tile_moe_pkd_lin_relu2_kernel(
 
         def scale(i):
             lo, hi = SHARED[i]
-            scaled = placed("scaled%d" % i, hi - lo, F32, scaled_at + slot * i)
+            f = max(j for j, (first, last) in enumerate(FETCHED) if first <= i)
+            byte = scaled_at2 + QUARTER * f + (lo - span(*FETCHED[f])[0]) * 4
+            scaled = placed("scaled%d" % i, hi - lo, F32, byte)
             for c in range(0, hi - lo, P):
                 block = (lo + c) // P
                 nc.scalar.activation(
@@ -314,25 +325,40 @@ def tile_moe_pkd_lin_relu2_kernel(
                     func=ACT.Copy,
                     scale=gate_columns[:, block : block + 1],
                 )
-            backward[i] = bank("backward", hi - lo, 3 + i % 5)
+            g = max(j for j, (first, last) in enumerate(ADDED) if first <= i)
+            start, end = span(*ADDED[g])
+            if g not in backward:
+                backward[g] = bank("backward", end - start, 3 + g)
             for c in range(0, hi - lo, P):
-                nc.tensor.transpose(backward[i][:, c : c + P], scaled[:, c : c + P], identity[:])
+                at = lo - start + c
+                nc.tensor.transpose(backward[g][:, at : at + P], scaled[:, c : c + P], identity[:])
 
         def add(lo, hi, one, other):
             nc.vector.tensor_tensor(out=total[:, lo:hi], in0=one, in1=other, op=ALU.add)
             nc.sync.dma_start(out=out[:, lo:hi], in_=total[:, lo:hi])
 
-        def add_shared(i):
-            add(*SHARED[i], backward[i][:], products[i][:])
-
-        own_first = gated("own_first", first_list, *OWN, strip_at + 2 * slot, first_gate(*OWN))
-        own_second = gated("own_second", second_list, *OWN, strip_at + 3 * slot, own_gate[:])
+        own_first = placed("own_first", C, F32, strip_at)
+        own_second = placed("own_second", C, F32, strip_at + slot)
+        gated(own_first[:], first_list, *OWN, first_gate(*OWN))
+        gated(own_second[:], second_list, *OWN, own_gate[:])
         count = len(SHARED)
+        product = {}
         for i in range(count + 2):
             if i >= 2:
                 scale(i - 2)
-                add_shared(i - 2)
+            for g, (first, last) in enumerate(ADDED):
+                if last == i - 1:
+                    lo, hi = span(first, last)
+                    f = max(j for j, (a, z) in enumerate(FETCHED) if a <= first)
+                    at = lo - span(*FETCHED[f])[0]
+                    add(lo, hi, backward[g][:], product[f][:, at : at + hi - lo])
             if i == 1:
                 add(*OWN, own_first[:], own_second[:])
             if i < count:
                 fetch(i)
+            for f, (first, last) in enumerate(FETCHED):
+                if i == (0, 1, 3, 5)[f]:
+                    lo, hi = span(first, last)
+                    byte = scaled_at + lo * 4 if f < 2 else scaled_at2 + QUARTER * (f - 2)
+                    product[f] = placed("product%d" % f, hi - lo, F32, byte)
+                    gated(product[f][:], first_list, lo, hi, first_gate(lo, hi))

@@ -41,11 +41,9 @@ BY_PASS = (5, 11)
 BY_TWO_PASSES = (11, 14)
 BEHIND = {4: (0, 2), 6: (2, 4), 8: (4, 5), 12: (5, 7)}
 
-SHARED = [(0, 128), (128, 384), (384, 640), (640, 896), (896, 1152), (1152, 1408), (1408, 1664), (1664, 1792)]
-OWN = (1792, 2048)
-FETCHED = [(0, 2), (2, 4), (4, 6), (6, 8)]
-ADDED = [(0, 2), (2, 4), (4, 6), (6, 7), (7, 8)]
-GATED = [(0, 896), (896, 1792), (1792, 2048)]
+SHARED = [(0, 256), (256, 512), (512, 768), (768, 1024), (1024, 1280), (1280, 1536), (1536, 1664)]
+OWN = (1664, 2048)
+GATED = [(0, 768), (768, 1664), (1664, 2048)]
 
 
 def tile_moe_pkd_lin_relu2_kernel(
@@ -285,10 +283,10 @@ def tile_moe_pkd_lin_relu2_kernel(
 
         slot = 4 * C
         strip_at = place_of(0)
-        fetched_at = strip_at + 4 * slot
+        fetched_at = strip_at + 6 * slot
         scaled_at = place_of(2)
-        scaled_at2 = place_of(6)
         total = placed("total", T, F32, place_of(4))
+        products = {}
         forward = {}
         backward = {}
 
@@ -296,16 +294,17 @@ def tile_moe_pkd_lin_relu2_kernel(
             i = max(j for j, (start, end) in enumerate(GATED) if start <= lo)
             return first_gates[i][:, lo - GATED[i][0] : hi - GATED[i][0]]
 
-        def span(first, last):
-            return SHARED[first][0], SHARED[last - 1][1]
-
-        def gated(product, listed, lo, hi, factor):
+        def gated(name, listed, lo, hi, byte, factor):
+            product = placed(name, hi - lo, F32, byte)
             nc.vector.tensor_tensor(
-                out=product, in0=y[:].indirect(entries(listed, lo, hi)), in1=factor, op=ALU.mult
+                out=product[:], in0=y[:].indirect(entries(listed, lo, hi)), in1=factor, op=ALU.mult
             )
+            return product
 
         def fetch(i):
             lo, hi = SHARED[i]
+            byte = strip_at + slot * i if i < 2 else scaled_at + slot * (i - 2)
+            products[i] = gated("product%d" % i, first_list, lo, hi, byte, first_gate(lo, hi))
             fetched = placed("fetched%d" % i, hi - lo, F32, fetched_at + slot * (i % 2))
             nc.scalar.activation(out=fetched[:], in_=y[:].indirect(entries(second_list, lo, hi)), func=ACT.Copy)
             forward[i] = bank("forward", hi - lo, i % 3)
@@ -314,9 +313,7 @@ def tile_moe_pkd_lin_relu2_kernel(
 
         def scale(i):
             lo, hi = SHARED[i]
-            f = max(j for j, (first, last) in enumerate(FETCHED) if first <= i)
-            byte = scaled_at2 + QUARTER * f + (lo - span(*FETCHED[f])[0]) * 4
-            scaled = placed("scaled%d" % i, hi - lo, F32, byte)
+            scaled = placed("scaled%d" % i, hi - lo, F32, scaled_at + slot * i)
             for c in range(0, hi - lo, P):
                 block = (lo + c) // P
                 nc.scalar.activation(
@@ -325,40 +322,25 @@ def tile_moe_pkd_lin_relu2_kernel(
                     func=ACT.Copy,
                     scale=gate_columns[:, block : block + 1],
                 )
-            g = max(j for j, (first, last) in enumerate(ADDED) if first <= i)
-            start, end = span(*ADDED[g])
-            if g not in backward:
-                backward[g] = bank("backward", end - start, 3 + g)
+            backward[i] = bank("backward", hi - lo, 3 + i % 5)
             for c in range(0, hi - lo, P):
-                at = lo - start + c
-                nc.tensor.transpose(backward[g][:, at : at + P], scaled[:, c : c + P], identity[:])
+                nc.tensor.transpose(backward[i][:, c : c + P], scaled[:, c : c + P], identity[:])
 
         def add(lo, hi, one, other):
             nc.vector.tensor_tensor(out=total[:, lo:hi], in0=one, in1=other, op=ALU.add)
             nc.sync.dma_start(out=out[:, lo:hi], in_=total[:, lo:hi])
 
-        own_first = placed("own_first", C, F32, strip_at)
-        own_second = placed("own_second", C, F32, strip_at + slot)
-        gated(own_first[:], first_list, *OWN, first_gate(*OWN))
-        gated(own_second[:], second_list, *OWN, own_gate[:])
+        def add_shared(i):
+            add(*SHARED[i], backward[i][:], products[i][:])
+
+        own_first = gated("own_first", first_list, *OWN, strip_at + 2 * slot, first_gate(*OWN))
+        own_second = gated("own_second", second_list, *OWN, strip_at + 4 * slot, own_gate[:])
         count = len(SHARED)
-        product = {}
         for i in range(count + 2):
             if i >= 2:
                 scale(i - 2)
-            for g, (first, last) in enumerate(ADDED):
-                if last == i - 1:
-                    lo, hi = span(first, last)
-                    f = max(j for j, (a, z) in enumerate(FETCHED) if a <= first)
-                    at = lo - span(*FETCHED[f])[0]
-                    add(lo, hi, backward[g][:], product[f][:, at : at + hi - lo])
+                add_shared(i - 2)
             if i == 1:
                 add(*OWN, own_first[:], own_second[:])
             if i < count:
                 fetch(i)
-            for f, (first, last) in enumerate(FETCHED):
-                if i == (0, 1, 3, 5)[f]:
-                    lo, hi = span(first, last)
-                    byte = scaled_at + lo * 4 if f < 2 else scaled_at2 + QUARTER * (f - 2)
-                    product[f] = placed("product%d" % f, hi - lo, F32, byte)
-                    gated(product[f][:], first_list, lo, hi, first_gate(lo, hi))

@@ -41,9 +41,12 @@ BY_PASS = (5, 11)
 BY_TWO_PASSES = (11, 14)
 BEHIND = {4: (0, 2), 6: (2, 4), 8: (4, 5), 12: (5, 7)}
 
-SHARED = [(0, 256), (256, 512), (512, 768), (768, 1024), (1024, 1280), (1280, 1536), (1536, 1664)]
-OWN = (1664, 2048)
-GATED = [(0, 768), (768, 1664), (1664, 2048)]
+OWN = (0, 256)
+SHARED = [(256, 512), (512, 1024), (1024, 1408), (1408, 1664), (1664, 1920), (1920, 2048)]
+SHARED_BLOCKS = (T - OWN[1]) // P
+LAG = 2
+FORWARD_BANKS = 3
+GATED = [(0, 1024), (1024, 2048)]
 
 
 def tile_moe_pkd_lin_relu2_kernel(
@@ -66,7 +69,7 @@ def tile_moe_pkd_lin_relu2_kernel(
         y = keep.tile([P, SLOTS], F32, name="y")
         identity = keep.tile([P, P], F32, name="identity")
         gate_rows = keep.tile([P, P], F32, name="gate_rows")
-        gate_columns = keep.tile([P, T // P], F32, name="gate_columns")
+        gate_columns = keep.tile([P, SHARED_BLOCKS], F32, name="gate_columns")
         first_gates = [keep.tile([P, hi - lo], F32, name="first_gate%d" % lo) for lo, hi in GATED]
         own_gate = keep.tile([P, OWN[1] - OWN[0]], F32, name="own_gate")
         nc.gpsimd.memset(token_scales[2 * QUADRANT : P, :].bitcast(I32), 0)
@@ -194,7 +197,9 @@ def tile_moe_pkd_lin_relu2_kernel(
         load_weights(1)
         load_weights(2)
         nc.sync.dma_start(out=bias[:], in_=b)
-        nc.sync.dma_start(out=gate_rows[0 : T // P, :], in_=gate[1, 0].rearrange("(c t) -> c t", t=P))
+        nc.sync.dma_start(
+            out=gate_rows[0:SHARED_BLOCKS, :], in_=gate[1, 0, OWN[1] : T].rearrange("(c t) -> c t", t=P)
+        )
         for e in range(3, PLACES):
             load_weights(e)
         nc.sync.dma_start(first_list[:], pos1)
@@ -202,7 +207,7 @@ def tile_moe_pkd_lin_relu2_kernel(
 
         turned_gate = bank("turned_gate", P, BANKS - 1)
         nc.tensor.transpose(turned_gate[:], gate_rows[:], identity[:])
-        nc.scalar.copy(out=gate_columns[:], in_=turned_gate[:, 0 : T // P])
+        nc.scalar.copy(out=gate_columns[:], in_=turned_gate[:, 0:SHARED_BLOCKS])
 
         for lo in range(0, SLOTS, RUN):
             hi = min(lo + RUN, SLOTS)
@@ -224,7 +229,7 @@ def tile_moe_pkd_lin_relu2_kernel(
                 load_weights(PLACES + run)
             if PLACES + run == E - 1:
                 nc.sync.dma_start(out=own_gate[:], in_=gate[1, :, OWN[0] : OWN[1]])
-                for i in (2, 0, 1):
+                for i in range(len(GATED)):
                     nc.sync.dma_start(out=first_gates[i][:], in_=gate[0, :, GATED[i][0] : GATED[i][1]])
             if even in BEHIND:
                 activate(*BEHIND[even], place_of(even) + 3 * QUARTER)
@@ -253,12 +258,12 @@ def tile_moe_pkd_lin_relu2_kernel(
         words_last = placed("words_last", 2 * C, U32, QUARTER)
         gather_words(words_last, E - 1, E, [2])
         halves = [slice(0, C // 2), slice(C // 2, C)]
-        slot_words[E - 1, 3] = words_last[:, C : 2 * C]
+        slot_words[E - 1, PASSES - 1] = words_last[:, C : 2 * C]
         for columns in halves:
             lo = (E - 1) * C + columns.start
             nc.vector.tensor_copy(
-                out=slot_words[E - 1, 3][:, columns],
-                in_=token_words[3][:].bitcast(U32).indirect(entries(slot_list, lo, lo + C // 2)),
+                out=slot_words[E - 1, PASSES - 1][:, columns],
+                in_=token_words[PASSES - 1][:].bitcast(U32).indirect(entries(slot_list, lo, lo + C // 2)),
             )
 
         activate(7, 9, last_place + QUARTER)
@@ -274,16 +279,25 @@ def tile_moe_pkd_lin_relu2_kernel(
         rear = keep.tile([P, C // 2], F32, name="rear")
         y_last = y[:, (E - 1) * C : E * C]
         last_bias = bias[:, E - 1 : E]
-        nc.scalar.activation(out=front[:], in_=half_sums[0][:], func=ACT.Relu, bias=last_bias)
-        nc.scalar.activation(out=y_last[:, halves[0]], in_=front[:], func=ACT.Square)
-        nc.vector.tensor_scalar(
-            out=rear[:], in0=half_sums[1][:], scalar1=last_bias, scalar2=0.0, op0=ALU.add, op1=ALU.max
-        )
-        nc.vector.tensor_tensor(out=y_last[:, halves[1]], in0=rear[:], in1=rear[:], op=ALU.mult)
+        parts = [slice(0, C // 4), slice(C // 4, C // 2)]
+        for part in parts:
+            nc.scalar.activation(out=front[:, part], in_=half_sums[0][:, part], func=ACT.Relu, bias=last_bias)
+            nc.vector.tensor_scalar(
+                out=rear[:, part],
+                in0=half_sums[1][:, part],
+                scalar1=last_bias,
+                scalar2=0.0,
+                op0=ALU.add,
+                op1=ALU.max,
+            )
+        for part in parts:
+            nc.scalar.activation(out=y_last[:, halves[0]][:, part], in_=front[:, part], func=ACT.Square)
+            nc.vector.tensor_tensor(
+                out=y_last[:, halves[1]][:, part], in0=rear[:, part], in1=rear[:, part], op=ALU.mult
+            )
 
-        slot = 4 * C
-        strip_at = place_of(0)
-        fetched_at = strip_at + 6 * slot
+        products_at = place_of(0)
+        fetched_at = place_of(1)
         scaled_at = place_of(2)
         total = placed("total", T, F32, place_of(4))
         products = {}
@@ -303,26 +317,27 @@ def tile_moe_pkd_lin_relu2_kernel(
 
         def fetch(i):
             lo, hi = SHARED[i]
-            byte = strip_at + slot * i if i < 2 else scaled_at + slot * (i - 2)
-            products[i] = gated("product%d" % i, first_list, lo, hi, byte, first_gate(lo, hi))
-            fetched = placed("fetched%d" % i, hi - lo, F32, fetched_at + slot * (i % 2))
+            if i > 0:
+                byte = products_at + QUARTER * i if i < LAG else scaled_at + QUARTER * (i - LAG)
+                products[i] = gated("product%d" % i, first_list, lo, hi, byte, first_gate(lo, hi))[:]
+            fetched = placed("fetched%d" % i, hi - lo, F32, fetched_at + QUARTER * (i % LAG))
             nc.scalar.activation(out=fetched[:], in_=y[:].indirect(entries(second_list, lo, hi)), func=ACT.Copy)
-            forward[i] = bank("forward", hi - lo, i % 3)
+            forward[i] = bank("forward", hi - lo, i % FORWARD_BANKS)
             for c in range(0, hi - lo, P):
                 nc.tensor.transpose(forward[i][:, c : c + P], fetched[:, c : c + P], identity[:])
 
         def scale(i):
             lo, hi = SHARED[i]
-            scaled = placed("scaled%d" % i, hi - lo, F32, scaled_at + slot * i)
+            scaled = placed("scaled%d" % i, hi - lo, F32, scaled_at + QUARTER * i)
             for c in range(0, hi - lo, P):
-                block = (lo + c) // P
+                block = (lo + c - OWN[1]) // P
                 nc.scalar.activation(
                     out=scaled[:, c : c + P],
                     in_=forward[i][:, c : c + P],
                     func=ACT.Copy,
                     scale=gate_columns[:, block : block + 1],
                 )
-            backward[i] = bank("backward", hi - lo, 3 + i % 5)
+            backward[i] = bank("backward", hi - lo, FORWARD_BANKS + i % (BANKS - FORWARD_BANKS))
             for c in range(0, hi - lo, P):
                 nc.tensor.transpose(backward[i][:, c : c + P], scaled[:, c : c + P], identity[:])
 
@@ -330,17 +345,17 @@ def tile_moe_pkd_lin_relu2_kernel(
             nc.vector.tensor_tensor(out=total[:, lo:hi], in0=one, in1=other, op=ALU.add)
             nc.sync.dma_start(out=out[:, lo:hi], in_=total[:, lo:hi])
 
-        def add_shared(i):
-            add(*SHARED[i], backward[i][:], products[i][:])
-
-        own_first = gated("own_first", first_list, *OWN, strip_at + 2 * slot, first_gate(*OWN))
-        own_second = gated("own_second", second_list, *OWN, strip_at + 4 * slot, own_gate[:])
+        lead = (OWN[0], SHARED[0][1])
+        leading = gated("leading", first_list, *lead, products_at, first_gate(*lead))
+        own_first = leading[:, 0 : OWN[1]]
+        products[0] = leading[:, OWN[1] : lead[1]]
+        own_second = gated("own_second", second_list, *OWN, products_at + 3 * QUARTER, own_gate[:])
         count = len(SHARED)
-        for i in range(count + 2):
-            if i >= 2:
-                scale(i - 2)
-                add_shared(i - 2)
-            if i == 1:
-                add(*OWN, own_first[:], own_second[:])
+        for i in range(count + LAG):
+            if i >= LAG:
+                scale(i - LAG)
+                add(*SHARED[i - LAG], backward[i - LAG][:], products[i - LAG])
+            if i == LAG - 1:
+                add(*OWN, own_first, own_second[:])
             if i < count:
                 fetch(i)

@@ -37,6 +37,7 @@ QUARTER = PLACE // 4
 
 RUN = 1536
 HEAD = 5
+EARLY = 2 * RUN
 BY_PASS = (5, 11)
 BY_TWO_PASSES = (11, 14)
 BEHIND = {4: (0, 2), 6: (2, 4), 8: (4, 5), 12: (5, 7)}
@@ -63,7 +64,10 @@ def tile_moe_pkd_lin_relu2_kernel(
         first_list = keep.tile([P, T // STRIPE], U16, name="first_list")
         second_list = keep.tile([P, T // STRIPE], U16, name="second_list")
         token_scales = keep.tile([P, T], U8, name="token_scales", align_bytes=64)
-        slot_scales = keep.tile([P, SLOTS], U8, name="slot_scales", align_bytes=64)
+        slot_scales = keep.tile([P, EARLY], U8, name="slot_scales", align_bytes=64)
+        token_rows = keep.tile([P, T], U8, name="token_rows", align_bytes=64)
+        late_rows = keep.tile([P, SLOTS - EARLY], U8, name="late_rows", align_bytes=64)
+        late_scales = keep.tile([P, SLOTS - EARLY], U8, name="late_scales", align_bytes=64)
         token_words = [keep.tile([P, T], I32, name="token_words%d" % a, align_bytes=64) for a in range(PASSES)]
         bias = keep.tile([P, E], F32, name="bias")
         y = keep.tile([P, SLOTS], F32, name="y")
@@ -75,6 +79,9 @@ def tile_moe_pkd_lin_relu2_kernel(
         nc.gpsimd.memset(token_scales[2 * QUADRANT : P, :].bitcast(I32), 0)
         nc.gpsimd.memset(gate_rows[:], 0.0)
         make_identity(nc, identity[:])
+        nc.gpsimd.memset(late_scales[:].bitcast(I32), 0)
+        nc.vector.memset(token_rows[0:QUADRANT, :].bitcast(I32), 0)
+        nc.vector.memset(token_rows[P - QUADRANT : P, :].bitcast(I32), 0)
 
         raw = {}
         w_codes = {}
@@ -104,6 +111,13 @@ def tile_moe_pkd_lin_relu2_kernel(
             nc.sync.dma_start(
                 out=token_scales[QUADRANT * q : QUADRANT * q + LIVE, :].bitcast(I32),
                 in_=x_scales[:, 4 * q : 4 * q + 4, :].bitcast(I32),
+            )
+
+        def move_scales(queue, a, q):
+            row = QUADRANT + LIVE * a + 4 * q
+            queue.dma_start(
+                out=late_scales[QUADRANT * q + 4 * a : QUADRANT * q + 4 * a + 4, :].bitcast(I32),
+                in_=late_rows[row : row + 4, :].bitcast(I32),
             )
 
         def load_weights(e):
@@ -153,13 +167,18 @@ def tile_moe_pkd_lin_relu2_kernel(
                 for e in range(lo, hi):
                     slot_words[e, a] = dst[:, (e - lo) * C : (e - lo + 1) * C]
 
+        def scales_of(e):
+            if e * C < EARLY:
+                return slot_scales[:, e * C : (e + 1) * C]
+            return late_scales[:, e * C - EARLY : (e + 1) * C - EARLY]
+
         def multiply_pass(dst, e, a, columns, start, stop):
             nc.tensor.matmul_mx(
                 out=dst,
                 lhsT=w_codes[e][:, a * N : (a + 1) * N].bitcast(FP8X4),
                 lhsT_scale=w_scales[e][:, a * N : (a + 1) * N],
                 rhs=slot_words[e, a][:, columns].bitcast(FP8X4),
-                rhs_scale=slot_scales[4 * a : P, e * C : (e + 1) * C][:, columns],
+                rhs_scale=scales_of(e)[4 * a : P, columns],
                 start=start,
                 stop=stop,
             )
@@ -183,9 +202,13 @@ def tile_moe_pkd_lin_relu2_kernel(
                 )
             nc.scalar.activation(out=y[:, lo * C : hi * C], in_=positive[:], func=ACT.Square)
 
+        nc.sync.dma_start(
+            out=token_rows[QUADRANT : P - QUADRANT, :].bitcast(I32),
+            in_=x_scales.rearrange("a f t -> (a f) t").bitcast(I32),
+        )
+        nc.sync.dma_start(slot_list[:], offs)
         load_scales(0)
         load_scales(1)
-        nc.sync.dma_start(slot_list[:], offs)
         for q in range(2):
             unused = token_scales[QUADRANT * q + LIVE : QUADRANT * (q + 1), :]
             nc.sync.dma_start(out=unused.bitcast(I32), in_=x_scales[q].bitcast(I32))
@@ -200,8 +223,14 @@ def tile_moe_pkd_lin_relu2_kernel(
         nc.sync.dma_start(
             out=gate_rows[0:SHARED_BLOCKS, :], in_=gate[1, 0, OWN[1] : T].rearrange("(c t) -> c t", t=P)
         )
+        nc.vector.tensor_copy(out=late_rows[:], in_=token_rows[:].indirect(entries(slot_list, EARLY, SLOTS)))
+        for q in range(2):
+            for a in range(PASSES):
+                move_scales(nc.gpsimd, a, q)
         for e in range(3, PLACES):
             load_weights(e)
+            if e < 11:
+                move_scales(nc.sync, (e - 3) % PASSES, 2 + (e - 3) // PASSES)
         nc.sync.dma_start(first_list[:], pos1)
         nc.sync.dma_start(second_list[:], pos2)
 
@@ -209,8 +238,8 @@ def tile_moe_pkd_lin_relu2_kernel(
         nc.tensor.transpose(turned_gate[:], gate_rows[:], identity[:])
         nc.scalar.copy(out=gate_columns[:], in_=turned_gate[:, 0:SHARED_BLOCKS])
 
-        for lo in range(0, SLOTS, RUN):
-            hi = min(lo + RUN, SLOTS)
+        for lo in range(0, EARLY, RUN):
+            hi = lo + RUN
             nc.vector.tensor_copy(
                 out=slot_scales[:, lo:hi], in_=token_scales[:].indirect(entries(slot_list, lo, hi))
             )

@@ -229,8 +229,6 @@ def tile_moe_pkd_lin_relu2_kernel(
                 move_scales(nc.gpsimd, a, q)
         for e in range(3, PLACES):
             load_weights(e)
-            if e < 11:
-                move_scales(nc.sync, (e - 3) % PASSES, 2 + (e - 3) // PASSES)
         nc.sync.dma_start(first_list[:], pos1)
         nc.sync.dma_start(second_list[:], pos2)
 
@@ -257,6 +255,9 @@ def tile_moe_pkd_lin_relu2_kernel(
             if PLACES + run < E:
                 load_weights(PLACES + run)
             if PLACES + run == E - 1:
+                for q in (2, 3):
+                    for a in range(PASSES):
+                        move_scales(nc.sync, a, q)
                 nc.sync.dma_start(out=own_gate[:], in_=gate[1, :, OWN[0] : OWN[1]])
                 for i in range(len(GATED)):
                     nc.sync.dma_start(out=first_gates[i][:], in_=gate[0, :, GATED[i][0] : GATED[i][1]])

@@ -304,7 +304,7 @@ def tile_moe_pkd_lin_relu2_kernel(
         activate(9, 11, last_place + 2 * QUARTER)
         activate(11, 13, last_place + 3 * QUARTER)
         activate(13, 14, last_place + QUARTER)
-        activate(14, 15, last_place + QUARTER)
+        activate(14, 15, last_place + 2 * QUARTER)
         front = placed("front", C // 2, F32, last_place + QUARTER)
         rear = keep.tile([P, C // 2], F32, name="rear")
         y_last = y[:, (E - 1) * C : E * C]

@@ -113,9 +113,9 @@ def tile_moe_pkd_lin_relu2_kernel(
                 in_=x_scales[:, 4 * q : 4 * q + 4, :].bitcast(I32),
             )
 
-        def move_scales(queue, a, q):
+        def move_scales(a, q):
             row = QUADRANT + LIVE * a + 4 * q
-            queue.dma_start(
+            nc.sync.dma_start(
                 out=late_scales[QUADRANT * q + 4 * a : QUADRANT * q + 4 * a + 4, :].bitcast(I32),
                 in_=late_rows[row : row + 4, :].bitcast(I32),
             )
@@ -224,11 +224,10 @@ def tile_moe_pkd_lin_relu2_kernel(
             out=gate_rows[0:SHARED_BLOCKS, :], in_=gate[1, 0, OWN[1] : T].rearrange("(c t) -> c t", t=P)
         )
         nc.vector.tensor_copy(out=late_rows[:], in_=token_rows[:].indirect(entries(slot_list, EARLY, SLOTS)))
-        for q in range(2):
-            for a in range(PASSES):
-                move_scales(nc.gpsimd, a, q)
         for e in range(3, PLACES):
             load_weights(e)
+            if e - 3 < 2 * PASSES:
+                move_scales((e - 3) % PASSES, (e - 3) // PASSES)
         nc.sync.dma_start(first_list[:], pos1)
         nc.sync.dma_start(second_list[:], pos2)
 
@@ -257,7 +256,7 @@ def tile_moe_pkd_lin_relu2_kernel(
             if PLACES + run == E - 1:
                 for q in (2, 3):
                     for a in range(PASSES):
-                        move_scales(nc.sync, a, q)
+                        move_scales(a, q)
                 nc.sync.dma_start(out=own_gate[:], in_=gate[1, :, OWN[0] : OWN[1]])
                 for i in range(len(GATED)):
                     nc.sync.dma_start(out=first_gates[i][:], in_=gate[0, :, GATED[i][0] : GATED[i][1]])

from contextlib import ExitStack

import concourse.mybir as mybir
from concourse.masks import make_identity

K, T, E, C, N = 2048, 2048, 16, 256, 128
SLOTS = E * C
P = 128
PACK = 4
PASSES = K // (P * PACK)
FLOPS = 2 * K * SLOTS * N

F32 = mybir.dt.float32
BF16 = mybir.dt.bfloat16
I32 = mybir.dt.int32
U32 = mybir.dt.uint32
U16 = mybir.dt.uint16
U8 = mybir.dt.uint8
FP8X4 = mybir.dt.float8_e4m3fn_x4
ACT = mybir.ActivationFunctionType
ALU = mybir.AluOpType

STRIPE = 16
QUADRANT = 32
LIVE = PASSES * 4
BANKS = 8
WORDS = PASSES * N
VALUES = WORDS * PACK
LINE = 4

ROOM = VALUES * 2
ROOMS = E // 2
PLACE = VALUES * 4
PLACES = 12
PLACES_AT = ROOMS * ROOM
QUARTER = PLACE // 4

RUN = 1536
HEAD = 5
EARLY = 2 * RUN
BY_PASS = (5, 11)
BY_TWO_PASSES = (11, 14)
BEHIND = {4: (0, 2), 6: (2, 4), 8: (4, 5), 12: (5, 7)}

OWN = (0, 256)
SHARED = [(256, 512), (512, 1024), (1024, 1408), (1408, 1664), (1664, 1920), (1920, 2048)]
SHARED_BLOCKS = (T - OWN[1]) // P
LAG = 2
FORWARD_BANKS = 3
GATED = [(0, 1024), (1024, 2048)]


def tile_moe_pkd_lin_relu2_kernel(
    tc, x_words, x_scales, w, b, gate, offs, pos1, pos2, out
):
    nc = tc.nc
    with ExitStack() as ctx:
        keep = ctx.enter_context(tc.tile_pool(name="keep", bufs=1))
        reused = ctx.enter_context(tc.tile_pool(name="reused", bufs=1))
        pairs = ctx.enter_context(tc.tile_pool(name="pairs", bufs=3))
        psum = ctx.enter_context(tc.psum_pool(name="psum", bufs=1))

        slot_list = keep.tile([P, SLOTS // STRIPE], U16, name="slot_list")
        first_list = keep.tile([P, T // STRIPE], U16, name="first_list")
        second_list = keep.tile([P, T // STRIPE], U16, name="second_list")
        token_scales = keep.tile([P, T], U8, name="token_scales", align_bytes=64)
        slot_scales = keep.tile([P, EARLY], U8, name="slot_scales", align_bytes=64)
        token_rows = keep.tile([P, T], U8, name="token_rows", align_bytes=64)
        late_rows = keep.tile([P, SLOTS - EARLY], U8, name="late_rows", align_bytes=64)
        late_scales = keep.tile([P, SLOTS - EARLY], U8, name="late_scales", align_bytes=64)
        token_words = [keep.tile([P, T], I32, name="token_words%d" % a, align_bytes=64) for a in range(PASSES)]
        bias = keep.tile([P, E], F32, name="bias")
        y = keep.tile([P, SLOTS], F32, name="y")
        identity = keep.tile([P, P], F32, name="identity")
        gate_rows = keep.tile([P, P], F32, name="gate_rows")
        gate_columns = keep.tile([P, SHARED_BLOCKS], F32, name="gate_columns")
        first_gates = [keep.tile([P, hi - lo], F32, name="first_gate%d" % lo) for lo, hi in GATED]
        own_gate = keep.tile([P, OWN[1] - OWN[0]], F32, name="own_gate")
        nc.gpsimd.memset(token_scales[2 * QUADRANT : P, :].bitcast(I32), 0)
        nc.gpsimd.memset(gate_rows[:], 0.0)
        make_identity(nc, identity[:])
        nc.gpsimd.memset(late_scales[:].bitcast(I32), 0)
        nc.vector.memset(token_rows[0:QUADRANT, :].bitcast(I32), 0)
        nc.vector.memset(token_rows[P - QUADRANT : P, :].bitcast(I32), 0)

        raw = {}
        w_codes = {}
        w_scales = {}
        slot_words = {}
        sums = {}

        def placed(name, columns, dtype, byte):
            return reused.tile([P, columns], dtype, name=name, offset=byte, align_bytes=64)

        def place_of(e):
            return PLACES_AT + PLACE * (e if e < PLACES else 2 * (e - PLACES) + 1)

        def bank(name, columns, i):
            return psum.tile([P, columns], F32, name=name, tag="bank%d" % i)

        def entries(listed, lo, hi):
            return listed[:, lo // STRIPE : hi // STRIPE]

        rooms = placed("rooms", ROOMS * VALUES, BF16, 0)

        def rounded(e, count=1):
            room = e // 2 if e < E - 1 else (E - 3) // 2 - 1
            return rooms[:, room * VALUES : (room + count) * VALUES]

        def load_scales(q):
            nc.sync.dma_start(
                out=token_scales[QUADRANT * q : QUADRANT * q + LIVE, :].bitcast(I32),
                in_=x_scales[:, 4 * q : 4 * q + 4, :].bitcast(I32),
            )

        def move_scales(a, q):
            row = QUADRANT + LIVE * a + 4 * q
            nc.sync.dma_start(
                out=late_scales[QUADRANT * q + 4 * a : QUADRANT * q + 4 * a + 4, :].bitcast(I32),
                in_=late_rows[row : row + 4, :].bitcast(I32),
            )

        def load_weights(e):
            raw[e] = placed("raw%d" % e, VALUES, F32, place_of(e))
            nc.sync.dma_start(
                out=raw[e][:].rearrange("p (a m) -> p a m", a=PASSES),
                in_=w[e].rearrange("(a p j) n -> p a (j n)", a=PASSES, j=PACK),
            )

        def round_on_scalar(e):
            nc.scalar.copy(
                out=rounded(e).rearrange("p (a c i j) -> p a c j i", a=PASSES, i=LINE, j=PACK),
                in_=raw[e][:].rearrange("p (a j c i) -> p a c j i", a=PASSES, j=PACK, i=LINE),
            )

        def round_on_gpsimd(e):
            nc.gpsimd.tensor_scalar(
                out=rounded(e).rearrange("p (a n j) -> p a n j", a=PASSES, j=PACK),
                in0=raw[e][:].rearrange("p (a j n) -> p a n j", a=PASSES, j=PACK),
                scalar1=1.0,
                scalar2=0.0,
                op0=ALU.mult,
                op1=ALU.add,
            )

        def quantise(*experts):
            if len(experts) == 1:
                codes = keep.tile([P, WORDS], U32, name="lone_codes", align_bytes=64)
                scales = keep.tile([P, WORDS], U8, name="lone_scales", align_bytes=64)
            else:
                codes = pairs.tile([P, 2 * WORDS], U32, name="codes", align_bytes=64)
                scales = pairs.tile([P, 2 * WORDS], U8, name="scales", align_bytes=64)
            for i, e in enumerate(experts):
                w_codes[e] = codes[:, i * WORDS : (i + 1) * WORDS]
                w_scales[e] = scales[:, i * WORDS : (i + 1) * WORDS]
            nc.vector.quantize_mx(
                out=codes[:].bitcast(FP8X4), scales=scales[:], in_=rounded(experts[0], len(experts))
            )

        def gather_words(words, lo, hi, passes):
            width = (hi - lo) * C
            for i, a in enumerate(passes):
                dst = words[:, i * width : (i + 1) * width]
                nc.vector.tensor_copy(
                    out=dst, in_=token_words[a][:].bitcast(U32).indirect(entries(slot_list, lo * C, hi * C))
                )
                for e in range(lo, hi):
                    slot_words[e, a] = dst[:, (e - lo) * C : (e - lo + 1) * C]

        def scales_of(e):
            if e * C < EARLY:
                return slot_scales[:, e * C : (e + 1) * C]
            return late_scales[:, e * C - EARLY : (e + 1) * C - EARLY]

        def multiply_pass(dst, e, a, columns, start, stop):
            nc.tensor.matmul_mx(
                out=dst,
                lhsT=w_codes[e][:, a * N : (a + 1) * N].bitcast(FP8X4),
                lhsT_scale=w_scales[e][:, a * N : (a + 1) * N],
                rhs=slot_words[e, a][:, columns].bitcast(FP8X4),
                rhs_scale=scales_of(e)[4 * a : P, columns],
                start=start,
                stop=stop,
            )

        def multiply_ready():
            ready = [e for e in w_codes if e not in sums and (e, PASSES - 1) in slot_words]
            for e in ready:
                sums[e] = bank("sums", C, e % BANKS)
                order = range(PASSES - 1, -1, -1) if e < E - 2 else range(PASSES)
                for a in order:
                    multiply_pass(sums[e][:], e, a, slice(0, C), a == order[0], a == order[-1])

        def activate(lo, hi, byte):
            positive = placed("positive%d" % lo, (hi - lo) * C, F32, byte)
            for e in range(lo, hi):
                nc.scalar.activation(
                    out=positive[:, (e - lo) * C : (e - lo + 1) * C],
                    in_=sums[e][:],
                    func=ACT.Relu,
                    bias=bias[:, e : e + 1],
                )
            nc.scalar.activation(out=y[:, lo * C : hi * C], in_=positive[:], func=ACT.Square)

        nc.sync.dma_start(
            out=token_rows[QUADRANT : P - QUADRANT, :].bitcast(I32),
            in_=x_scales.rearrange("a f t -> (a f) t").bitcast(I32),
        )
        nc.sync.dma_start(slot_list[:], offs)
        load_scales(0)
        load_scales(1)
        for q in range(2):
            unused = token_scales[QUADRANT * q + LIVE : QUADRANT * (q + 1), :]
            nc.sync.dma_start(out=unused.bitcast(I32), in_=x_scales[q].bitcast(I32))
        load_scales(2)
        load_scales(3)
        load_weights(0)
        for a in range(PASSES):
            nc.sync.dma_start(out=token_words[a][:], in_=x_words[a].rearrange("p t r -> p (t r)").bitcast(I32))
        load_weights(1)
        load_weights(2)
        nc.sync.dma_start(out=bias[:], in_=b)
        nc.sync.dma_start(
            out=gate_rows[0:SHARED_BLOCKS, :], in_=gate[1, 0, OWN[1] : T].rearrange("(c t) -> c t", t=P)
        )
        nc.vector.tensor_copy(out=late_rows[:], in_=token_rows[:].indirect(entries(slot_list, EARLY, SLOTS)))
        for e in range(3, PLACES):
            load_weights(e)
            if e - 3 < 2 * PASSES:
                move_scales((e - 3) % PASSES, (e - 3) // PASSES)
        nc.sync.dma_start(first_list[:], pos1)
        nc.sync.dma_start(second_list[:], pos2)

        turned_gate = bank("turned_gate", P, BANKS - 1)
        nc.tensor.transpose(turned_gate[:], gate_rows[:], identity[:])
        nc.scalar.copy(out=gate_columns[:], in_=turned_gate[:, 0:SHARED_BLOCKS])

        for lo in range(0, EARLY, RUN):
            hi = lo + RUN
            nc.vector.tensor_copy(
                out=slot_scales[:, lo:hi], in_=token_scales[:].indirect(entries(slot_list, lo, hi))
            )
        for a in range(PASSES):
            head_words = keep.tile([P, HEAD * C], U32, name="head_words%d" % a, align_bytes=64)
            gather_words(head_words, 0, HEAD, [a])
        round_on_scalar(0)
        quantise(0)
        multiply_ready()

        for run, odd in enumerate(range(1, E - 1, 2)):
            even = odd + 1
            round_on_gpsimd(odd)
            round_on_scalar(even)
            if PLACES + run < E:
                load_weights(PLACES + run)
            if PLACES + run == E - 1:
                for q in (2, 3):
                    for a in range(PASSES):
                        move_scales(a, q)
                nc.sync.dma_start(out=own_gate[:], in_=gate[1, :, OWN[0] : OWN[1]])
                for i in range(len(GATED)):
                    nc.sync.dma_start(out=first_gates[i][:], in_=gate[0, :, GATED[i][0] : GATED[i][1]])
            if even in BEHIND:
                activate(*BEHIND[even], place_of(even) + 3 * QUARTER)
            if even < E - 2:
                quantise(odd, even)
            else:
                quantise(even)
            multiply_ready()
            if run < PASSES:
                group, passes = BY_PASS, [run]
            elif even < E - 2:
                group, passes = BY_TWO_PASSES, [2 * (run - PASSES), 2 * (run - PASSES) + 1]
            else:
                group, passes = (E - 2, E), [0]
            words = placed("words%d" % run, len(passes) * (group[1] - group[0]) * C, U32, place_of(even))
            gather_words(words, *group, passes)
            multiply_ready()

        round_on_scalar(E - 1)
        quantise(E - 1, E - 3)
        multiply_ready()
        last_place = place_of(E - 1)
        gather_words(placed("words_pair", 2 * C, U32, last_place), E - 2, E, [1])
        gather_words(placed("words_rear", 2 * C, U32, 0), E - 2, E - 1, [2, 3])
        multiply_ready()
        words_last = placed("words_last", 2 * C, U32, QUARTER)
        gather_words(words_last, E - 1, E, [2])
        halves = [slice(0, C // 2), slice(C // 2, C)]
        slot_words[E - 1, PASSES - 1] = words_last[:, C : 2 * C]
        for columns in halves:
            lo = (E - 1) * C + columns.start
            nc.vector.tensor_copy(
                out=slot_words[E - 1, PASSES - 1][:, columns],
                in_=token_words[PASSES - 1][:].bitcast(U32).indirect(entries(slot_list, lo, lo + C // 2)),
            )

        activate(7, 9, last_place + QUARTER)
        half_sums = [bank("half_sums", C // 2, e % BANKS) for e in (7, 8)]
        for a in range(PASSES):
            for half_sum, columns in zip(half_sums, halves):
                multiply_pass(half_sum[:], E - 1, a, columns, a == 0, a == PASSES - 1)
        activate(9, 11, last_place + 2 * QUARTER)
        activate(11, 13, last_place + 3 * QUARTER)
        activate(13, 14, last_place + QUARTER)
        activate(14, 15, last_place + 2 * QUARTER)
        front = placed("front", C // 2, F32, last_place + QUARTER)
        rear = keep.tile([P, C // 2], F32, name="rear")
        y_last = y[:, (E - 1) * C : E * C]
        last_bias = bias[:, E - 1 : E]
        parts = [slice(0, C // 4), slice(C // 4, C // 2)]
        for part in parts:
            nc.scalar.activation(out=front[:, part], in_=half_sums[0][:, part], func=ACT.Relu, bias=last_bias)
            nc.vector.tensor_scalar(
                out=rear[:, part],
                in0=half_sums[1][:, part],
                scalar1=last_bias,
                scalar2=0.0,
                op0=ALU.add,
                op1=ALU.max,
            )
        for part in parts:
            nc.scalar.activation(out=y_last[:, halves[0]][:, part], in_=front[:, part], func=ACT.Square)
            nc.vector.tensor_tensor(
                out=y_last[:, halves[1]][:, part], in0=rear[:, part], in1=rear[:, part], op=ALU.mult
            )

        products_at = place_of(0)
        fetched_at = place_of(1)
        scaled_at = place_of(2)
        total = placed("total", T, F32, place_of(4))
        products = {}
        forward = {}
        backward = {}

        def first_gate(lo, hi):
            i = max(j for j, (start, end) in enumerate(GATED) if start <= lo)
            return first_gates[i][:, lo - GATED[i][0] : hi - GATED[i][0]]

        def gated(name, listed, lo, hi, byte, factor):
            product = placed(name, hi - lo, F32, byte)
            nc.vector.tensor_tensor(
                out=product[:], in0=y[:].indirect(entries(listed, lo, hi)), in1=factor, op=ALU.mult
            )
            return product

        def fetch(i):
            lo, hi = SHARED[i]
            if i > 0:
                byte = products_at + QUARTER * i if i < LAG else scaled_at + QUARTER * (i - LAG)
                products[i] = gated("product%d" % i, first_list, lo, hi, byte, first_gate(lo, hi))[:]
            fetched = placed("fetched%d" % i, hi - lo, F32, fetched_at + QUARTER * (i % LAG))
            nc.scalar.activation(out=fetched[:], in_=y[:].indirect(entries(second_list, lo, hi)), func=ACT.Copy)
            forward[i] = bank("forward", hi - lo, i % FORWARD_BANKS)
            for c in range(0, hi - lo, P):
                nc.tensor.transpose(forward[i][:, c : c + P], fetched[:, c : c + P], identity[:])

        def scale(i):
            lo, hi = SHARED[i]
            scaled = placed("scaled%d" % i, hi - lo, F32, scaled_at + QUARTER * i)
            for c in range(0, hi - lo, P):
                block = (lo + c - OWN[1]) // P
                nc.scalar.activation(
                    out=scaled[:, c : c + P],
                    in_=forward[i][:, c : c + P],
                    func=ACT.Copy,
                    scale=gate_columns[:, block : block + 1],
                )
            backward[i] = bank("backward", hi - lo, FORWARD_BANKS + i % (BANKS - FORWARD_BANKS))
            for c in range(0, hi - lo, P):
                nc.tensor.transpose(backward[i][:, c : c + P], scaled[:, c : c + P], identity[:])

        def add(lo, hi, one, other):
            nc.vector.tensor_tensor(out=total[:, lo:hi], in0=one, in1=other, op=ALU.add)
            nc.sync.dma_start(out=out[:, lo:hi], in_=total[:, lo:hi])

        lead = (OWN[0], SHARED[0][1])
        leading = gated("leading", first_list, *lead, products_at, first_gate(*lead))
        own_first = leading[:, 0 : OWN[1]]
        products[0] = leading[:, OWN[1] : lead[1]]
        own_second = gated("own_second", second_list, *OWN, products_at + 3 * QUARTER, own_gate[:])
        count = len(SHARED)
        for i in range(count + LAG):
            if i >= LAG:
                scale(i - LAG)
                add(*SHARED[i - LAG], backward[i - LAG][:], products[i - LAG])
            if i == LAG - 1:
                add(*OWN, own_first, own_second[:])
            if i < count:
                fetch(i)
